import numpy as np
import ml_dtypes


def mxq(x, axis, fmt="e4m3"):
    dtype, down = {"e4m3": (ml_dtypes.float8_e4m3fn, 7), "e5m2": (ml_dtypes.float8_e5m2, 14)}[fmt]
    v = np.moveaxis(np.asarray(x, np.float32).astype(ml_dtypes.bfloat16).astype(np.float64), axis, -1)
    blocks = v.reshape(v.shape[:-1] + (-1, 32))
    amax = np.abs(blocks).max(-1, keepdims=True)
    byte = np.maximum(np.where(amax > 0, np.frexp(amax)[1] - 1 + 127, 0) - down, 1)
    scale = np.exp2(byte - 127.0)
    codes = (blocks / scale).astype(np.float32).astype(dtype).astype(np.float64)
    return np.moveaxis((codes * scale).reshape(v.shape), -1, axis)


WIDE = False


def mx_kscale(k):
    if not WIDE:
        return np.ones(k)
    levels = np.array([10, -10, 5, -5, 0])
    if k % 512:
        return np.exp2(np.random.permutation(np.resize(levels, k // 32))).repeat(32)
    a = np.empty((k // 512, 16))
    for p in range(k // 512):
        a[p, :8] = np.random.permutation(np.resize(levels, 8))
        for g in range(8):
            far = levels[np.abs(levels - a[p, g]) >= 10]
            a[p, g + 8] = far[np.random.randint(len(far))]
    return np.exp2(a.ravel()).repeat(32)


BF16 = ml_dtypes.bfloat16


def bf(x):
    return np.asarray(x, np.float32).astype(BF16)


def f64(x):
    return np.asarray(x).astype(np.float64)


E2M1 = np.array([0.0, 0.5, 1.0, 1.5, 2.0, 3.0, 4.0, 6.0, -0.0, -0.5, -1.0, -1.5, -2.0, -3.0, -4.0, -6.0])


def pack_weight(w, fmt):
    k, n = w.shape
    w = f64(bf(w)).reshape(k // 32, 32, n)
    amax = np.abs(w).max(1)
    if fmt == "e4m3":
        byte = np.frexp(amax)[1] - 1 + 127 - 7
    else:
        mant, ex = np.frexp(amax / 6.0)
        byte = np.where(mant > 0.5, ex, ex - 1) + 127
    byte = np.clip(np.where(amax > 0, byte, 1), 1, 254)
    scaled = (w * np.exp2(127.0 - byte)[:, None, :]).reshape(k, n).astype(np.float32)
    by_word = np.ascontiguousarray(scaled.reshape(k // 512, 128, 4, n).transpose(0, 1, 3, 2))
    if fmt == "e4m3":
        words = by_word.astype(ml_dtypes.float8_e4m3fn).view(np.uint8)
    else:
        c = by_word.astype(ml_dtypes.float4_e2m1fn).view(np.uint8) & 0xF
        words = c[..., 0::2] | (c[..., 1::2] << 4)
    return np.ascontiguousarray(words), np.ascontiguousarray(byte.astype(np.uint8).reshape(k // 512, 16, n))


def unpack_weight(words, scales, fmt):
    g, p, n, _ = words.shape
    if fmt == "e4m3":
        vals = np.ascontiguousarray(words).view(ml_dtypes.float8_e4m3fn).astype(np.float64)
    else:
        nib = np.empty((g, p, n, 4), np.uint8)
        nib[..., 0::2] = words & 0xF
        nib[..., 1::2] = words >> 4
        vals = E2M1[nib]
    vals = vals * np.repeat(np.exp2(scales.astype(np.float64) - 127.0), 8, axis=1)[..., None]
    return vals.transpose(0, 1, 3, 2).reshape(g * 512, n)
def pack4(w):
    words, scales = pack_weight(w, "e2m1")
    return words.reshape(words.shape[0], 128, -1), scales


def unpack4(words, scales):
    return unpack_weight(words.reshape(words.shape[0], 128, -1, 2), scales, "e2m1")


E4M3FN = np.array([(-1.0 if i & 128 else 1.0) * ((1.0 + (i & 7) / 8.0) * 2.0 ** (((i >> 3) & 15) - 7) if i & 120 else (i & 7) * 2.0 ** -9) for i in range(256)])


def e4m3fn_bytes(y):
    return np.clip(np.asarray(y, np.float64), -448.0, 448.0).astype(np.float32).astype(ml_dtypes.float8_e4m3fn).view(np.uint8)


def e4m3fn_values(b):
    return E4M3FN[b]


M, N, B = 1024, 1536, 128


def setup_inputs():
    s, t = mx_kscale(N), mx_kscale(M)
    grad = np.random.standard_normal((M, N)) * s * t[:, None]
    right = np.random.standard_normal((N, N)) / np.sqrt(N) / s[:, None]
    grad_scale = (np.abs(grad).reshape(M, N // B, B).max(axis=2) / 448).astype(np.float32)
    right_scale = (np.abs(right).reshape(N // B, B, N // B, B).max(axis=(1, 3)) / 448).astype(np.float32)
    grad_bytes = e4m3fn_bytes(grad / np.repeat(f64(grad_scale), B, axis=1))
    right_bytes = e4m3fn_bytes(right / np.repeat(np.repeat(f64(right_scale), B, axis=0), B, axis=1))
    lt_words, lt_scales = pack4(np.random.standard_normal((M, M)) / np.sqrt(M) / t[:, None])
    return {"grad_bytes": grad_bytes, "grad_scale": grad_scale,
            "right_bytes": right_bytes, "right_scale": right_scale,
            "step": bf(np.exp(0.4 * np.random.standard_normal(N))),
            "lt_words": lt_words, "lt_scales": lt_scales,
            "w": bf(np.random.standard_normal((M, N)))}


def reference(grad_bytes, grad_scale, right_bytes, right_scale, step, lt_words, lt_scales, w):
    grad = e4m3fn_values(grad_bytes) * np.repeat(f64(grad_scale), B, axis=1)
    right = e4m3fn_values(right_bytes) * np.repeat(np.repeat(f64(right_scale), B, axis=0), B, axis=1)
    h = (mxq(grad, 1, "e4m3") @ mxq(right, 0, "e4m3")) * f64(step)
    lt = unpack4(lt_words, lt_scales)
    u = lt.T @ mxq(h, 0, "e4m3")
    return f64(w) - u

@@ -1,0 +1,321 @@
+from contextlib import ExitStack
+
+import concourse.mybir as mybir
+from concourse.masks import make_identity
+
+M, N, B = 1024, 1536, 128
+FLOPS = 2 * M * N * N + 2 * M * M * N
+
+F32 = mybir.dt.float32
+BF16 = mybir.dt.bfloat16
+U32 = mybir.dt.uint32
+I32 = mybir.dt.int32
+U8 = mybir.dt.uint8
+E4M3 = mybir.dt.float8_e4m3fn
+E4M3X4 = mybir.dt.float8_e4m3fn_x4
+E2M1X4 = mybir.dt.float4_e2m1fn_x4
+MULT = mybir.AluOpType.mult
+SUB = mybir.AluOpType.subtract
+COPY = mybir.ActivationFunctionType.Copy
+
+P = 128
+G = M // 512
+Q = N // 512
+NB = N // B
+VEC_SHARE = (4, 5, 8, 4, 2, 3, 3, 3, 4, 2, 4, 3)
+GE_VEC = (2, 5, 9, 11)
+OP_WIDE = (0, 1, 2, 4, 5, 6, 7, 8, 10, 11)
+OP_NARROW = (0, 3)
+CHUNKS = ((0, 1), (1, 1), (2, 1), (3, 1), (4, 1), (5, 1), (6, 1), (7, 1), (8, 1), (9, 1), (10, 1), (11, 1))
+PATH = ("vvv", "vvv", "avv", "vva", "vav", "avv", "vva", "vav", "vvv", "vvv", "avv", "ava")
+HEAD = {4: 3, 9: 3, 11: 2, 12: 1}
+STEADY = {1: 1, 2: 4, 3: 1, 4: 2, 5: 4, 6: 5, 7: 2, 8: 4}
+EARLY_S1 = 8
+
+
+def tile_two_sided_preconditioned_step_d4_kernel(
+        tc, grad_bytes, grad_scale, right_bytes, right_scale, step, lt_words, lt_scales, w, out):
+    nc = tc.nc
+    with ExitStack() as ctx:
+        keep = ctx.enter_context(tc.tile_pool(name="keep", bufs=1))
+        rot = ctx.enter_context(tc.tile_pool(name="rot", bufs=4))
+        ps_h = ctx.enter_context(tc.psum_pool(name="ps_h", bufs=3))
+        ps_o = ctx.enter_context(tc.psum_pool(name="ps_o", bufs=5))
+
+        gb = grad_bytes.rearrange("(g p t) k -> g p t k", p=P, t=4)
+        rb = right_bytes.rearrange("(q p t) n -> q p t n", p=P, t=4)
+        ov = out.rearrange("(r p) n -> p r n", p=P)
+        wv = w.rearrange("(r p) n -> p r n", p=P)
+
+        gs = keep.tile([P, G, 4 * NB], F32, name="gs")
+        nc.scalar.dma_start(out=gs[:], in_=grad_scale.rearrange("(g p t) c -> p g (t c)", p=P, t=4))
+
+        ident = keep.tile([P, P], F32, name="ident")
+        make_identity(nc, ident[:])
+        lts = keep.tile([P, G, M], U8, name="lts", align_bytes=64)
+        nc.gpsimd.memset(lts[:].rearrange("p g n -> p (g n)").bitcast(I32), 0)
+
+        graw = [[keep.tile([P, 2, N], U8, name="graw%d%d" % (g, tp)) for tp in range(2)] for g in range(G)]
+        rraw = [[keep.tile([P, 4, 512], U8, name="rraw%d%d" % (j, q)) for q in range(Q)] for j in range(3)]
+
+        def load_grad(g, tp):
+            nc.sync.dma_start(out=graw[g][tp][:], in_=gb[g][:, 2 * tp : 2 * tp + 2, :])
+
+        def load_right(j, q):
+            nc.sync.dma_start(out=rraw[j][q][:], in_=rb[q][:, :, 512 * j : 512 * j + 512])
+
+        for q in range(Q):
+            nc.sync.dma_start(out=graw[0][0][:, :, 512 * q : 512 * q + 512], in_=gb[0][:, 0:2, 512 * q : 512 * q + 512])
+        load_grad(0, 1)
+        rs_all = keep.tile([P, NB * NB], F32, name="rs_all")
+        nc.sync.dma_start(out=rs_all[:], in_=right_scale.rearrange("a c -> (a c)").partition_broadcast(P))
+        for q in range(Q):
+            load_right(0, q)
+        load_grad(1, 0)
+        load_grad(1, 1)
+        stepb = keep.tile([P, N], BF16, name="stepb")
+        nc.sync.dma_start(out=stepb[:], in_=step.partition_broadcast(P))
+        for q in range(Q):
+            load_right(1, q)
+        ltw = keep.tile([P, G, 2 * M], U8, name="ltw", align_bytes=64)
+        for s in range(4):
+            nc.sync.dma_start(out=lts[32 * s : 32 * s + 4, :, :].bitcast(I32),
+                              in_=lt_scales.rearrange("g (s r) n -> s r g n", s=4)[s].bitcast(I32))
+        nc.sync.dma_start(out=ltw[:], in_=lt_words.rearrange("g p n -> p g n"))
+        for q in range(Q):
+            load_right(2, q)
+        w_sb = keep.tile([P, 8, N], BF16, name="w_sb")
+        for r in range(0, 8, 2):
+            nc.sync.dma_start(out=w_sb[:, r : r + 2, :], in_=wv[:, r : r + 2, :])
+
+        rs = keep.tile([P, Q, NB], F32, name="rs")
+        rs_v = rs_all[:].rearrange("p (q s c) -> p s q c", s=4, c=NB)
+        for s in range(4):
+            sl = slice(32 * s, 32 * s + 32)
+            nc.gpsimd.tensor_copy(out=rs[sl, :, :], in_=rs_v[sl, s, :, :])
+
+        gw = [[keep.tile([P, N], BF16, name="gw%d%d" % (g, t)) for t in range(4)] for g in range(G)]
+        gc = {}
+        gsc = {}
+        units = [(g, tp, q) for g in range(G) for tp in range(2) for q in range(Q)]
+        turned = {}
+
+        def widen(u):
+            g, tp, q = units[u]
+            n = 0
+            for tl in range(2):
+                t = 2 * tp + tl
+                for c in range(4 * q, 4 * q + 4):
+                    src = graw[g][tp][:, tl, c * B : c * B + B].bitcast(E4M3)
+                    dst = gw[g][t][:, c * B : c * B + B]
+                    col = gs[:, g, t * NB + c : t * NB + c + 1]
+                    if n % 8 in (0, 2, 4, 6, 7, 1, 3, 5)[:VEC_SHARE[u]]:
+                        nc.vector.tensor_scalar(out=dst, in0=src, scalar1=col, scalar2=None, op0=MULT)
+                    else:
+                        nc.scalar.activation(out=dst, in_=src, func=COPY, scale=col)
+                    n += 1
+
+        def turn(u):
+            g, tp, q = units[u]
+            xt = ps_o.tile([P, 2, 2, P], F32, name="po")
+            for tl in range(2):
+                words = gw[g][2 * tp + tl][:].bitcast(F32)
+                for e in range(2):
+                    nc.tensor.transpose(xt[:, tl, e, :], words[:, 256 * q + e : 256 * (q + 1) : 2], ident[:])
+            gx = rot.tile([P, 1024], BF16, name="gx", align_bytes=64)
+            dst = gx[:].bitcast(F32).rearrange("p (t m e) -> p t m e", t=2, e=2)
+            src = xt[:].rearrange("p t e m -> p t m e")
+            if u in GE_VEC:
+                nc.vector.tensor_copy(out=dst, in_=src)
+            else:
+                nc.scalar.copy(out=dst, in_=src)
+            turned[u] = gx
+
+        def quant_grad(u):
+            key = units[u]
+            c = keep.tile([P, 256], U32, name="gc%d" % u, align_bytes=64)
+            s = keep.tile([P, 256], U8, name="gsc%d" % u, align_bytes=64)
+            nc.vector.quantize_mx(out=c[:].bitcast(E4M3X4), scales=s[:], in_=turned[u][:])
+            gc[key] = c
+            gsc[key] = s
+
+        rc = {}
+        rsc = {}
+        rjobs = [(k, q) for k in range(len(CHUNKS)) for q in range(Q)]
+        rwide = {}
+
+        def prep_right(k, q):
+            i0, wd = CHUNKS[k]
+            src = rraw[i0 // 4][q]
+            off = B * (i0 % 4)
+            wide = rot.tile([P, wd * 512], BF16, name="rw%d" % (wd * 10 + q), align_bytes=64, bufs=2)
+            if PATH[k][q] == "a":
+                for b in range(wd):
+                    pl = rot.tile([P, 4, B], BF16, name="rp")
+                    for t in range(4):
+                        nc.scalar.activation(out=pl[:, t, :], in_=src[:, t, off + B * b : off + B * b + B].bitcast(E4M3),
+                                             func=COPY, scale=rs[:, q, i0 + b : i0 + b + 1])
+                    nc.scalar.copy(out=wide[:, 512 * b : 512 * b + 512].rearrange("p (n t) -> p n t", t=4), in_=pl[:].rearrange("p t n -> p n t"))
+            else:
+                eng = nc.vector if PATH[k][q] == "v" else nc.gpsimd
+                il = rot.tile([P, wd * 512], U8, name="il%d" % (wd * 10 + q), align_bytes=64, bufs=2)
+                eng.tensor_copy(out=il[:].rearrange("p (n t) -> p n t", t=4),
+                                in_=src[:, :, off : off + B * wd].rearrange("p t n -> p n t"))
+                for b in range(wd):
+                    nc.scalar.activation(out=wide[:, 512 * b : 512 * b + 512], in_=il[:, 512 * b : 512 * b + 512].bitcast(E4M3),
+                                         func=COPY, scale=rs[:, q, i0 + b : i0 + b + 1])
+            rwide[k, q] = wide
+
+        def quant_right(k, q):
+            i0, wd = CHUNKS[k]
+            c = keep.tile([P, B * wd], U32, name="rc%d_%d" % (k, q), align_bytes=64)
+            s = keep.tile([P, B * wd], U8, name="rsc%d_%d" % (k, q), align_bytes=64)
+            nc.vector.quantize_mx(out=c[:].bitcast(E4M3X4), scales=s[:], in_=rwide[k, q][:])
+            for b in range(wd):
+                rc[i0 + b, q] = c[:, B * b : B * b + B]
+                rsc[i0 + b, q] = s[:, B * b : B * b + B]
+
+        rpos = [0, 0]
+
+        def right_step(n, lag):
+            for x in range(n):
+                if rpos[0] < len(rjobs):
+                    prep_right(*rjobs[rpos[0]])
+                    rpos[0] += 1
+                while rpos[1] < rpos[0] - lag or (rpos[0] == len(rjobs) and lag == 0 and rpos[1] < len(rjobs)):
+                    quant_right(*rjobs[rpos[1]])
+                    rpos[1] += 1
+
+        def right_ready(i):
+            while (i, Q - 1) not in rc:
+                if rpos[1] >= rpos[0]:
+                    prep_right(*rjobs[rpos[0]])
+                    rpos[0] += 1
+                quant_right(*rjobs[rpos[1]])
+                rpos[1] += 1
+
+        h_ps = {}
+        hb = {}
+        hc = {}
+        hs = {}
+        for g in range(G):
+            for j in range(3):
+                hc[g, j] = keep.tile([P, 512], U32, name="hc%d%d" % (g, j), align_bytes=64)
+                hs[g, j] = keep.tile([P, 512], U8, name="hs%d%d" % (g, j), align_bytes=64)
+
+        def first(g, i):
+            ps = ps_h.tile([P, 4, B], F32, name="ps")
+            for t in range(4):
+                m = slice(P * (t % 2), P * (t % 2) + P)
+                for q in range(Q):
+                    key = (g, t // 2, q)
+                    nc.tensor.matmul_mx(
+                        out=ps[:, t, :],
+                        lhsT=gc[key][:, m].bitcast(E4M3X4), lhsT_scale=gsc[key][:, m],
+                        rhs=rc[i, q].bitcast(E4M3X4), rhs_scale=rsc[i, q],
+                        start=(q == 0), stop=(q == Q - 1))
+            h_ps[g, i] = ps
+
+        def make_h(g, i):
+            t = rot.tile([P, 512], BF16, name="hb", align_bytes=64)
+            nc.vector.tensor_tensor(
+                out=t[:].rearrange("p (n t) -> p n t", t=4),
+                in0=h_ps[g, i][:].rearrange("p t n -> p n t"),
+                in1=stepb[:, B * i : B * i + B].unsqueeze(2).to_broadcast([P, B, 4]), op=MULT)
+            hb[g, i] = t
+
+        def quant_h(g, i):
+            n = slice(B * (i % 4), B * (i % 4) + B)
+            nc.vector.quantize_mx(out=hc[g, i // 4][:, n].bitcast(E4M3X4), scales=hs[g, i // 4][:, n], in_=hb[g, i][:])
+
+        o_ps = {}
+
+        def second(r, j):
+            ps = ps_o.tile([P, 512], F32, name="po")
+            for g in range(G):
+                nc.tensor.matmul_mx(
+                    out=ps[:],
+                    lhsT=ltw[:, g, 256 * r : 256 * r + 256].bitcast(E2M1X4), lhsT_scale=lts[:, g, P * r : P * r + P],
+                    rhs=hc[g, j][:].bitcast(E4M3X4), rhs_scale=hs[g, j][:], start=(g == 0), stop=(g == G - 1))
+            o_ps[r, j] = ps
+
+        def finish(r, j):
+            o = rot.tile([P, 512], F32, name="ob")
+            cols = slice(512 * j, 512 * j + 512)
+            if (r + 8 * j) in OP_WIDE:
+                u = rot.tile([P, 512], F32, name="ou")
+                nc.scalar.copy(out=u[:], in_=o_ps[r, j][:])
+                nc.gpsimd.tensor_tensor(out=o[:], in0=w_sb[:, r, cols], in1=u[:], op=SUB)
+            else:
+                nc.vector.tensor_tensor(out=o[:], in0=w_sb[:, r, cols], in1=o_ps[r, j][:], op=SUB)
+            nc.sync.dma_start(out=ov[:, r, cols], in_=o[:])
+
+        def second_narrow(half, i):
+            ps = ps_o.tile([P, 4, B], F32, name="po")
+            n = slice(B * (i % 4), B * (i % 4) + B)
+            for rr in range(4):
+                r = 4 * half + rr
+                for g in range(G):
+                    nc.tensor.matmul_mx(
+                        out=ps[:, rr, :],
+                        lhsT=ltw[:, g, 256 * r : 256 * r + 256].bitcast(E2M1X4), lhsT_scale=lts[:, g, P * r : P * r + P],
+                        rhs=hc[g, i // 4][:, n].bitcast(E4M3X4), rhs_scale=hs[g, i // 4][:, n],
+                        start=(g == 0), stop=(g == G - 1))
+            o_ps[half, "n", i] = ps
+
+        def finish_narrow(half, i):
+            o = rot.tile([P, 4, B], F32, name="on")
+            cols = slice(B * i, B * i + B)
+            rows = slice(4 * half, 4 * half + 4)
+            if (half + 2 * (i - 8)) in OP_NARROW:
+                u = rot.tile([P, 4, B], F32, name="un")
+                nc.scalar.copy(out=u[:], in_=o_ps[half, "n", i][:])
+                nc.gpsimd.tensor_tensor(out=o[:], in0=w_sb[:, rows, cols], in1=u[:], op=SUB)
+            else:
+                nc.vector.tensor_tensor(out=o[:], in0=w_sb[:, rows, cols], in1=o_ps[half, "n", i][:], op=SUB)
+            nc.sync.dma_start(out=ov[:, rows, cols], in_=o[:])
+
+        nu = len(units)
+        for s in range(nu + 2):
+            if s < nu:
+                widen(s)
+            if 1 <= s < nu + 1:
+                turn(s - 1)
+            if s >= 2:
+                quant_grad(s - 2)
+            if s in HEAD:
+                right_step(HEAD[s], 1)
+            if s == EARLY_S1:
+                right_ready(0)
+                first(0, 0)
+            if s == EARLY_S1 + 1:
+                make_h(0, 0)
+
+        for i in range(NB + 2):
+            if i < NB:
+                right_ready(i)
+                if i > 0:
+                    first(0, i)
+                first(1, i)
+            if 1 <= i <= NB:
+                quant_h(0, i - 1)
+                quant_h(1, i - 1)
+            pend = []
+            lo = 2 * (i - 4)
+            if 0 <= lo < 16:
+                pend = [(x % 8, x // 8) for x in range(lo, lo + 2)]
+            for r, j in pend:
+                second(r, j)
+            if 9 <= i <= NB:
+                second_narrow(0, i - 1)
+                second_narrow(1, i - 1)
+            right_step(STEADY.get(i, 0), 1)
+            if i < NB:
+                if i > 0:
+                    make_h(0, i)
+                make_h(1, i)
+            for r, j in pend:
+                finish(r, j)
+            if 9 <= i <= NB:
+                finish_narrow(0, i - 1)
+                finish_narrow(1, i - 1)

@@ -159,8 +159,8 @@ def tile_two_sided_preconditioned_step_d4_kernel(
             else:
                 eng = nc.vector if PATH[k][q] == "v" else nc.gpsimd
                 il = rot.tile([P, wd * 512], U8, name="il%d" % (wd * 10 + q), align_bytes=64, bufs=2)
-                eng.tensor_copy(out=il[:].rearrange("p (n t) -> p n t", t=4),
-                                in_=src[:, :, off : off + B * wd].rearrange("p t n -> p n t"))
+                eng.tensor_copy(out=il[:].rearrange("p (c e t) -> p c t e", t=4, e=4),
+                                in_=src[:, :, off : off + B * wd].rearrange("p t (c e) -> p c t e", e=4))
                 for b in range(wd):
                     nc.scalar.activation(out=wide[:, 512 * b : 512 * b + 512], in_=il[:, 512 * b : 512 * b + 512].bitcast(E4M3),
                                          func=COPY, scale=rs[:, q, i0 + b : i0 + b + 1])
@@ -219,9 +219,9 @@ def tile_two_sided_preconditioned_step_d4_kernel(
         def make_h(g, i):
             t = rot.tile([P, 512], BF16, name="hb", align_bytes=64)
             nc.vector.tensor_tensor(
-                out=t[:].rearrange("p (n t) -> p n t", t=4),
-                in0=h_ps[g, i][:].rearrange("p t n -> p n t"),
-                in1=stepb[:, B * i : B * i + B].unsqueeze(2).to_broadcast([P, B, 4]), op=MULT)
+                out=t[:].rearrange("p (c e t) -> p c t e", t=4, e=2),
+                in0=h_ps[g, i][:].rearrange("p t (c e) -> p c t e", e=2),
+                in1=stepb[:, B * i : B * i + B].rearrange("p (c e) -> p c e", e=2).unsqueeze(2).to_broadcast([P, B // 2, 4, 2]), op=MULT)
             hb[g, i] = t
 
         def quant_h(g, i):

@@ -22,15 +22,18 @@ P = 128
 G = M // 512
 Q = N // 512
 NB = N // B
-VEC_SHARE = (4, 5, 8, 4, 2, 3, 3, 3, 4, 2, 4, 3)
-GE_VEC = (2, 5, 9, 11)
-OP_WIDE = (0, 1, 2, 4, 5, 6, 7, 8, 10, 11)
-OP_NARROW = (0, 3)
-CHUNKS = ((0, 1), (1, 1), (2, 1), (3, 1), (4, 1), (5, 1), (6, 1), (7, 1), (8, 1), (9, 1), (10, 1), (11, 1))
-PATH = ("vvv", "vvv", "avv", "vva", "vav", "avv", "vva", "vav", "vvv", "vvv", "avv", "ava")
-HEAD = {4: 3, 9: 3, 11: 2, 12: 1}
-STEADY = {1: 1, 2: 4, 3: 1, 4: 2, 5: 4, 6: 5, 7: 2, 8: 4}
-EARLY_S1 = 8
+OUT_BANKS = 4
+NARROW_FROM = 0
+SCALAR_EVERY = 100
+SCALE_AHEAD = 7
+QUANT_AHEAD = 5
+POOL_EVERY = 100
+POOL_UNTIL = 23
+HEAD_ON_VECTOR = 1
+ON_VECTOR = 0
+LATE = 24
+VECTOR_UNTIL = 9
+CAST1 = 11
 
 
 def tile_two_sided_preconditioned_step_d4_kernel(
@@ -39,8 +42,9 @@ def tile_two_sided_preconditioned_step_d4_kernel(
     with ExitStack() as ctx:
         keep = ctx.enter_context(tc.tile_pool(name="keep", bufs=1))
         rot = ctx.enter_context(tc.tile_pool(name="rot", bufs=4))
-        ps_h = ctx.enter_context(tc.psum_pool(name="ps_h", bufs=3))
-        ps_o = ctx.enter_context(tc.psum_pool(name="ps_o", bufs=5))
+        ps_h = ctx.enter_context(tc.psum_pool(name="ps_h", bufs=4))
+        ps_o = ctx.enter_context(tc.psum_pool(name="ps_o", bufs=OUT_BANKS))
+        ctx.enter_context(tc.manual_schedule())
 
         gb = grad_bytes.rearrange("(g p t) k -> g p t k", p=P, t=4)
         rb = right_bytes.rearrange("(q p t) n -> q p t n", p=P, t=4)
@@ -49,273 +53,269 @@ def tile_two_sided_preconditioned_step_d4_kernel(
 
         gs = keep.tile([P, G, 4 * NB], F32, name="gs")
         nc.scalar.dma_start(out=gs[:], in_=grad_scale.rearrange("(g p t) c -> p g (t c)", p=P, t=4))
+        rs_all = keep.tile([P, NB * NB], F32, name="rs_all")
+        nc.scalar.dma_start(out=rs_all[:], in_=right_scale.rearrange("a c -> (a c)").partition_broadcast(P))
 
         ident = keep.tile([P, P], F32, name="ident")
         make_identity(nc, ident[:])
         lts = keep.tile([P, G, M], U8, name="lts", align_bytes=64)
         nc.gpsimd.memset(lts[:].rearrange("p g n -> p (g n)").bitcast(I32), 0)
 
-        graw = [[keep.tile([P, 2, N], U8, name="graw%d%d" % (g, tp)) for tp in range(2)] for g in range(G)]
-        rraw = [[keep.tile([P, 4, 512], U8, name="rraw%d%d" % (j, q)) for q in range(Q)] for j in range(3)]
+        graw = [[keep.tile([P, 2, N], U8, name="graw%d%d" % (g, u)) for u in range(2)] for g in range(G)]
+        rraw = [[keep.tile([P, 4, 512], U8, name="rraw%d%d" % (j, q)) for q in range(Q)] for j in range(Q)]
+        w_sb = [keep.tile([P, 8, 512], BF16, name="w_sb%d" % j) for j in range(Q)]
+        ltw = keep.tile([P, G, 2 * M], U8, name="ltw", align_bytes=64)
 
-        def load_grad(g, tp):
-            nc.sync.dma_start(out=graw[g][tp][:], in_=gb[g][:, 2 * tp : 2 * tp + 2, :])
+        def load_grad(g, u, lo, hi):
+            nc.sync.dma_start(out=graw[g][u][:, :, lo:hi], in_=gb[g][:, 2 * u : 2 * u + 2, lo:hi])
 
         def load_right(j, q):
             nc.sync.dma_start(out=rraw[j][q][:], in_=rb[q][:, :, 512 * j : 512 * j + 512])
 
-        for q in range(Q):
-            nc.sync.dma_start(out=graw[0][0][:, :, 512 * q : 512 * q + 512], in_=gb[0][:, 0:2, 512 * q : 512 * q + 512])
-        load_grad(0, 1)
-        rs_all = keep.tile([P, NB * NB], F32, name="rs_all")
-        nc.sync.dma_start(out=rs_all[:], in_=right_scale.rearrange("a c -> (a c)").partition_broadcast(P))
-        for q in range(Q):
-            load_right(0, q)
-        load_grad(1, 0)
-        load_grad(1, 1)
+        def load_w(j):
+            for r in range(0, 8, 4):
+                nc.sync.dma_start(out=w_sb[j][:, r : r + 4, :], in_=wv[:, r : r + 4, 512 * j : 512 * j + 512])
+
+        load_grad(0, 0, 0, 512)
+        load_grad(0, 0, 512, N)
+        load_right(0, 0)
+        load_grad(0, 1, 0, N)
+        load_right(0, 1)
+        load_right(0, 2)
+        load_grad(1, 0, 0, N)
+        load_grad(1, 1, 0, N)
         stepb = keep.tile([P, N], BF16, name="stepb")
         nc.sync.dma_start(out=stepb[:], in_=step.partition_broadcast(P))
         for q in range(Q):
             load_right(1, q)
-        ltw = keep.tile([P, G, 2 * M], U8, name="ltw", align_bytes=64)
         for s in range(4):
             nc.sync.dma_start(out=lts[32 * s : 32 * s + 4, :, :].bitcast(I32),
                               in_=lt_scales.rearrange("g (s r) n -> s r g n", s=4)[s].bitcast(I32))
         nc.sync.dma_start(out=ltw[:], in_=lt_words.rearrange("g p n -> p g n"))
+        load_w(0)
         for q in range(Q):
             load_right(2, q)
-        w_sb = keep.tile([P, 8, N], BF16, name="w_sb")
-        for r in range(0, 8, 2):
-            nc.sync.dma_start(out=w_sb[:, r : r + 2, :], in_=wv[:, r : r + 2, :])
+        load_w(1)
+        load_w(2)
 
         rs = keep.tile([P, Q, NB], F32, name="rs")
-        rs_v = rs_all[:].rearrange("p (q s c) -> p s q c", s=4, c=NB)
-        for s in range(4):
-            sl = slice(32 * s, 32 * s + 32)
-            nc.gpsimd.tensor_copy(out=rs[sl, :, :], in_=rs_v[sl, s, :, :])
 
-        gw = [[keep.tile([P, N], BF16, name="gw%d%d" % (g, t)) for t in range(4)] for g in range(G)]
-        gc = {}
-        gsc = {}
-        units = [(g, tp, q) for g in range(G) for tp in range(2) for q in range(Q)]
-        turned = {}
+        def spread_scales():
+            rs_v = rs_all[:].rearrange("p (q s c) -> p s q c", s=4, c=NB)
+            for s in range(4):
+                sl = slice(32 * s, 32 * s + 32)
+                nc.scalar.copy(out=rs[sl, :, :], in_=rs_v[sl, s, :, :])
 
-        def widen(u):
-            g, tp, q = units[u]
-            n = 0
-            for tl in range(2):
-                t = 2 * tp + tl
-                for c in range(4 * q, 4 * q + 4):
-                    src = graw[g][tp][:, tl, c * B : c * B + B].bitcast(E4M3)
-                    dst = gw[g][t][:, c * B : c * B + B]
-                    col = gs[:, g, t * NB + c : t * NB + c + 1]
-                    if n % 8 in (0, 2, 4, 6, 7, 1, 3, 5)[:VEC_SHARE[u]]:
-                        nc.vector.tensor_scalar(out=dst, in0=src, scalar1=col, scalar2=None, op0=MULT)
+        units = [(g, u, q) for g in range(G) for u in range(2) for q in range(Q)]
+        gc = [[keep.tile([P, 512], U32, name="gc%d%d" % (g, q), align_bytes=64) for q in range(Q)] for g in range(G)]
+        gsc = [[keep.tile([P, 512], U8, name="gsc%d%d" % (g, q), align_bytes=64) for q in range(Q)] for g in range(G)]
+        gw = {}
+        gx = {}
+
+        def on_scalar(s, e):
+            return e == 1 and s % SCALAR_EVERY == 0
+
+        def widen_grad(s):
+            g, u, q = units[s]
+            for e in range(2):
+                t = 2 * u + e
+                wide = rot.tile([P, 512], BF16, name="gw", bufs=6)
+                dst = wide[:].rearrange("p (h a f) -> p a h f", h=2, f=2)
+                for c in range(4):
+                    k0 = 512 * q + B * c
+                    src = graw[g][u][:, e, k0 : k0 + B].bitcast(E4M3)
+                    col = t * NB + 4 * q + c
+                    if on_scalar(s, e):
+                        nc.scalar.activation(out=wide[:, B * c : B * c + B], in_=src, func=COPY, scale=gs[:, g, col : col + 1])
                     else:
-                        nc.scalar.activation(out=dst, in_=src, func=COPY, scale=col)
-                    n += 1
+                        nc.vector.tensor_scalar(out=dst[:, 32 * c : 32 * c + 32, :, :],
+                                                in0=src.rearrange("p (a h f) -> p a h f", h=2, f=2),
+                                                scalar1=gs[:, g, col : col + 1], scalar2=None, op0=MULT)
+                gw[s, e] = wide
 
-        def turn(u):
-            g, tp, q = units[u]
-            xt = ps_o.tile([P, 2, 2, P], F32, name="po")
-            for tl in range(2):
-                words = gw[g][2 * tp + tl][:].bitcast(F32)
-                for e in range(2):
-                    nc.tensor.transpose(xt[:, tl, e, :], words[:, 256 * q + e : 256 * (q + 1) : 2], ident[:])
-            gx = rot.tile([P, 1024], BF16, name="gx", align_bytes=64)
-            dst = gx[:].bitcast(F32).rearrange("p (t m e) -> p t m e", t=2, e=2)
-            src = xt[:].rearrange("p t e m -> p t m e")
-            if u in GE_VEC:
-                nc.vector.tensor_copy(out=dst, in_=src)
-            else:
-                nc.scalar.copy(out=dst, in_=src)
-            turned[u] = gx
+        def turn_grad(s):
+            ps = ps_o.tile([P, 2, 2, P], F32, name="po")
+            for e in range(2):
+                words = gw[s, e][:].bitcast(F32)
+                for h in range(2):
+                    part = words[:, h : 2 * P : 2] if on_scalar(s, e) else words[:, P * h : P * h + P]
+                    nc.tensor.transpose(ps[:, e, h, :], part, ident[:])
+            x = rot.tile([P, 1024], BF16, name="gx", align_bytes=64, bufs=4)
+            nc.scalar.copy(out=x[:].bitcast(F32).rearrange("p (e m h) -> p e m h", e=2, h=2),
+                           in_=ps[:].rearrange("p e h m -> p e m h"))
+            gx[s] = x
 
-        def quant_grad(u):
-            key = units[u]
-            c = keep.tile([P, 256], U32, name="gc%d" % u, align_bytes=64)
-            s = keep.tile([P, 256], U8, name="gsc%d" % u, align_bytes=64)
-            nc.vector.quantize_mx(out=c[:].bitcast(E4M3X4), scales=s[:], in_=turned[u][:])
-            gc[key] = c
-            gsc[key] = s
+        def quant_grad(s):
+            g, u, q = units[s]
+            m = slice(256 * u, 256 * u + 256)
+            nc.vector.quantize_mx(out=gc[g][q][:, m].bitcast(E4M3X4), scales=gsc[g][q][:, m], in_=gx[s][:])
 
+        rp = {}
+        rw = {}
         rc = {}
         rsc = {}
-        rjobs = [(k, q) for k in range(len(CHUNKS)) for q in range(Q)]
-        rwide = {}
 
-        def prep_right(k, q):
-            i0, wd = CHUNKS[k]
-            src = rraw[i0 // 4][q]
-            off = B * (i0 % 4)
-            wide = rot.tile([P, wd * 512], BF16, name="rw%d" % (wd * 10 + q), align_bytes=64, bufs=2)
-            if PATH[k][q] == "a":
-                for b in range(wd):
-                    pl = rot.tile([P, 4, B], BF16, name="rp")
-                    for t in range(4):
-                        nc.scalar.activation(out=pl[:, t, :], in_=src[:, t, off + B * b : off + B * b + B].bitcast(E4M3),
-                                             func=COPY, scale=rs[:, q, i0 + b : i0 + b + 1])
-                    nc.scalar.copy(out=wide[:, 512 * b : 512 * b + 512].rearrange("p (n t) -> p n t", t=4), in_=pl[:].rearrange("p t n -> p n t"))
-            else:
-                eng = nc.vector if PATH[k][q] == "v" else nc.gpsimd
-                il = rot.tile([P, wd * 512], U8, name="il%d" % (wd * 10 + q), align_bytes=64, bufs=2)
-                eng.tensor_copy(out=il[:].rearrange("p (c e t) -> p c t e", t=4, e=4),
-                                in_=src[:, :, off : off + B * wd].rearrange("p t (c e) -> p c t e", e=4))
-                for b in range(wd):
-                    nc.scalar.activation(out=wide[:, 512 * b : 512 * b + 512], in_=il[:, 512 * b : 512 * b + 512].bitcast(E4M3),
-                                         func=COPY, scale=rs[:, q, i0 + b : i0 + b + 1])
-            rwide[k, q] = wide
+        def cast_right(j, q, half):
+            if half == 0:
+                rp[j, q] = rot.tile([P, 4, 512], BF16, name="rp", bufs=6)
+            t = slice(2 * half, 2 * half + 2)
+            nc.scalar.copy(out=rp[j, q][:, t, :].rearrange("p t n -> p (t n)"),
+                           in_=rraw[j][q][:, t, :].rearrange("p t n -> p (t n)").bitcast(E4M3))
+
+        def scale_right(k, q, on_vector):
+            rw[k, q] = rot.tile([P, 1024], BF16, name="rw", align_bytes=64, bufs=6)
+            for b in range(2):
+                i = 2 * k + b
+                n = slice(B * (i % 4), B * (i % 4) + B)
+                dst = rw[k, q][:, 512 * b : 512 * b + 512].rearrange("p (c e t) -> p c t e", t=4, e=4)
+                src = rp[i // 4, q][:, :, n].rearrange("p t (c e) -> p c t e", e=4)
+                if b < on_vector:
+                    nc.vector.tensor_scalar(out=dst, in0=src, scalar1=rs[:, q, i : i + 1], scalar2=None, op0=MULT)
+                else:
+                    nc.scalar.activation(out=dst, in_=src, func=COPY, scale=rs[:, q, i : i + 1])
 
         def quant_right(k, q):
-            i0, wd = CHUNKS[k]
-            c = keep.tile([P, B * wd], U32, name="rc%d_%d" % (k, q), align_bytes=64)
-            s = keep.tile([P, B * wd], U8, name="rsc%d_%d" % (k, q), align_bytes=64)
-            nc.vector.quantize_mx(out=c[:].bitcast(E4M3X4), scales=s[:], in_=rwide[k, q][:])
-            for b in range(wd):
-                rc[i0 + b, q] = c[:, B * b : B * b + B]
-                rsc[i0 + b, q] = s[:, B * b : B * b + B]
-
-        rpos = [0, 0]
-
-        def right_step(n, lag):
-            for x in range(n):
-                if rpos[0] < len(rjobs):
-                    prep_right(*rjobs[rpos[0]])
-                    rpos[0] += 1
-                while rpos[1] < rpos[0] - lag or (rpos[0] == len(rjobs) and lag == 0 and rpos[1] < len(rjobs)):
-                    quant_right(*rjobs[rpos[1]])
-                    rpos[1] += 1
-
-        def right_ready(i):
-            while (i, Q - 1) not in rc:
-                if rpos[1] >= rpos[0]:
-                    prep_right(*rjobs[rpos[0]])
-                    rpos[0] += 1
-                quant_right(*rjobs[rpos[1]])
-                rpos[1] += 1
+            if q == 0:
+                rc[k] = rot.tile([P, Q, 256], U32, name="rc", align_bytes=64, bufs=6)
+                rsc[k] = rot.tile([P, Q, 256], U8, name="rsc", align_bytes=64, bufs=6)
+            nc.vector.quantize_mx(out=rc[k][:, q, :].bitcast(E4M3X4), scales=rsc[k][:, q, :], in_=rw[k, q][:])
 
         h_ps = {}
-        hb = {}
-        hc = {}
-        hs = {}
-        for g in range(G):
-            for j in range(3):
-                hc[g, j] = keep.tile([P, 512], U32, name="hc%d%d" % (g, j), align_bytes=64)
-                hs[g, j] = keep.tile([P, 512], U8, name="hs%d%d" % (g, j), align_bytes=64)
+        hp = {}
+        hx = {}
+        hc = [[keep.tile([P, 512], U32, name="hc%d%d" % (g, j), align_bytes=64) for j in range(Q)] for g in range(G)]
+        hs = [[keep.tile([P, 512], U8, name="hs%d%d" % (g, j), align_bytes=64) for j in range(Q)] for g in range(G)]
 
-        def first(g, i):
-            ps = ps_h.tile([P, 4, B], F32, name="ps")
-            for t in range(4):
-                m = slice(P * (t % 2), P * (t % 2) + P)
+        def first(k, g, u):
+            ps = ps_h.tile([P, 2, 256], F32, name="ph")
+            for e in range(2):
+                m = slice(P * (2 * u + e), P * (2 * u + e) + P)
                 for q in range(Q):
-                    key = (g, t // 2, q)
-                    nc.tensor.matmul_mx(
-                        out=ps[:, t, :],
-                        lhsT=gc[key][:, m].bitcast(E4M3X4), lhsT_scale=gsc[key][:, m],
-                        rhs=rc[i, q].bitcast(E4M3X4), rhs_scale=rsc[i, q],
-                        start=(q == 0), stop=(q == Q - 1))
-            h_ps[g, i] = ps
+                    nc.tensor.matmul_mx(out=ps[:, e, :], lhsT=gc[g][q][:, m].bitcast(E4M3X4), lhsT_scale=gsc[g][q][:, m],
+                                        rhs=rc[k][:, q, :].bitcast(E4M3X4), rhs_scale=rsc[k][:, q, :],
+                                        start=(q == 0), stop=(q == Q - 1))
+            h_ps[k, g, u] = ps
 
-        def make_h(g, i):
-            t = rot.tile([P, 512], BF16, name="hb", align_bytes=64)
-            nc.vector.tensor_tensor(
-                out=t[:].rearrange("p (c e t) -> p c t e", t=4, e=2),
-                in0=h_ps[g, i][:].rearrange("p t (c e) -> p c t e", e=2),
-                in1=stepb[:, B * i : B * i + B].rearrange("p (c e) -> p c e", e=2).unsqueeze(2).to_broadcast([P, B // 2, 4, 2]), op=MULT)
-            hb[g, i] = t
+        def step_h(k, g, u):
+            if u == 0:
+                hp[k, g] = rot.tile([P, 2, 512], BF16, name="hp", bufs=3)
+            nc.vector.tensor_tensor(out=hp[k, g][:, u, :].rearrange("p (n e) -> p n e", e=2),
+                                    in0=h_ps[k, g, u][:].rearrange("p e n -> p n e"),
+                                    in1=stepb[:, 256 * k : 256 * k + 256].unsqueeze(2).to_broadcast([P, 256, 2]), op=MULT)
 
-        def quant_h(g, i):
-            n = slice(B * (i % 4), B * (i % 4) + B)
-            nc.vector.quantize_mx(out=hc[g, i // 4][:, n].bitcast(E4M3X4), scales=hs[g, i // 4][:, n], in_=hb[g, i][:])
+        def join_h(k, g):
+            x = rot.tile([P, 1024], BF16, name="hx", align_bytes=64, bufs=3)
+            nc.scalar.copy(out=x[:].bitcast(F32).rearrange("p (n u) -> p n u", u=2),
+                           in_=hp[k, g][:].bitcast(F32).rearrange("p u n -> p n u"))
+            hx[k, g] = x
 
-        o_ps = {}
+        def quant_h(k, g):
+            n = slice(256 * (k % 2), 256 * (k % 2) + 256)
+            nc.vector.quantize_mx(out=hc[g][k // 2][:, n].bitcast(E4M3X4), scales=hs[g][k // 2][:, n], in_=hx[k, g][:])
 
-        def second(r, j):
-            ps = ps_o.tile([P, 512], F32, name="po")
-            for g in range(G):
-                nc.tensor.matmul_mx(
-                    out=ps[:],
-                    lhsT=ltw[:, g, 256 * r : 256 * r + 256].bitcast(E2M1X4), lhsT_scale=lts[:, g, P * r : P * r + P],
-                    rhs=hc[g, j][:].bitcast(E4M3X4), rhs_scale=hs[g, j][:], start=(g == 0), stop=(g == G - 1))
-            o_ps[r, j] = ps
+        waiting = []
+        done = []
 
-        def finish(r, j):
-            o = rot.tile([P, 512], F32, name="ob")
-            cols = slice(512 * j, 512 * j + 512)
-            if (r + 8 * j) in OP_WIDE:
-                u = rot.tile([P, 512], F32, name="ou")
-                nc.scalar.copy(out=u[:], in_=o_ps[r, j][:])
-                nc.gpsimd.tensor_tensor(out=o[:], in0=w_sb[:, r, cols], in1=u[:], op=SUB)
+        def second(rows, j, n):
+            if len(waiting) == OUT_BANKS:
+                finish()
+            width = n.stop - n.start
+            ps = ps_o.tile([P, len(rows), width], F32, name="po")
+            run = width if width == 512 else B
+            for x, r in enumerate(rows):
+                for c in range(0, width, run):
+                    cols = slice(n.start + c, n.start + c + run)
+                    for g in range(G):
+                        nc.tensor.matmul_mx(
+                            out=ps[:, x, c : c + run],
+                            lhsT=ltw[:, g, 256 * r : 256 * r + 256].bitcast(E2M1X4), lhsT_scale=lts[:, g, P * r : P * r + P],
+                            rhs=hc[g][j][:, cols].bitcast(E4M3X4), rhs_scale=hs[g][j][:, cols],
+                            start=(g == 0), stop=(g == G - 1))
+            waiting.append((ps, rows, j, n))
+
+        def finish():
+            ps, rows, j, n = waiting.pop(0)
+            width = n.stop - n.start
+            rsl = slice(rows[0], rows[-1] + 1)
+            o = rot.tile([P, len(rows), width], F32, name="ob", bufs=6)
+            done.append(rows)
+            if len(done) % POOL_EVERY == POOL_EVERY - 1 and len(done) < POOL_UNTIL:
+                neg = rot.tile([P, len(rows), width], F32, name="ou", bufs=2)
+                nc.scalar.copy(out=neg[:], in_=ps[:])
+                nc.gpsimd.tensor_tensor(out=o[:], in0=w_sb[j][:, rsl, n], in1=neg[:], op=SUB)
             else:
-                nc.vector.tensor_tensor(out=o[:], in0=w_sb[:, r, cols], in1=o_ps[r, j][:], op=SUB)
-            nc.sync.dma_start(out=ov[:, r, cols], in_=o[:])
+                nc.vector.tensor_tensor(out=o[:], in0=w_sb[j][:, rsl, n], in1=ps[:], op=SUB)
+            nc.sync.dma_start(out=ov[:, rsl, 512 * j + n.start : 512 * j + n.stop], in_=o[:])
 
-        def second_narrow(half, i):
-            ps = ps_o.tile([P, 4, B], F32, name="po")
-            n = slice(B * (i % 4), B * (i % 4) + B)
-            for rr in range(4):
-                r = 4 * half + rr
-                for g in range(G):
-                    nc.tensor.matmul_mx(
-                        out=ps[:, rr, :],
-                        lhsT=ltw[:, g, 256 * r : 256 * r + 256].bitcast(E2M1X4), lhsT_scale=lts[:, g, P * r : P * r + P],
-                        rhs=hc[g, i // 4][:, n].bitcast(E4M3X4), rhs_scale=hs[g, i // 4][:, n],
-                        start=(g == 0), stop=(g == G - 1))
-            o_ps[half, "n", i] = ps
-
-        def finish_narrow(half, i):
-            o = rot.tile([P, 4, B], F32, name="on")
-            cols = slice(B * i, B * i + B)
-            rows = slice(4 * half, 4 * half + 4)
-            if (half + 2 * (i - 8)) in OP_NARROW:
-                u = rot.tile([P, 4, B], F32, name="un")
-                nc.scalar.copy(out=u[:], in_=o_ps[half, "n", i][:])
-                nc.gpsimd.tensor_tensor(out=o[:], in0=w_sb[:, rows, cols], in1=u[:], op=SUB)
-            else:
-                nc.vector.tensor_tensor(out=o[:], in0=w_sb[:, rows, cols], in1=o_ps[half, "n", i][:], op=SUB)
-            nc.sync.dma_start(out=ov[:, rows, cols], in_=o[:])
+        def second_tiles(k):
+            j = k // 2
+            if 2 * k >= NARROW_FROM:
+                return [([r, r + 1], j, slice(256 * (k % 2), 256 * (k % 2) + 256)) for r in range(0, 8, 2)]
+            return [([r], j, slice(0, 512)) for r in range(8)] if k % 2 == 1 else []
 
         nu = len(units)
-        for s in range(nu + 2):
-            if s < nu:
-                widen(s)
-            if 1 <= s < nu + 1:
-                turn(s - 1)
-            if s >= 2:
-                quant_grad(s - 2)
-            if s in HEAD:
-                right_step(HEAD[s], 1)
-            if s == EARLY_S1:
-                right_ready(0)
-                first(0, 0)
-            if s == EARLY_S1 + 1:
-                make_h(0, 0)
+        nk = NB // 2
+        ready = []
 
-        for i in range(NB + 2):
-            if i < NB:
-                right_ready(i)
-                if i > 0:
-                    first(0, i)
-                first(1, i)
-            if 1 <= i <= NB:
-                quant_h(0, i - 1)
-                quant_h(1, i - 1)
-            pend = []
-            lo = 2 * (i - 4)
-            if 0 <= lo < 16:
-                pend = [(x % 8, x // 8) for x in range(lo, lo + 2)]
-            for r, j in pend:
-                second(r, j)
-            if 9 <= i <= NB:
-                second_narrow(0, i - 1)
-                second_narrow(1, i - 1)
-            right_step(STEADY.get(i, 0), 1)
-            if i < NB:
-                if i > 0:
-                    make_h(0, i)
-                make_h(1, i)
-            for r, j in pend:
-                finish(r, j)
-            if 9 <= i <= NB:
-                finish_narrow(0, i - 1)
-                finish_narrow(1, i - 1)
+        def on_vector(k, q):
+            return HEAD_ON_VECTOR if k < 2 else 2 if Q * k + q < VECTOR_UNTIL else ON_VECTOR
+
+        def cast_pass(j, q):
+            cast_right(j, q, 0)
+            cast_right(j, q, 1)
+
+        def right_jobs(y):
+            k, q = divmod(y + SCALE_AHEAD, 4)
+            if 2 <= k < nk and q < Q:
+                scale_right(k, q, on_vector(k, q))
+            if q == Q and 1 <= k <= Q:
+                cast_pass(2, k - 1)
+            k, q = divmod(y + QUANT_AHEAD, 4)
+            if 1 <= k < nk and q < Q:
+                quant_right(k, q)
+
+        for s in range(nu + 3):
+            if s < nu:
+                widen_grad(s)
+            if 1 <= s <= nu:
+                turn_grad(s - 1)
+            if s == 1:
+                spread_scales()
+            if 1 <= s <= 2 * Q:
+                cast_right(0, (s - 1) // 2, (s - 1) % 2)
+            if 2 * Q < s <= 4 * Q:
+                scale_right(*divmod(s - 2 * Q - 1, Q), on_vector(*divmod(s - 2 * Q - 1, Q)))
+            if s >= 3:
+                quant_grad(s - 3)
+            if nu - Q <= s < nu:
+                quant_right(0, s - nu + Q)
+            if CAST1 <= s < CAST1 + Q:
+                cast_pass(1, s - CAST1)
+            if s == nu:
+                first(0, 0, 0)
+                first(0, 0, 1)
+        right_jobs(-1)
+
+        for y in range(4 * nk + 2):
+            k, x = divmod(y, 4)
+            g, u = divmod(x, 2)
+            if y + 2 < 4 * nk:
+                first((y + 2) // 4, (y + 2) // 2 % 2, y % 2)
+            if y >= 2 and u == 0:
+                join_h((y - 2) // 4, (y - 2) // 2 % 2)
+            right_jobs(y)
+            if k < nk:
+                step_h(k, g, u)
+            if y >= 3 and u == 1:
+                quant_h((y - 3) // 4, (y - 3) // 2 % 2)
+            per_slot = 1 if y < LATE else 2
+            for z in range(min(per_slot, len(waiting))):
+                finish()
+            if y >= 5 and x == 1:
+                ready.extend(second_tiles(k - 1))
+            for z in range(min(per_slot, len(ready))):
+                second(*ready.pop(0))
+        for z in range(len(ready)):
+            second(*ready.pop(0))
+        for z in range(len(waiting)):
+            finish()

@@ -24,16 +24,23 @@ Q = N // 512
 NB = N // B
 OUT_BANKS = 4
 NARROW_FROM = 0
-SCALAR_EVERY = 100
+SCALAR_UNITS = 0
 SCALE_AHEAD = 7
+CAST_AHEAD = 9
+CAST0 = 2
 QUANT_AHEAD = 5
 POOL_EVERY = 100
 POOL_UNTIL = 23
 HEAD_ON_VECTOR = 1
 ON_VECTOR = 0
-LATE = 24
-VECTOR_UNTIL = 9
-CAST1 = 11
+LAST_JOIN_V = 0
+HOLD = (22,)
+POOL_FROM = 12
+VECTOR_UNTIL = 8
+CAST1 = 9
+SCALE0 = 6
+PAIR1_ON_VECTOR = 1
+FIRST0 = 12
 
 
 def tile_two_sided_preconditioned_step_d4_kernel(
@@ -53,58 +60,70 @@ def tile_two_sided_preconditioned_step_d4_kernel(
 
         gs = keep.tile([P, G, 4 * NB], F32, name="gs")
         nc.scalar.dma_start(out=gs[:], in_=grad_scale.rearrange("(g p t) c -> p g (t c)", p=P, t=4))
-        rs_all = keep.tile([P, NB * NB], F32, name="rs_all")
-        nc.scalar.dma_start(out=rs_all[:], in_=right_scale.rearrange("a c -> (a c)").partition_broadcast(P))
+        rs_cols = keep.tile([NB, NB], F32, name="rs_cols")
+        with nc.allow_non_contiguous_dma(reason="144 scales, turned while they load"):
+            nc.scalar.dma_start(out=rs_cols[:], in_=right_scale.rearrange("a c -> c a"))
 
         ident = keep.tile([P, P], F32, name="ident")
         make_identity(nc, ident[:])
+        rs_rep = keep.tile([P, NB, 32], F32, name="rs_rep")
+        nc.gpsimd.memset(rs_rep[:], 0.0)
         lts = keep.tile([P, G, M], U8, name="lts", align_bytes=64)
         nc.gpsimd.memset(lts[:].rearrange("p g n -> p (g n)").bitcast(I32), 0)
 
         graw = [[keep.tile([P, 2, N], U8, name="graw%d%d" % (g, u)) for u in range(2)] for g in range(G)]
-        rraw = [[keep.tile([P, 4, 512], U8, name="rraw%d%d" % (j, q)) for q in range(Q)] for j in range(Q)]
+        rraw = [[keep.tile([P, 4, 256], U8, name="rraw%d%d" % (k, q)) for q in range(Q)] for k in range(NB // 2)]
         w_sb = [keep.tile([P, 8, 512], BF16, name="w_sb%d" % j) for j in range(Q)]
         ltw = keep.tile([P, G, 2 * M], U8, name="ltw", align_bytes=64)
 
         def load_grad(g, u, lo, hi):
             nc.sync.dma_start(out=graw[g][u][:, :, lo:hi], in_=gb[g][:, 2 * u : 2 * u + 2, lo:hi])
 
-        def load_right(j, q):
-            nc.sync.dma_start(out=rraw[j][q][:], in_=rb[q][:, :, 512 * j : 512 * j + 512])
+        def load_right(k, q):
+            nc.sync.dma_start(out=rraw[k][q][:], in_=rb[q][:, :, 256 * k : 256 * k + 256])
 
         def load_w(j):
             for r in range(0, 8, 4):
                 nc.sync.dma_start(out=w_sb[j][:, r : r + 4, :], in_=wv[:, r : r + 4, 512 * j : 512 * j + 512])
 
+        stepb = keep.tile([P, N], BF16, name="stepb")
         load_grad(0, 0, 0, 512)
         load_grad(0, 0, 512, N)
-        load_right(0, 0)
         load_grad(0, 1, 0, N)
-        load_right(0, 1)
-        load_right(0, 2)
+        for q in range(Q):
+            load_right(0, q)
         load_grad(1, 0, 0, N)
         load_grad(1, 1, 0, N)
-        stepb = keep.tile([P, N], BF16, name="stepb")
+        for k in (1, 2):
+            for q in range(Q):
+                load_right(k, q)
         nc.sync.dma_start(out=stepb[:], in_=step.partition_broadcast(P))
-        for q in range(Q):
-            load_right(1, q)
         for s in range(4):
             nc.sync.dma_start(out=lts[32 * s : 32 * s + 4, :, :].bitcast(I32),
                               in_=lt_scales.rearrange("g (s r) n -> s r g n", s=4)[s].bitcast(I32))
         nc.sync.dma_start(out=ltw[:], in_=lt_words.rearrange("g p n -> p g n"))
-        load_w(0)
         for q in range(Q):
-            load_right(2, q)
+            load_right(3, q)
+        load_w(0)
+        for k in (4, 5):
+            for q in range(Q):
+                load_right(k, q)
         load_w(1)
         load_w(2)
 
         rs = keep.tile([P, Q, NB], F32, name="rs")
 
         def spread_scales():
-            rs_v = rs_all[:].rearrange("p (q s c) -> p s q c", s=4, c=NB)
-            for s in range(4):
-                sl = slice(32 * s, 32 * s + 32)
-                nc.scalar.copy(out=rs[sl, :, :], in_=rs_v[sl, s, :, :])
+            nc.scalar.copy(out=rs_rep[0:NB, :, :], in_=rs_cols[:].unsqueeze(2).to_broadcast([NB, NB, 32]))
+
+        def turn_scales():
+            ps = ps_h.tile([P, Q, P], F32, name="ph")
+            for q in range(Q):
+                nc.tensor.transpose(ps[:, q, :], rs_rep[:, 4 * q : 4 * q + 4, :].rearrange("p s r -> p (s r)"), ident[:])
+            return ps
+
+        def leave_scales(ps):
+            nc.scalar.copy(out=rs[:], in_=ps[:, :, 0:NB])
 
         units = [(g, u, q) for g in range(G) for u in range(2) for q in range(Q)]
         gc = [[keep.tile([P, 512], U32, name="gc%d%d" % (g, q), align_bytes=64) for q in range(Q)] for g in range(G)]
@@ -113,7 +132,7 @@ def tile_two_sided_preconditioned_step_d4_kernel(
         gx = {}
 
         def on_scalar(s, e):
-            return e == 1 and s % SCALAR_EVERY == 0
+            return e == 1 and s < SCALAR_UNITS
 
         def widen_grad(s):
             g, u, q = units[s]
@@ -155,20 +174,18 @@ def tile_two_sided_preconditioned_step_d4_kernel(
         rc = {}
         rsc = {}
 
-        def cast_right(j, q, half):
-            if half == 0:
-                rp[j, q] = rot.tile([P, 4, 512], BF16, name="rp", bufs=6)
-            t = slice(2 * half, 2 * half + 2)
-            nc.scalar.copy(out=rp[j, q][:, t, :].rearrange("p t n -> p (t n)"),
-                           in_=rraw[j][q][:, t, :].rearrange("p t n -> p (t n)").bitcast(E4M3))
+        def cast_right(k, q):
+            rp[k, q] = rot.tile([P, 4, 256], BF16, name="rp", bufs=6)
+            nc.scalar.copy(out=rp[k, q][:].rearrange("p t n -> p (t n)"),
+                           in_=rraw[k][q][:].rearrange("p t n -> p (t n)").bitcast(E4M3))
 
         def scale_right(k, q, on_vector):
             rw[k, q] = rot.tile([P, 1024], BF16, name="rw", align_bytes=64, bufs=6)
             for b in range(2):
                 i = 2 * k + b
-                n = slice(B * (i % 4), B * (i % 4) + B)
+                n = slice(B * b, B * b + B)
                 dst = rw[k, q][:, 512 * b : 512 * b + 512].rearrange("p (c e t) -> p c t e", t=4, e=4)
-                src = rp[i // 4, q][:, :, n].rearrange("p t (c e) -> p c t e", e=4)
+                src = rp[k, q][:, :, n].rearrange("p t (c e) -> p c t e", e=4)
                 if b < on_vector:
                     nc.vector.tensor_scalar(out=dst, in0=src, scalar1=rs[:, q, i : i + 1], scalar2=None, op0=MULT)
                 else:
@@ -203,10 +220,14 @@ def tile_two_sided_preconditioned_step_d4_kernel(
                                     in0=h_ps[k, g, u][:].rearrange("p e n -> p n e"),
                                     in1=stepb[:, 256 * k : 256 * k + 256].unsqueeze(2).to_broadcast([P, 256, 2]), op=MULT)
 
-        def join_h(k, g):
+        def join_h(k, g, on_vec):
             x = rot.tile([P, 1024], BF16, name="hx", align_bytes=64, bufs=3)
-            nc.scalar.copy(out=x[:].bitcast(F32).rearrange("p (n u) -> p n u", u=2),
-                           in_=hp[k, g][:].bitcast(F32).rearrange("p u n -> p n u"))
+            dst = x[:].bitcast(F32).rearrange("p (n u) -> p n u", u=2)
+            src = hp[k, g][:].bitcast(F32).rearrange("p u n -> p n u")
+            if on_vec and LAST_JOIN_V:
+                nc.vector.tensor_copy(out=dst, in_=src)
+            else:
+                nc.scalar.copy(out=dst, in_=src)
             hx[k, g] = x
 
         def quant_h(k, g):
@@ -239,7 +260,7 @@ def tile_two_sided_preconditioned_step_d4_kernel(
             rsl = slice(rows[0], rows[-1] + 1)
             o = rot.tile([P, len(rows), width], F32, name="ob", bufs=6)
             done.append(rows)
-            if len(done) % POOL_EVERY == POOL_EVERY - 1 and len(done) < POOL_UNTIL:
+            if len(done) % POOL_EVERY == 0 and POOL_FROM <= len(done) < POOL_UNTIL:
                 neg = rot.tile([P, len(rows), width], F32, name="ou", bufs=2)
                 nc.scalar.copy(out=neg[:], in_=ps[:])
                 nc.gpsimd.tensor_tensor(out=o[:], in0=w_sb[j][:, rsl, n], in1=neg[:], op=SUB)
@@ -258,18 +279,15 @@ def tile_two_sided_preconditioned_step_d4_kernel(
         ready = []
 
         def on_vector(k, q):
-            return HEAD_ON_VECTOR if k < 2 else 2 if Q * k + q < VECTOR_UNTIL else ON_VECTOR
-
-        def cast_pass(j, q):
-            cast_right(j, q, 0)
-            cast_right(j, q, 1)
+            return 2 if Q * k + q < VECTOR_UNTIL else ON_VECTOR
 
         def right_jobs(y):
             k, q = divmod(y + SCALE_AHEAD, 4)
             if 2 <= k < nk and q < Q:
                 scale_right(k, q, on_vector(k, q))
-            if q == Q and 1 <= k <= Q:
-                cast_pass(2, k - 1)
+            k, q = divmod(y + CAST_AHEAD, 4)
+            if 3 <= k < nk and q < Q:
+                cast_right(k, q)
             k, q = divmod(y + QUANT_AHEAD, 4)
             if 1 <= k < nk and q < Q:
                 quant_right(k, q)
@@ -279,41 +297,48 @@ def tile_two_sided_preconditioned_step_d4_kernel(
                 widen_grad(s)
             if 1 <= s <= nu:
                 turn_grad(s - 1)
-            if s == 1:
+            if s == 2:
                 spread_scales()
-            if 1 <= s <= 2 * Q:
-                cast_right(0, (s - 1) // 2, (s - 1) % 2)
-            if 2 * Q < s <= 4 * Q:
-                scale_right(*divmod(s - 2 * Q - 1, Q), on_vector(*divmod(s - 2 * Q - 1, Q)))
+            if s == 3:
+                scales_ps = turn_scales()
+            if s == 4:
+                leave_scales(scales_ps)
+            if CAST0 <= s < CAST0 + Q:
+                cast_right(0, s - CAST0)
+            if SCALE0 <= s < SCALE0 + Q:
+                scale_right(0, s - SCALE0, HEAD_ON_VECTOR)
+            if CAST1 <= s < CAST1 + Q:
+                cast_right(1, s - CAST1)
+            if s >= nu:
+                scale_right(1, s - nu, PAIR1_ON_VECTOR)
+                cast_right(2, s - nu)
             if s >= 3:
                 quant_grad(s - 3)
-            if nu - Q <= s < nu:
-                quant_right(0, s - nu + Q)
-            if CAST1 <= s < CAST1 + Q:
-                cast_pass(1, s - CAST1)
-            if s == nu:
+            if SCALE0 + 2 <= s < SCALE0 + 2 + Q:
+                quant_right(0, s - SCALE0 - 2)
+            if s == FIRST0:
                 first(0, 0, 0)
                 first(0, 0, 1)
         right_jobs(-1)
 
-        for y in range(4 * nk + 2):
+        last = 4 * nk - 1
+        for y in range(last + 3):
             k, x = divmod(y, 4)
             g, u = divmod(x, 2)
-            if y + 2 < 4 * nk:
+            if y + 2 <= last:
                 first((y + 2) // 4, (y + 2) // 2 % 2, y % 2)
             if y >= 2 and u == 0:
-                join_h((y - 2) // 4, (y - 2) // 2 % 2)
-            right_jobs(y)
-            if k < nk:
+                join_h((y - 2) // 4, (y - 2) // 2 % 2, y > last)
+            if y <= last:
                 step_h(k, g, u)
             if y >= 3 and u == 1:
                 quant_h((y - 3) // 4, (y - 3) // 2 % 2)
-            per_slot = 1 if y < LATE else 2
-            for z in range(min(per_slot, len(waiting))):
+            if waiting and y not in HOLD:
                 finish()
+            right_jobs(y)
             if y >= 5 and x == 1:
                 ready.extend(second_tiles(k - 1))
-            for z in range(min(per_slot, len(ready))):
+            if ready:
                 second(*ready.pop(0))
         for z in range(len(ready)):
             second(*ready.pop(0))

@@ -216,9 +216,10 @@ def tile_two_sided_preconditioned_step_d4_kernel(
         def step_h(k, g, u):
             if u == 0:
                 hp[k, g] = rot.tile([P, 2, 512], BF16, name="hp", bufs=3)
-            nc.vector.tensor_tensor(out=hp[k, g][:, u, :].rearrange("p (n e) -> p n e", e=2),
-                                    in0=h_ps[k, g, u][:].rearrange("p e n -> p n e"),
-                                    in1=stepb[:, 256 * k : 256 * k + 256].unsqueeze(2).to_broadcast([P, 256, 2]), op=MULT)
+            nc.vector.tensor_tensor(out=hp[k, g][:, u, :].rearrange("p (c i e) -> p c e i", i=2, e=2),
+                                    in0=h_ps[k, g, u][:].rearrange("p e (c i) -> p c e i", i=2),
+                                    in1=stepb[:, 256 * k : 256 * k + 256].rearrange("p (c i) -> p c i", i=2).unsqueeze(2).to_broadcast([P, B, 2, 2]),
+                                    op=MULT)
 
         def join_h(k, g, on_vec):
             x = rot.tile([P, 1024], BF16, name="hx", align_bytes=64, bufs=3)

@@ -19,28 +19,22 @@ SUB = mybir.AluOpType.subtract
 COPY = mybir.ActivationFunctionType.Copy
 
 P = 128
-G = M // 512
-Q = N // 512
-NB = N // B
-OUT_BANKS = 4
-NARROW_FROM = 0
-SCALAR_UNITS = 0
+PASS = 4 * P
+GROUPS = M // PASS
+PASSES = N // PASS
+BLOCKS = N // B
+PAIR = 2 * B
+PAIRS = N // PAIR
+ROW_TILES = M // P
+BANKS = 4
+SLOTS = 4
+
+CAST_AHEAD = 10
 SCALE_AHEAD = 7
-CAST_AHEAD = 9
-CAST0 = 2
 QUANT_AHEAD = 5
-POOL_EVERY = 100
-POOL_UNTIL = 23
-HEAD_ON_VECTOR = 1
-ON_VECTOR = 0
-LAST_JOIN_V = 0
-HOLD = (22,)
-POOL_FROM = 12
-VECTOR_UNTIL = 8
-CAST1 = 9
-SCALE0 = 6
-PAIR1_ON_VECTOR = 1
-FIRST0 = 12
+FIRST_CAST = 1
+FIRST_SCALE = 5
+VECTOR_JOBS = 8
 
 
 def tile_two_sided_preconditioned_step_d4_kernel(
@@ -48,300 +42,285 @@ def tile_two_sided_preconditioned_step_d4_kernel(
     nc = tc.nc
     with ExitStack() as ctx:
         keep = ctx.enter_context(tc.tile_pool(name="keep", bufs=1))
-        rot = ctx.enter_context(tc.tile_pool(name="rot", bufs=4))
-        ps_h = ctx.enter_context(tc.psum_pool(name="ps_h", bufs=4))
-        ps_o = ctx.enter_context(tc.psum_pool(name="ps_o", bufs=OUT_BANKS))
+        rot = ctx.enter_context(tc.tile_pool(name="rot", bufs=3))
+        ps_h = ctx.enter_context(tc.psum_pool(name="ps_h", bufs=BANKS))
+        ps_o = ctx.enter_context(tc.psum_pool(name="ps_o", bufs=BANKS))
         ctx.enter_context(tc.manual_schedule())
 
-        gb = grad_bytes.rearrange("(g p t) k -> g p t k", p=P, t=4)
-        rb = right_bytes.rearrange("(q p t) n -> q p t n", p=P, t=4)
-        ov = out.rearrange("(r p) n -> p r n", p=P)
-        wv = w.rearrange("(r p) n -> p r n", p=P)
+        grad_v = grad_bytes.rearrange("(g p t) k -> g p t k", p=P, t=4)
+        right_v = right_bytes.rearrange("(q p t) n -> q p t n", p=P, t=4)
+        out_v = out.rearrange("(r p) n -> p r n", p=P)
+        w_v = w.rearrange("(r p) n -> p r n", p=P)
 
-        gs = keep.tile([P, G, 4 * NB], F32, name="gs")
-        nc.scalar.dma_start(out=gs[:], in_=grad_scale.rearrange("(g p t) c -> p g (t c)", p=P, t=4))
-        rs_cols = keep.tile([NB, NB], F32, name="rs_cols")
+        g_scale = keep.tile([P, GROUPS, 4 * BLOCKS], F32, name="g_scale")
+        nc.scalar.dma_start(out=g_scale[:], in_=grad_scale.rearrange("(g p t) c -> p g (t c)", p=P, t=4))
+        r_cols = keep.tile([BLOCKS, BLOCKS], F32, name="r_cols")
         with nc.allow_non_contiguous_dma(reason="144 scales, turned while they load"):
-            nc.scalar.dma_start(out=rs_cols[:], in_=right_scale.rearrange("a c -> c a"))
+            nc.scalar.dma_start(out=r_cols[:], in_=right_scale.rearrange("a c -> c a"))
 
         ident = keep.tile([P, P], F32, name="ident")
         make_identity(nc, ident[:])
-        rs_rep = keep.tile([P, NB, 32], F32, name="rs_rep")
-        nc.gpsimd.memset(rs_rep[:], 0.0)
-        lts = keep.tile([P, G, M], U8, name="lts", align_bytes=64)
-        nc.gpsimd.memset(lts[:].rearrange("p g n -> p (g n)").bitcast(I32), 0)
+        r_rep = keep.tile([P, BLOCKS, 32], F32, name="r_rep")
+        nc.gpsimd.memset(r_rep[:], 0.0)
+        lt_s = keep.tile([P, GROUPS, M], U8, name="lt_s", align_bytes=64)
+        nc.gpsimd.memset(lt_s[:].rearrange("p g n -> p (g n)").bitcast(I32), 0)
 
-        graw = [[keep.tile([P, 2, N], U8, name="graw%d%d" % (g, u)) for u in range(2)] for g in range(G)]
-        rraw = [[keep.tile([P, 4, 256], U8, name="rraw%d%d" % (k, q)) for q in range(Q)] for k in range(NB // 2)]
-        w_sb = [keep.tile([P, 8, 512], BF16, name="w_sb%d" % j) for j in range(Q)]
-        ltw = keep.tile([P, G, 2 * M], U8, name="ltw", align_bytes=64)
+        g_raw = [[keep.tile([P, 2, N], U8, name="g_raw%d%d" % (g, u)) for u in range(2)] for g in range(GROUPS)]
+        r_raw = [[keep.tile([P, 4, PAIR], U8, name="r_raw%d%d" % (k, q)) for q in range(PASSES)] for k in range(PAIRS)]
+        w_sb = [keep.tile([P, ROW_TILES, PASS], BF16, name="w_sb%d" % j) for j in range(PASSES)]
+        lt_w = keep.tile([P, GROUPS, 2 * M], U8, name="lt_w", align_bytes=64)
+        step_all = keep.tile([P, N], BF16, name="step_all")
 
         def load_grad(g, u, lo, hi):
-            nc.sync.dma_start(out=graw[g][u][:, :, lo:hi], in_=gb[g][:, 2 * u : 2 * u + 2, lo:hi])
+            nc.sync.dma_start(out=g_raw[g][u][:, :, lo:hi], in_=grad_v[g][:, 2 * u : 2 * u + 2, lo:hi])
 
         def load_right(k, q):
-            nc.sync.dma_start(out=rraw[k][q][:], in_=rb[q][:, :, 256 * k : 256 * k + 256])
+            nc.sync.dma_start(out=r_raw[k][q][:], in_=right_v[q][:, :, PAIR * k : PAIR * k + PAIR])
+
+        def load_pair(k):
+            for q in range(PASSES):
+                load_right(k, q)
 
         def load_w(j):
-            for r in range(0, 8, 4):
-                nc.sync.dma_start(out=w_sb[j][:, r : r + 4, :], in_=wv[:, r : r + 4, 512 * j : 512 * j + 512])
+            for r in range(0, ROW_TILES, 4):
+                nc.sync.dma_start(out=w_sb[j][:, r : r + 4, :], in_=w_v[:, r : r + 4, PASS * j : PASS * j + PASS])
 
-        stepb = keep.tile([P, N], BF16, name="stepb")
-        load_grad(0, 0, 0, 512)
-        load_grad(0, 0, 512, N)
+        load_grad(0, 0, 0, PASS)
+        load_right(0, 0)
+        load_grad(0, 0, PASS, N)
+        load_right(0, 1)
         load_grad(0, 1, 0, N)
-        for q in range(Q):
-            load_right(0, q)
+        load_right(0, 2)
         load_grad(1, 0, 0, N)
         load_grad(1, 1, 0, N)
-        for k in (1, 2):
-            for q in range(Q):
-                load_right(k, q)
-        nc.sync.dma_start(out=stepb[:], in_=step.partition_broadcast(P))
+        load_pair(1)
+        load_pair(2)
+        nc.sync.dma_start(out=step_all[:], in_=step.partition_broadcast(P))
         for s in range(4):
-            nc.sync.dma_start(out=lts[32 * s : 32 * s + 4, :, :].bitcast(I32),
+            nc.sync.dma_start(out=lt_s[32 * s : 32 * s + 4, :, :].bitcast(I32),
                               in_=lt_scales.rearrange("g (s r) n -> s r g n", s=4)[s].bitcast(I32))
-        nc.sync.dma_start(out=ltw[:], in_=lt_words.rearrange("g p n -> p g n"))
-        for q in range(Q):
-            load_right(3, q)
+        nc.sync.dma_start(out=lt_w[:], in_=lt_words.rearrange("g p n -> p g n"))
+        load_pair(3)
         load_w(0)
-        for k in (4, 5):
-            for q in range(Q):
-                load_right(k, q)
+        load_pair(4)
+        load_pair(5)
         load_w(1)
         load_w(2)
 
-        rs = keep.tile([P, Q, NB], F32, name="rs")
+        r_scale = keep.tile([P, PASSES, BLOCKS], F32, name="r_scale")
+        r_scale_ps = []
 
-        def spread_scales():
-            nc.scalar.copy(out=rs_rep[0:NB, :, :], in_=rs_cols[:].unsqueeze(2).to_broadcast([NB, NB, 32]))
+        def repeat_scales():
+            nc.scalar.copy(out=r_rep[0:BLOCKS, :, :], in_=r_cols[:].unsqueeze(2).to_broadcast([BLOCKS, BLOCKS, 32]))
 
         def turn_scales():
-            ps = ps_h.tile([P, Q, P], F32, name="ph")
-            for q in range(Q):
-                nc.tensor.transpose(ps[:, q, :], rs_rep[:, 4 * q : 4 * q + 4, :].rearrange("p s r -> p (s r)"), ident[:])
-            return ps
+            ps = ps_h.tile([P, PASSES, P], F32, name="bank_h")
+            for q in range(PASSES):
+                nc.tensor.transpose(ps[:, q, :], r_rep[:, 4 * q : 4 * q + 4, :].rearrange("p s r -> p (s r)"), ident[:])
+            r_scale_ps.append(ps)
 
-        def leave_scales(ps):
-            nc.scalar.copy(out=rs[:], in_=ps[:, :, 0:NB])
+        def leave_scales():
+            nc.scalar.copy(out=r_scale[:], in_=r_scale_ps[0][:, :, 0:BLOCKS])
 
-        units = [(g, u, q) for g in range(G) for u in range(2) for q in range(Q)]
-        gc = [[keep.tile([P, 512], U32, name="gc%d%d" % (g, q), align_bytes=64) for q in range(Q)] for g in range(G)]
-        gsc = [[keep.tile([P, 512], U8, name="gsc%d%d" % (g, q), align_bytes=64) for q in range(Q)] for g in range(G)]
-        gw = {}
-        gx = {}
-
-        def on_scalar(s, e):
-            return e == 1 and s < SCALAR_UNITS
+        units = [(g, u, q) for g in range(GROUPS) for u in range(2) for q in range(PASSES)]
+        g_codes = [[keep.tile([P, PASS], U32, name="g_codes%d%d" % (g, q), align_bytes=64) for q in range(PASSES)]
+                   for g in range(GROUPS)]
+        g_bytes = [[keep.tile([P, PASS], U8, name="g_bytes%d%d" % (g, q), align_bytes=64) for q in range(PASSES)]
+                   for g in range(GROUPS)]
+        g_wide = {}
+        g_ps = {}
+        g_turned = {}
 
         def widen_grad(s):
             g, u, q = units[s]
             for e in range(2):
-                t = 2 * u + e
-                wide = rot.tile([P, 512], BF16, name="gw", bufs=6)
+                wide = rot.tile([P, PASS], BF16, name="g_wide", bufs=6)
                 dst = wide[:].rearrange("p (h a f) -> p a h f", h=2, f=2)
                 for c in range(4):
-                    k0 = 512 * q + B * c
-                    src = graw[g][u][:, e, k0 : k0 + B].bitcast(E4M3)
-                    col = t * NB + 4 * q + c
-                    if on_scalar(s, e):
-                        nc.scalar.activation(out=wide[:, B * c : B * c + B], in_=src, func=COPY, scale=gs[:, g, col : col + 1])
-                    else:
-                        nc.vector.tensor_scalar(out=dst[:, 32 * c : 32 * c + 32, :, :],
-                                                in0=src.rearrange("p (a h f) -> p a h f", h=2, f=2),
-                                                scalar1=gs[:, g, col : col + 1], scalar2=None, op0=MULT)
-                gw[s, e] = wide
+                    k0 = PASS * q + B * c
+                    src = g_raw[g][u][:, e, k0 : k0 + B].bitcast(E4M3).rearrange("p (a h f) -> p a h f", h=2, f=2)
+                    col = (2 * u + e) * BLOCKS + 4 * q + c
+                    nc.vector.tensor_scalar(out=dst[:, 32 * c : 32 * c + 32, :, :], in0=src,
+                                            scalar1=g_scale[:, g, col : col + 1], scalar2=None, op0=MULT)
+                g_wide[s, e] = wide
 
         def turn_grad(s):
-            ps = ps_o.tile([P, 2, 2, P], F32, name="po")
+            ps = ps_o.tile([P, 2, 2, P], F32, name="bank_o")
             for e in range(2):
-                words = gw[s, e][:].bitcast(F32)
+                words = g_wide[s, e][:].bitcast(F32)
                 for h in range(2):
-                    part = words[:, h : 2 * P : 2] if on_scalar(s, e) else words[:, P * h : P * h + P]
-                    nc.tensor.transpose(ps[:, e, h, :], part, ident[:])
-            x = rot.tile([P, 1024], BF16, name="gx", align_bytes=64, bufs=4)
+                    nc.tensor.transpose(ps[:, e, h, :], words[:, P * h : P * h + P], ident[:])
+            g_ps[s] = ps
+
+        def leave_grad(s):
+            x = rot.tile([P, 2 * PASS], BF16, name="g_turned", align_bytes=64, bufs=4)
             nc.scalar.copy(out=x[:].bitcast(F32).rearrange("p (e m h) -> p e m h", e=2, h=2),
-                           in_=ps[:].rearrange("p e h m -> p e m h"))
-            gx[s] = x
+                           in_=g_ps[s][:].rearrange("p e h m -> p e m h"))
+            g_turned[s] = x
 
         def quant_grad(s):
             g, u, q = units[s]
-            m = slice(256 * u, 256 * u + 256)
-            nc.vector.quantize_mx(out=gc[g][q][:, m].bitcast(E4M3X4), scales=gsc[g][q][:, m], in_=gx[s][:])
+            m = slice(2 * P * u, 2 * P * u + 2 * P)
+            nc.vector.quantize_mx(out=g_codes[g][q][:, m].bitcast(E4M3X4), scales=g_bytes[g][q][:, m], in_=g_turned[s][:])
 
-        rp = {}
-        rw = {}
-        rc = {}
-        rsc = {}
+        r_planes = {}
+        r_wide = {}
+        r_codes = {}
+        r_bytes = {}
 
         def cast_right(k, q):
-            rp[k, q] = rot.tile([P, 4, 256], BF16, name="rp", bufs=6)
-            nc.scalar.copy(out=rp[k, q][:].rearrange("p t n -> p (t n)"),
-                           in_=rraw[k][q][:].rearrange("p t n -> p (t n)").bitcast(E4M3))
+            r_planes[k, q] = rot.tile([P, 4, PAIR], BF16, name="r_planes", bufs=6)
+            nc.scalar.copy(out=r_planes[k, q][:].rearrange("p t n -> p (t n)"),
+                           in_=r_raw[k][q][:].rearrange("p t n -> p (t n)").bitcast(E4M3))
 
-        def scale_right(k, q, on_vector):
-            rw[k, q] = rot.tile([P, 1024], BF16, name="rw", align_bytes=64, bufs=6)
+        def vector_blocks(k, q):
+            if k < 2:
+                return 1
+            if PASSES * k + q < VECTOR_JOBS:
+                return 2
+            return 1 if q == 0 else 0
+
+        def scale_right(k, q):
+            on_vector = vector_blocks(k, q)
+            r_wide[k, q] = rot.tile([P, 4 * PAIR], BF16, name="r_wide", align_bytes=64, bufs=6)
             for b in range(2):
-                i = 2 * k + b
-                n = slice(B * b, B * b + B)
-                dst = rw[k, q][:, 512 * b : 512 * b + 512].rearrange("p (c e t) -> p c t e", t=4, e=4)
-                src = rp[k, q][:, :, n].rearrange("p t (c e) -> p c t e", e=4)
+                dst = r_wide[k, q][:, 4 * B * b : 4 * B * b + 4 * B].rearrange("p (c i t) -> p c t i", t=4, i=4)
+                src = r_planes[k, q][:, :, B * b : B * b + B].rearrange("p t (c i) -> p c t i", i=4)
+                scale = r_scale[:, q, 2 * k + b : 2 * k + b + 1]
                 if b < on_vector:
-                    nc.vector.tensor_scalar(out=dst, in0=src, scalar1=rs[:, q, i : i + 1], scalar2=None, op0=MULT)
+                    nc.vector.tensor_scalar(out=dst, in0=src, scalar1=scale, scalar2=None, op0=MULT)
                 else:
-                    nc.scalar.activation(out=dst, in_=src, func=COPY, scale=rs[:, q, i : i + 1])
+                    nc.scalar.activation(out=dst, in_=src, func=COPY, scale=scale)
 
         def quant_right(k, q):
             if q == 0:
-                rc[k] = rot.tile([P, Q, 256], U32, name="rc", align_bytes=64, bufs=6)
-                rsc[k] = rot.tile([P, Q, 256], U8, name="rsc", align_bytes=64, bufs=6)
-            nc.vector.quantize_mx(out=rc[k][:, q, :].bitcast(E4M3X4), scales=rsc[k][:, q, :], in_=rw[k, q][:])
+                r_codes[k] = keep.tile([P, PASSES, PAIR], U32, name="r_codes%d" % k, align_bytes=64)
+                r_bytes[k] = keep.tile([P, PASSES, PAIR], U8, name="r_bytes%d" % k, align_bytes=64)
+            nc.vector.quantize_mx(out=r_codes[k][:, q, :].bitcast(E4M3X4), scales=r_bytes[k][:, q, :], in_=r_wide[k, q][:])
 
+        slots = [(k, g, u) for k in range(PAIRS) for g in range(GROUPS) for u in range(2)]
+        h_codes = [keep.tile([P, N], U32, name="h_codes%d" % g, align_bytes=64) for g in range(GROUPS)]
+        h_bytes = [keep.tile([P, N], U8, name="h_bytes%d" % g, align_bytes=64) for g in range(GROUPS)]
         h_ps = {}
-        hp = {}
-        hx = {}
-        hc = [[keep.tile([P, 512], U32, name="hc%d%d" % (g, j), align_bytes=64) for j in range(Q)] for g in range(G)]
-        hs = [[keep.tile([P, 512], U8, name="hs%d%d" % (g, j), align_bytes=64) for j in range(Q)] for g in range(G)]
+        h_halves = {}
+        h_joined = {}
 
-        def first(k, g, u):
-            ps = ps_h.tile([P, 2, 256], F32, name="ph")
+        def first_product(k, g, u):
+            ps = ps_h.tile([P, 2, PAIR], F32, name="bank_h")
             for e in range(2):
                 m = slice(P * (2 * u + e), P * (2 * u + e) + P)
-                for q in range(Q):
-                    nc.tensor.matmul_mx(out=ps[:, e, :], lhsT=gc[g][q][:, m].bitcast(E4M3X4), lhsT_scale=gsc[g][q][:, m],
-                                        rhs=rc[k][:, q, :].bitcast(E4M3X4), rhs_scale=rsc[k][:, q, :],
-                                        start=(q == 0), stop=(q == Q - 1))
+                for q in range(PASSES):
+                    nc.tensor.matmul_mx(out=ps[:, e, :],
+                                        lhsT=g_codes[g][q][:, m].bitcast(E4M3X4), lhsT_scale=g_bytes[g][q][:, m],
+                                        rhs=r_codes[k][:, q, :].bitcast(E4M3X4), rhs_scale=r_bytes[k][:, q, :],
+                                        start=(q == 0), stop=(q == PASSES - 1))
             h_ps[k, g, u] = ps
 
         def step_h(k, g, u):
             if u == 0:
-                hp[k, g] = rot.tile([P, 2, 512], BF16, name="hp", bufs=3)
-            nc.vector.tensor_tensor(out=hp[k, g][:, u, :].rearrange("p (c i e) -> p c e i", i=2, e=2),
+                h_halves[k, g] = rot.tile([P, 2, 2 * PAIR], BF16, name="h_halves")
+            steps = step_all[:, PAIR * k : PAIR * k + PAIR].rearrange("p (c i) -> p c i", i=2)
+            nc.vector.tensor_tensor(out=h_halves[k, g][:, u, :].rearrange("p (c i e) -> p c e i", i=2, e=2),
                                     in0=h_ps[k, g, u][:].rearrange("p e (c i) -> p c e i", i=2),
-                                    in1=stepb[:, 256 * k : 256 * k + 256].rearrange("p (c i) -> p c i", i=2).unsqueeze(2).to_broadcast([P, B, 2, 2]),
-                                    op=MULT)
+                                    in1=steps.unsqueeze(2).to_broadcast([P, PAIR // 2, 2, 2]), op=MULT)
 
-        def join_h(k, g, on_vec):
-            x = rot.tile([P, 1024], BF16, name="hx", align_bytes=64, bufs=3)
-            dst = x[:].bitcast(F32).rearrange("p (n u) -> p n u", u=2)
-            src = hp[k, g][:].bitcast(F32).rearrange("p u n -> p n u")
-            if on_vec and LAST_JOIN_V:
-                nc.vector.tensor_copy(out=dst, in_=src)
-            else:
-                nc.scalar.copy(out=dst, in_=src)
-            hx[k, g] = x
+        def join_h(k, g):
+            x = rot.tile([P, 4 * PAIR], BF16, name="h_joined", align_bytes=64)
+            nc.scalar.copy(out=x[:].bitcast(F32).rearrange("p (n u) -> p n u", u=2),
+                           in_=h_halves[k, g][:].bitcast(F32).rearrange("p u n -> p n u"))
+            h_joined[k, g] = x
 
         def quant_h(k, g):
-            n = slice(256 * (k % 2), 256 * (k % 2) + 256)
-            nc.vector.quantize_mx(out=hc[g][k // 2][:, n].bitcast(E4M3X4), scales=hs[g][k // 2][:, n], in_=hx[k, g][:])
+            n = slice(PAIR * k, PAIR * k + PAIR)
+            nc.vector.quantize_mx(out=h_codes[g][:, n].bitcast(E4M3X4), scales=h_bytes[g][:, n], in_=h_joined[k, g][:])
 
-        waiting = []
-        done = []
-
-        def second(rows, j, n):
-            if len(waiting) == OUT_BANKS:
-                finish()
-            width = n.stop - n.start
-            ps = ps_o.tile([P, len(rows), width], F32, name="po")
-            run = width if width == 512 else B
-            for x, r in enumerate(rows):
-                for c in range(0, width, run):
-                    cols = slice(n.start + c, n.start + c + run)
-                    for g in range(G):
-                        nc.tensor.matmul_mx(
-                            out=ps[:, x, c : c + run],
-                            lhsT=ltw[:, g, 256 * r : 256 * r + 256].bitcast(E2M1X4), lhsT_scale=lts[:, g, P * r : P * r + P],
-                            rhs=hc[g][j][:, cols].bitcast(E4M3X4), rhs_scale=hs[g][j][:, cols],
-                            start=(g == 0), stop=(g == G - 1))
-            waiting.append((ps, rows, j, n))
-
-        def finish():
-            ps, rows, j, n = waiting.pop(0)
-            width = n.stop - n.start
-            rsl = slice(rows[0], rows[-1] + 1)
-            o = rot.tile([P, len(rows), width], F32, name="ob", bufs=6)
-            done.append(rows)
-            if len(done) % POOL_EVERY == 0 and POOL_FROM <= len(done) < POOL_UNTIL:
-                neg = rot.tile([P, len(rows), width], F32, name="ou", bufs=2)
-                nc.scalar.copy(out=neg[:], in_=ps[:])
-                nc.gpsimd.tensor_tensor(out=o[:], in0=w_sb[j][:, rsl, n], in1=neg[:], op=SUB)
-            else:
-                nc.vector.tensor_tensor(out=o[:], in0=w_sb[j][:, rsl, n], in1=ps[:], op=SUB)
-            nc.sync.dma_start(out=ov[:, rsl, 512 * j + n.start : 512 * j + n.stop], in_=o[:])
-
-        def second_tiles(k):
-            j = k // 2
-            if 2 * k >= NARROW_FROM:
-                return [([r, r + 1], j, slice(256 * (k % 2), 256 * (k % 2) + 256)) for r in range(0, 8, 2)]
-            return [([r], j, slice(0, 512)) for r in range(8)] if k % 2 == 1 else []
-
-        nu = len(units)
-        nk = NB // 2
         ready = []
+        waiting = []
 
-        def on_vector(k, q):
-            return 2 if Q * k + q < VECTOR_UNTIL else ON_VECTOR
+        def second_product(k, r0):
+            if len(waiting) == BANKS:
+                finish_tile()
+            ps = ps_o.tile([P, 2, PAIR], F32, name="bank_o")
+            for x in range(2):
+                r = r0 + x
+                for b in range(2):
+                    n = slice(PAIR * k + B * b, PAIR * k + B * b + B)
+                    for g in range(GROUPS):
+                        nc.tensor.matmul_mx(out=ps[:, x, B * b : B * b + B],
+                                            lhsT=lt_w[:, g, 2 * P * r : 2 * P * r + 2 * P].bitcast(E2M1X4),
+                                            lhsT_scale=lt_s[:, g, P * r : P * r + P],
+                                            rhs=h_codes[g][:, n].bitcast(E4M3X4), rhs_scale=h_bytes[g][:, n],
+                                            start=(g == 0), stop=(g == GROUPS - 1))
+            waiting.append((ps, k, r0))
 
-        def right_jobs(y):
-            k, q = divmod(y + SCALE_AHEAD, 4)
-            if 2 <= k < nk and q < Q:
-                scale_right(k, q, on_vector(k, q))
-            k, q = divmod(y + CAST_AHEAD, 4)
-            if 3 <= k < nk and q < Q:
+        def finish_tile():
+            ps, k, r0 = waiting.pop(0)
+            n = slice(PAIR * (k % 2), PAIR * (k % 2) + PAIR)
+            result = rot.tile([P, 2, PAIR], F32, name="result", bufs=6)
+            nc.vector.tensor_tensor(out=result[:], in0=w_sb[k // 2][:, r0 : r0 + 2, n], in1=ps[:], op=SUB)
+            nc.sync.dma_start(out=out_v[:, r0 : r0 + 2, PAIR * k : PAIR * k + PAIR], in_=result[:])
+
+        def jobs_at(y, ahead):
+            k, q = divmod(y + ahead, SLOTS)
+            return [(k, q)] if 1 <= k < PAIRS and q < PASSES else []
+
+        def widen_right(y):
+            for k, q in jobs_at(y, SCALE_AHEAD):
+                scale_right(k, q)
+            for k, q in jobs_at(y, CAST_AHEAD):
                 cast_right(k, q)
-            k, q = divmod(y + QUANT_AHEAD, 4)
-            if 1 <= k < nk and q < Q:
+
+        def quant_jobs(y):
+            for k, q in jobs_at(y, QUANT_AHEAD):
                 quant_right(k, q)
 
-        for s in range(nu + 3):
-            if s < nu:
+        head = len(units) + 3
+        for s in range(head):
+            if s < len(units):
                 widen_grad(s)
-            if 1 <= s <= nu:
+            if 1 <= s <= len(units):
                 turn_grad(s - 1)
-            if s == 2:
-                spread_scales()
-            if s == 3:
-                scales_ps = turn_scales()
-            if s == 4:
-                leave_scales(scales_ps)
-            if CAST0 <= s < CAST0 + Q:
-                cast_right(0, s - CAST0)
-            if SCALE0 <= s < SCALE0 + Q:
-                scale_right(0, s - SCALE0, HEAD_ON_VECTOR)
-            if CAST1 <= s < CAST1 + Q:
-                cast_right(1, s - CAST1)
-            if s >= nu:
-                scale_right(1, s - nu, PAIR1_ON_VECTOR)
-                cast_right(2, s - nu)
+            if 0 <= s - FIRST_CAST < PASSES:
+                cast_right(0, s - FIRST_CAST)
+            if s == FIRST_SCALE - 3:
+                repeat_scales()
+            if s == FIRST_SCALE - 2:
+                turn_scales()
+            if s == FIRST_SCALE - 1:
+                leave_scales()
+            if 0 <= s - FIRST_SCALE < PASSES:
+                scale_right(0, s - FIRST_SCALE)
+            widen_right(s - head)
+            if 1 <= s <= len(units):
+                leave_grad(s - 1)
             if s >= 3:
                 quant_grad(s - 3)
-            if SCALE0 + 2 <= s < SCALE0 + 2 + Q:
-                quant_right(0, s - SCALE0 - 2)
-            if s == FIRST0:
-                first(0, 0, 0)
-                first(0, 0, 1)
-        right_jobs(-1)
+            if 0 <= s - FIRST_SCALE - 2 < PASSES:
+                quant_right(0, s - FIRST_SCALE - 2)
+            quant_jobs(s - head)
+            if s == len(units):
+                first_product(*slots[0])
+                first_product(*slots[1])
 
-        last = 4 * nk - 1
+        last = len(slots) - 1
         for y in range(last + 3):
-            k, x = divmod(y, 4)
-            g, u = divmod(x, 2)
             if y + 2 <= last:
-                first((y + 2) // 4, (y + 2) // 2 % 2, y % 2)
-            if y >= 2 and u == 0:
-                join_h((y - 2) // 4, (y - 2) // 2 % 2, y > last)
+                first_product(*slots[y + 2])
+            if y >= 2 and y % 2 == 0:
+                join_h(*slots[y - 1][:2])
             if y <= last:
-                step_h(k, g, u)
-            if y >= 3 and u == 1:
-                quant_h((y - 3) // 4, (y - 3) // 2 % 2)
-            if waiting and y not in HOLD:
-                finish()
-            right_jobs(y)
-            if y >= 5 and x == 1:
-                ready.extend(second_tiles(k - 1))
+                step_h(*slots[y])
+            if y >= 3 and y % 2 == 1:
+                quant_h(*slots[y - 2][:2])
+            if waiting and y != last - 1:
+                finish_tile()
+            widen_right(y)
+            quant_jobs(y)
+            if y > SLOTS and y % SLOTS == 1:
+                ready.extend((y // SLOTS - 1, r0) for r0 in range(0, ROW_TILES, 2))
             if ready:
-                second(*ready.pop(0))
-        for z in range(len(ready)):
-            second(*ready.pop(0))
-        for z in range(len(waiting)):
-            finish()
+                second_product(*ready.pop(0))
+        for k, r0 in ready:
+            second_product(k, r0)
+        for x in range(len(waiting)):
+            finish_tile()

@@ -33,7 +33,7 @@ CAST_AHEAD = 10
 SCALE_AHEAD = 7
 QUANT_AHEAD = 5
 FIRST_CAST = 1
-FIRST_SCALE = 5
+FIRST_SCALE = 6
 VECTOR_JOBS = 8
 
 
@@ -61,9 +61,9 @@ def tile_two_sided_preconditioned_step_d4_kernel(
         ident = keep.tile([P, P], F32, name="ident")
         make_identity(nc, ident[:])
         r_rep = keep.tile([P, BLOCKS, 32], F32, name="r_rep")
-        nc.gpsimd.memset(r_rep[:], 0.0)
+        nc.vector.memset(r_rep[:], 0.0)
         lt_s = keep.tile([P, GROUPS, M], U8, name="lt_s", align_bytes=64)
-        nc.gpsimd.memset(lt_s[:].rearrange("p g n -> p (g n)").bitcast(I32), 0)
+        nc.vector.memset(lt_s[:].rearrange("p g n -> p (g n)").bitcast(I32), 0)
 
         g_raw = [[keep.tile([P, 2, N], U8, name="g_raw%d%d" % (g, u)) for u in range(2)] for g in range(GROUPS)]
         r_raw = [[keep.tile([P, 4, PAIR], U8, name="r_raw%d%d" % (k, q)) for q in range(PASSES)] for k in range(PAIRS)]
@@ -176,9 +176,7 @@ def tile_two_sided_preconditioned_step_d4_kernel(
         def vector_blocks(k, q):
             if k < 2:
                 return 1
-            if PASSES * k + q < VECTOR_JOBS:
-                return 2
-            return 1 if q == 0 else 0
+            return 2 if PASSES * k + q < VECTOR_JOBS else 0
 
         def scale_right(k, q):
             on_vector = vector_blocks(k, q)
@@ -312,7 +310,7 @@ def tile_two_sided_preconditioned_step_d4_kernel(
                 step_h(*slots[y])
             if y >= 3 and y % 2 == 1:
                 quant_h(*slots[y - 2][:2])
-            if waiting and y != last - 1:
+            if len(waiting) > 1:
                 finish_tile()
             widen_right(y)
             quant_jobs(y)

@@ -34,7 +34,8 @@ SCALE_AHEAD = 7
 QUANT_AHEAD = 5
 FIRST_CAST = 1
 FIRST_SCALE = 6
-VECTOR_JOBS = 8
+VECTOR_JOBS = 7
+DIRECT_PAIRS = 2
 
 
 def tile_two_sided_preconditioned_step_d4_kernel(
@@ -200,37 +201,46 @@ def tile_two_sided_preconditioned_step_d4_kernel(
         h_codes = [keep.tile([P, N], U32, name="h_codes%d" % g, align_bytes=64) for g in range(GROUPS)]
         h_bytes = [keep.tile([P, N], U8, name="h_bytes%d" % g, align_bytes=64) for g in range(GROUPS)]
         h_ps = {}
-        h_halves = {}
+        h_parts = {}
         h_joined = {}
 
+        def slot_shape(k, u):
+            if k < DIRECT_PAIRS:
+                return range(4), slice(B * u, B * u + B)
+            return range(2 * u, 2 * u + 2), slice(0, PAIR)
+
         def first_product(k, g, u):
-            ps = ps_h.tile([P, 2, PAIR], F32, name="bank_h")
-            for e in range(2):
-                m = slice(P * (2 * u + e), P * (2 * u + e) + P)
+            row_tiles, n = slot_shape(k, u)
+            ps = ps_h.tile([P, len(row_tiles), PASS // len(row_tiles)], F32, name="bank_h")
+            for e, t in enumerate(row_tiles):
+                m = slice(P * t, P * t + P)
                 for q in range(PASSES):
                     nc.tensor.matmul_mx(out=ps[:, e, :],
                                         lhsT=g_codes[g][q][:, m].bitcast(E4M3X4), lhsT_scale=g_bytes[g][q][:, m],
-                                        rhs=r_codes[k][:, q, :].bitcast(E4M3X4), rhs_scale=r_bytes[k][:, q, :],
+                                        rhs=r_codes[k][:, q, n].bitcast(E4M3X4), rhs_scale=r_bytes[k][:, q, n],
                                         start=(q == 0), stop=(q == PASSES - 1))
             h_ps[k, g, u] = ps
 
         def step_h(k, g, u):
+            row_tiles, n = slot_shape(k, u)
             if u == 0:
-                h_halves[k, g] = rot.tile([P, 2, 2 * PAIR], BF16, name="h_halves")
-            steps = step_all[:, PAIR * k : PAIR * k + PAIR].rearrange("p (c i) -> p c i", i=2)
-            nc.vector.tensor_tensor(out=h_halves[k, g][:, u, :].rearrange("p (c i e) -> p c e i", i=2, e=2),
+                h_parts[k, g] = rot.tile([P, 2, PASS], BF16, name="h_parts", align_bytes=64)
+            steps = step_all[:, PAIR * k + n.start : PAIR * k + n.stop].rearrange("p (c i) -> p c i", i=2)
+            nc.vector.tensor_tensor(out=h_parts[k, g][:, u, :].rearrange("p (c i e) -> p c e i", i=2, e=len(row_tiles)),
                                     in0=h_ps[k, g, u][:].rearrange("p e (c i) -> p c e i", i=2),
-                                    in1=steps.unsqueeze(2).to_broadcast([P, PAIR // 2, 2, 2]), op=MULT)
+                                    in1=steps.unsqueeze(2).to_broadcast([P, (n.stop - n.start) // 2, len(row_tiles), 2]),
+                                    op=MULT)
 
         def join_h(k, g):
             x = rot.tile([P, 4 * PAIR], BF16, name="h_joined", align_bytes=64)
             nc.scalar.copy(out=x[:].bitcast(F32).rearrange("p (n u) -> p n u", u=2),
-                           in_=h_halves[k, g][:].bitcast(F32).rearrange("p u n -> p n u"))
+                           in_=h_parts[k, g][:].bitcast(F32).rearrange("p u n -> p n u"))
             h_joined[k, g] = x
 
         def quant_h(k, g):
             n = slice(PAIR * k, PAIR * k + PAIR)
-            nc.vector.quantize_mx(out=h_codes[g][:, n].bitcast(E4M3X4), scales=h_bytes[g][:, n], in_=h_joined[k, g][:])
+            src = h_parts[k, g][:].rearrange("p u n -> p (u n)") if k < DIRECT_PAIRS else h_joined[k, g][:]
+            nc.vector.quantize_mx(out=h_codes[g][:, n].bitcast(E4M3X4), scales=h_bytes[g][:, n], in_=src)
 
         ready = []
         waiting = []
@@ -304,7 +314,7 @@ def tile_two_sided_preconditioned_step_d4_kernel(
         for y in range(last + 3):
             if y + 2 <= last:
                 first_product(*slots[y + 2])
-            if y >= 2 and y % 2 == 0:
+            if y > SLOTS * DIRECT_PAIRS and y % 2 == 0:
                 join_h(*slots[y - 1][:2])
             if y <= last:
                 step_h(*slots[y])

@@ -30,12 +30,22 @@ BANKS = 4
 SLOTS = 4
 
 CAST_AHEAD = 10
-SCALE_AHEAD = 7
+SCALE_AHEAD = 8
 QUANT_AHEAD = 5
 FIRST_CAST = 1
-FIRST_SCALE = 6
-VECTOR_JOBS = 7
-DIRECT_PAIRS = 2
+FIRST_SCALE = 5
+VEC = [1] * 6
+WARM_UPS = {}
+BACKLOG = 2
+TWO_EVERY = 2
+LOADS = 1
+FORMS = "DDDDJJ"
+SECOND = [2, 4, 4, 2]
+EARLY = 12
+POOL_FROM = 24
+POOL_TO = 24
+POOL_EVERY = 2
+HELD = 1
 
 
 def tile_two_sided_preconditioned_step_d4_kernel(
@@ -68,7 +78,9 @@ def tile_two_sided_preconditioned_step_d4_kernel(
 
         g_raw = [[keep.tile([P, 2, N], U8, name="g_raw%d%d" % (g, u)) for u in range(2)] for g in range(GROUPS)]
         r_raw = [[keep.tile([P, 4, PAIR], U8, name="r_raw%d%d" % (k, q)) for q in range(PASSES)] for k in range(PAIRS)]
-        w_sb = [keep.tile([P, ROW_TILES, PASS], BF16, name="w_sb%d" % j) for j in range(PASSES)]
+        w_sb = [keep.tile([P, ROW_TILES, PAIR], BF16, name="w_sb0"), keep.tile([P, ROW_TILES, PASS], BF16, name="w_sb1"),
+                keep.tile([P, ROW_TILES, PASS], BF16, name="w_sb2"), keep.tile([P, ROW_TILES, PAIR], BF16, name="w_sb3")]
+        w_from = [0, PAIR, PAIR + PASS, N - PAIR, N]
         lt_w = keep.tile([P, GROUPS, 2 * M], U8, name="lt_w", align_bytes=64)
         step_all = keep.tile([P, N], BF16, name="step_all")
 
@@ -84,14 +96,31 @@ def tile_two_sided_preconditioned_step_d4_kernel(
 
         def load_w(j):
             for r in range(0, ROW_TILES, 4):
-                nc.sync.dma_start(out=w_sb[j][:, r : r + 4, :], in_=w_v[:, r : r + 4, PASS * j : PASS * j + PASS])
+                nc.sync.dma_start(out=w_sb[j][:, r : r + 4, :], in_=w_v[:, r : r + 4, w_from[j] : w_from[j + 1]])
 
-        load_grad(0, 0, 0, PASS)
-        load_right(0, 0)
-        load_grad(0, 0, PASS, N)
-        load_right(0, 1)
-        load_grad(0, 1, 0, N)
-        load_right(0, 2)
+        if LOADS == 0:
+            load_grad(0, 0, 0, PASS)
+            load_right(0, 0)
+            load_grad(0, 0, PASS, N)
+            load_right(0, 1)
+            load_grad(0, 1, 0, N)
+            load_right(0, 2)
+        if LOADS == 1:
+            load_grad(0, 0, 0, PASS)
+            load_grad(0, 0, PASS, 2 * PASS)
+            load_right(0, 0)
+            load_grad(0, 0, 2 * PASS, N)
+            load_grad(0, 1, 0, PASS)
+            load_right(0, 1)
+            load_grad(0, 1, PASS, N)
+            load_right(0, 2)
+        if LOADS == 2:
+            load_grad(0, 0, 0, PASS)
+            load_grad(0, 0, PASS, N)
+            load_right(0, 0)
+            load_grad(0, 1, 0, N)
+            load_right(0, 1)
+            load_right(0, 2)
         load_grad(1, 0, 0, N)
         load_grad(1, 1, 0, N)
         load_pair(1)
@@ -101,12 +130,13 @@ def tile_two_sided_preconditioned_step_d4_kernel(
             nc.sync.dma_start(out=lt_s[32 * s : 32 * s + 4, :, :].bitcast(I32),
                               in_=lt_scales.rearrange("g (s r) n -> s r g n", s=4)[s].bitcast(I32))
         nc.sync.dma_start(out=lt_w[:], in_=lt_words.rearrange("g p n -> p g n"))
-        load_pair(3)
         load_w(0)
+        load_pair(3)
+        load_w(1)
         load_pair(4)
         load_pair(5)
-        load_w(1)
         load_w(2)
+        load_w(3)
 
         r_scale = keep.tile([P, PASSES, BLOCKS], F32, name="r_scale")
         r_scale_ps = []
@@ -153,6 +183,12 @@ def tile_two_sided_preconditioned_step_d4_kernel(
                     nc.tensor.transpose(ps[:, e, h, :], words[:, P * h : P * h + P], ident[:])
             g_ps[s] = ps
 
+        def warm_up(count):
+            ps = ps_h.tile([P, PASS], F32, name="bank_h")
+            planes = r_planes[0, 2][:].rearrange("p t n -> p (t n)")
+            for x in range(count):
+                nc.tensor.matmul(out=ps[:], lhsT=planes[:, 0:P], rhs=planes[:, 0:PASS], start=True, stop=True)
+
         def leave_grad(s):
             x = rot.tile([P, 2 * PASS], BF16, name="g_turned", align_bytes=64, bufs=4)
             nc.scalar.copy(out=x[:].bitcast(F32).rearrange("p (e m h) -> p e m h", e=2, h=2),
@@ -175,9 +211,8 @@ def tile_two_sided_preconditioned_step_d4_kernel(
                            in_=r_raw[k][q][:].rearrange("p t n -> p (t n)").bitcast(E4M3))
 
         def vector_blocks(k, q):
-            if k < 2:
-                return 1
-            return 2 if PASSES * k + q < VECTOR_JOBS else 0
+            j = PASSES * k + q
+            return VEC[j] if j < len(VEC) else 0
 
         def scale_right(k, q):
             on_vector = vector_blocks(k, q)
@@ -203,9 +238,11 @@ def tile_two_sided_preconditioned_step_d4_kernel(
         h_ps = {}
         h_parts = {}
         h_joined = {}
+        starts = [sum(SECOND[:j]) for j in range(len(SECOND))]
+        fine = [k for k in range(PAIRS) if 2 * k + 1 in starts]
 
         def slot_shape(k, u):
-            if k < DIRECT_PAIRS:
+            if FORMS[k] == "D":
                 return range(4), slice(B * u, B * u + B)
             return range(2 * u, 2 * u + 2), slice(0, PAIR)
 
@@ -224,7 +261,7 @@ def tile_two_sided_preconditioned_step_d4_kernel(
         def step_h(k, g, u):
             row_tiles, n = slot_shape(k, u)
             if u == 0:
-                h_parts[k, g] = rot.tile([P, 2, PASS], BF16, name="h_parts", align_bytes=64)
+                h_parts[k, g] = rot.tile([P, 2, PASS], BF16, name="h_parts", align_bytes=64, bufs=4)
             steps = step_all[:, PAIR * k + n.start : PAIR * k + n.stop].rearrange("p (c i) -> p c i", i=2)
             nc.vector.tensor_tensor(out=h_parts[k, g][:, u, :].rearrange("p (c i e) -> p c e i", i=2, e=len(row_tiles)),
                                     in0=h_ps[k, g, u][:].rearrange("p e (c i) -> p c e i", i=2),
@@ -237,36 +274,64 @@ def tile_two_sided_preconditioned_step_d4_kernel(
                            in_=h_parts[k, g][:].bitcast(F32).rearrange("p u n -> p n u"))
             h_joined[k, g] = x
 
-        def quant_h(k, g):
-            n = slice(PAIR * k, PAIR * k + PAIR)
-            src = h_parts[k, g][:].rearrange("p u n -> p (u n)") if k < DIRECT_PAIRS else h_joined[k, g][:]
+        def quant_h(k, g, u):
+            if k in fine and g == 1:
+                n = slice(PAIR * k + B * u, PAIR * k + B * u + B)
+                src = h_parts[k, g][:, u, :]
+            elif u == 1:
+                n = slice(PAIR * k, PAIR * k + PAIR)
+                src = h_parts[k, g][:].rearrange("p u n -> p (u n)") if FORMS[k] == "D" else h_joined[k, g][:]
+            else:
+                return
             nc.vector.quantize_mx(out=h_codes[g][:, n].bitcast(E4M3X4), scales=h_bytes[g][:, n], in_=src)
+            if g == 1:
+                for j, b0 in enumerate(starts):
+                    if B * (b0 + SECOND[j]) == n.stop:
+                        ready.extend((b0, SECOND[j], r0) for r0 in range(0, ROW_TILES, 4 // SECOND[j]))
 
         ready = []
         waiting = []
+        late = []
+        done = []
 
-        def second_product(k, r0):
+        def second_product(b0, nb, r0):
             if len(waiting) == BANKS:
                 finish_tile()
-            ps = ps_o.tile([P, 2, PAIR], F32, name="bank_o")
-            for x in range(2):
+            rows = 4 // nb
+            ps = ps_o.tile([P, rows, B * nb], F32, name="bank_o")
+            wide = PASS if nb == 4 else B
+            for x in range(rows):
                 r = r0 + x
-                for b in range(2):
-                    n = slice(PAIR * k + B * b, PAIR * k + B * b + B)
+                for c in range(0, B * nb, wide):
+                    n = slice(B * b0 + c, B * b0 + c + wide)
                     for g in range(GROUPS):
-                        nc.tensor.matmul_mx(out=ps[:, x, B * b : B * b + B],
+                        nc.tensor.matmul_mx(out=ps[:, x, c : c + wide],
                                             lhsT=lt_w[:, g, 2 * P * r : 2 * P * r + 2 * P].bitcast(E2M1X4),
                                             lhsT_scale=lt_s[:, g, P * r : P * r + P],
                                             rhs=h_codes[g][:, n].bitcast(E4M3X4), rhs_scale=h_bytes[g][:, n],
                                             start=(g == 0), stop=(g == GROUPS - 1))
-            waiting.append((ps, k, r0))
+            waiting.append((ps, b0, nb, r0))
+
+        def store(result, b0, nb, r0):
+            nc.sync.dma_start(out=out_v[:, r0 : r0 + 4 // nb, B * b0 : B * (b0 + nb)], in_=result[:])
 
         def finish_tile():
-            ps, k, r0 = waiting.pop(0)
-            n = slice(PAIR * (k % 2), PAIR * (k % 2) + PAIR)
-            result = rot.tile([P, 2, PAIR], F32, name="result", bufs=6)
-            nc.vector.tensor_tensor(out=result[:], in0=w_sb[k // 2][:, r0 : r0 + 2, n], in1=ps[:], op=SUB)
-            nc.sync.dma_start(out=out_v[:, r0 : r0 + 2, PAIR * k : PAIR * k + PAIR], in_=result[:])
+            ps, b0, nb, r0 = waiting.pop(0)
+            rows = 4 // nb
+            j = max(x for x in range(4) if w_from[x] <= B * b0)
+            w_part = w_sb[j][:, r0 : r0 + rows, B * b0 - w_from[j] : B * (b0 + nb) - w_from[j]]
+            result = rot.tile([P, rows, B * nb], F32, name="result", bufs=8)
+            x = len(done)
+            done.append(x)
+            if POOL_FROM <= x < POOL_TO and (x - POOL_FROM) % POOL_EVERY == 0:
+                nc.scalar.copy(out=result[:], in_=ps[:])
+                nc.gpsimd.tensor_tensor(out=result[:], in0=w_part, in1=result[:], op=SUB)
+                late.append((x, result, b0, nb, r0))
+            else:
+                nc.vector.tensor_tensor(out=result[:], in0=w_part, in1=ps[:], op=SUB)
+                store(result, b0, nb, r0)
+            if late and late[0][0] + 2 <= x:
+                store(*late.pop(0)[1:])
 
         def jobs_at(y, ahead):
             k, q = divmod(y + ahead, SLOTS)
@@ -282,12 +347,21 @@ def tile_two_sided_preconditioned_step_d4_kernel(
             for k, q in jobs_at(y, QUANT_AHEAD):
                 quant_right(k, q)
 
-        head = len(units) + 3
-        for s in range(head):
+        head = len(units) + 1
+        last = len(slots) - 1
+        for s in range(head + last + 5):
+            y = s - head
             if s < len(units):
                 widen_grad(s)
             if 1 <= s <= len(units):
                 turn_grad(s - 1)
+            if s in WARM_UPS:
+                warm_up(WARM_UPS[s])
+            if s == EARLY:
+                first_product(*slots[0])
+                first_product(*slots[1])
+            if 2 <= y - 0 and y <= last:
+                first_product(*slots[y])
             if 0 <= s - FIRST_CAST < PASSES:
                 cast_right(0, s - FIRST_CAST)
             if s == FIRST_SCALE - 3:
@@ -298,37 +372,38 @@ def tile_two_sided_preconditioned_step_d4_kernel(
                 leave_scales()
             if 0 <= s - FIRST_SCALE < PASSES:
                 scale_right(0, s - FIRST_SCALE)
-            widen_right(s - head)
+            z = y - 2
+            if z < 0:
+                widen_right(z)
             if 1 <= s <= len(units):
                 leave_grad(s - 1)
-            if s >= 3:
+            if 3 <= s < len(units) + 3:
                 quant_grad(s - 3)
             if 0 <= s - FIRST_SCALE - 2 < PASSES:
                 quant_right(0, s - FIRST_SCALE - 2)
-            quant_jobs(s - head)
-            if s == len(units):
-                first_product(*slots[0])
-                first_product(*slots[1])
-
-        last = len(slots) - 1
-        for y in range(last + 3):
-            if y + 2 <= last:
-                first_product(*slots[y + 2])
-            if y > SLOTS * DIRECT_PAIRS and y % 2 == 0:
-                join_h(*slots[y - 1][:2])
-            if y <= last:
-                step_h(*slots[y])
-            if y >= 3 and y % 2 == 1:
-                quant_h(*slots[y - 2][:2])
-            if len(waiting) > 1:
+            if z < 0:
+                quant_jobs(z)
+                continue
+            if 1 <= z <= last + 1 and slots[z - 1][2] == 1 and FORMS[slots[z - 1][0]] == "J":
+                join_h(*slots[z - 1][:2])
+            if z <= last:
+                step_h(*slots[z])
+            for back in (1, 2):
+                if 0 <= z - back <= last and (FORMS[slots[z - back][0]] == "J") == (back == 2):
+                    quant_h(*slots[z - back])
+            if len(waiting) > HELD:
                 finish_tile()
-            widen_right(y)
-            quant_jobs(y)
-            if y > SLOTS and y % SLOTS == 1:
-                ready.extend((y // SLOTS - 1, r0) for r0 in range(0, ROW_TILES, 2))
+            widen_right(z)
+            quant_jobs(z)
             if ready:
                 second_product(*ready.pop(0))
-        for k, r0 in ready:
-            second_product(k, r0)
+            if len(ready) > BACKLOG and z % TWO_EVERY == 0:
+                if len(waiting) > HELD + 1:
+                    finish_tile()
+                second_product(*ready.pop(0))
+        for tile in list(ready):
+            second_product(*tile)
         for x in range(len(waiting)):
             finish_tile()
+        for x in late:
+            store(*x[1:])

@@ -29,23 +29,31 @@ ROW_TILES = M // P
 BANKS = 4
 SLOTS = 4
 
-CAST_AHEAD = 10
-SCALE_AHEAD = 8
-QUANT_AHEAD = 5
-FIRST_CAST = 1
-FIRST_SCALE = 5
-VEC = [1] * 6
+CAST_AHEAD = 8
+SCALE_AHEAD = 5
+QUANT_AHEAD = 3
+CASTS = [1, 6]
+SCALES = [5, 9]
+QUANTS = [7, 10]
+SPREAD = 2
+VEC = [1] * 11
 WARM_UPS = {}
-BACKLOG = 2
+BACKLOG = 1
 TWO_EVERY = 2
 LOADS = 1
-FORMS = "DDDDJJ"
-SECOND = [2, 4, 4, 2]
-EARLY = 12
+FORMS = "JJJJJJ"
+SECOND = [2, 2, 2, 4, 2]
+FIRST_SLOT = 10
+STEP_LAG = 2
+GQ_LAG = 3
+CROSS = 2
 POOL_FROM = 24
 POOL_TO = 24
 POOL_EVERY = 2
 HELD = 1
+ORDER = 1
+SPLIT_LAST = 0
+ALIGN = 64
 
 
 def tile_two_sided_preconditioned_step_d4_kernel(
@@ -73,7 +81,7 @@ def tile_two_sided_preconditioned_step_d4_kernel(
         make_identity(nc, ident[:])
         r_rep = keep.tile([P, BLOCKS, 32], F32, name="r_rep")
         nc.vector.memset(r_rep[:], 0.0)
-        lt_s = keep.tile([P, GROUPS, M], U8, name="lt_s", align_bytes=64)
+        lt_s = keep.tile([P, GROUPS, M], U8, name="lt_s", align_bytes=ALIGN)
         nc.vector.memset(lt_s[:].rearrange("p g n -> p (g n)").bitcast(I32), 0)
 
         g_raw = [[keep.tile([P, 2, N], U8, name="g_raw%d%d" % (g, u)) for u in range(2)] for g in range(GROUPS)]
@@ -81,7 +89,7 @@ def tile_two_sided_preconditioned_step_d4_kernel(
         w_sb = [keep.tile([P, ROW_TILES, PAIR], BF16, name="w_sb0"), keep.tile([P, ROW_TILES, PASS], BF16, name="w_sb1"),
                 keep.tile([P, ROW_TILES, PASS], BF16, name="w_sb2"), keep.tile([P, ROW_TILES, PAIR], BF16, name="w_sb3")]
         w_from = [0, PAIR, PAIR + PASS, N - PAIR, N]
-        lt_w = keep.tile([P, GROUPS, 2 * M], U8, name="lt_w", align_bytes=64)
+        lt_w = keep.tile([P, GROUPS, 2 * M], U8, name="lt_w", align_bytes=ALIGN)
         step_all = keep.tile([P, N], BF16, name="step_all")
 
         def load_grad(g, u, lo, hi):
@@ -154,9 +162,9 @@ def tile_two_sided_preconditioned_step_d4_kernel(
             nc.scalar.copy(out=r_scale[:], in_=r_scale_ps[0][:, :, 0:BLOCKS])
 
         units = [(g, u, q) for g in range(GROUPS) for u in range(2) for q in range(PASSES)]
-        g_codes = [[keep.tile([P, PASS], U32, name="g_codes%d%d" % (g, q), align_bytes=64) for q in range(PASSES)]
+        g_codes = [[keep.tile([P, PASS], U32, name="g_codes%d%d" % (g, q), align_bytes=ALIGN) for q in range(PASSES)]
                    for g in range(GROUPS)]
-        g_bytes = [[keep.tile([P, PASS], U8, name="g_bytes%d%d" % (g, q), align_bytes=64) for q in range(PASSES)]
+        g_bytes = [[keep.tile([P, PASS], U8, name="g_bytes%d%d" % (g, q), align_bytes=ALIGN) for q in range(PASSES)]
                    for g in range(GROUPS)]
         g_wide = {}
         g_ps = {}
@@ -190,7 +198,7 @@ def tile_two_sided_preconditioned_step_d4_kernel(
                 nc.tensor.matmul(out=ps[:], lhsT=planes[:, 0:P], rhs=planes[:, 0:PASS], start=True, stop=True)
 
         def leave_grad(s):
-            x = rot.tile([P, 2 * PASS], BF16, name="g_turned", align_bytes=64, bufs=4)
+            x = rot.tile([P, 2 * PASS], BF16, name="g_turned", align_bytes=ALIGN, bufs=4)
             nc.scalar.copy(out=x[:].bitcast(F32).rearrange("p (e m h) -> p e m h", e=2, h=2),
                            in_=g_ps[s][:].rearrange("p e h m -> p e m h"))
             g_turned[s] = x
@@ -216,7 +224,7 @@ def tile_two_sided_preconditioned_step_d4_kernel(
 
         def scale_right(k, q):
             on_vector = vector_blocks(k, q)
-            r_wide[k, q] = rot.tile([P, 4 * PAIR], BF16, name="r_wide", align_bytes=64, bufs=6)
+            r_wide[k, q] = rot.tile([P, 4 * PAIR], BF16, name="r_wide", align_bytes=ALIGN, bufs=6)
             for b in range(2):
                 dst = r_wide[k, q][:, 4 * B * b : 4 * B * b + 4 * B].rearrange("p (c i t) -> p c t i", t=4, i=4)
                 src = r_planes[k, q][:, :, B * b : B * b + B].rearrange("p t (c i) -> p c t i", i=4)
@@ -228,13 +236,17 @@ def tile_two_sided_preconditioned_step_d4_kernel(
 
         def quant_right(k, q):
             if q == 0:
-                r_codes[k] = keep.tile([P, PASSES, PAIR], U32, name="r_codes%d" % k, align_bytes=64)
-                r_bytes[k] = keep.tile([P, PASSES, PAIR], U8, name="r_bytes%d" % k, align_bytes=64)
+                r_codes[k] = keep.tile([P, PASSES, PAIR], U32, name="r_codes%d" % k, align_bytes=ALIGN)
+                r_bytes[k] = keep.tile([P, PASSES, PAIR], U8, name="r_bytes%d" % k, align_bytes=ALIGN)
             nc.vector.quantize_mx(out=r_codes[k][:, q, :].bitcast(E4M3X4), scales=r_bytes[k][:, q, :], in_=r_wide[k, q][:])
 
         slots = [(k, g, u) for k in range(PAIRS) for g in range(GROUPS) for u in range(2)]
-        h_codes = [keep.tile([P, N], U32, name="h_codes%d" % g, align_bytes=64) for g in range(GROUPS)]
-        h_bytes = [keep.tile([P, N], U8, name="h_bytes%d" % g, align_bytes=64) for g in range(GROUPS)]
+        if CROSS == 1:
+            slots = [(k, g, u) for g in range(GROUPS) for k in range(2) for u in range(2)] + slots[8:]
+        if CROSS == 2:
+            slots = slots[0:3] + slots[4:6] + [slots[3]] + slots[6:]
+        h_codes = [keep.tile([P, N], U32, name="h_codes%d" % g, align_bytes=ALIGN) for g in range(GROUPS)]
+        h_bytes = [keep.tile([P, N], U8, name="h_bytes%d" % g, align_bytes=ALIGN) for g in range(GROUPS)]
         h_ps = {}
         h_parts = {}
         h_joined = {}
@@ -261,7 +273,7 @@ def tile_two_sided_preconditioned_step_d4_kernel(
         def step_h(k, g, u):
             row_tiles, n = slot_shape(k, u)
             if u == 0:
-                h_parts[k, g] = rot.tile([P, 2, PASS], BF16, name="h_parts", align_bytes=64, bufs=4)
+                h_parts[k, g] = rot.tile([P, 2, PASS], BF16, name="h_parts", align_bytes=ALIGN, bufs=4)
             steps = step_all[:, PAIR * k + n.start : PAIR * k + n.stop].rearrange("p (c i) -> p c i", i=2)
             nc.vector.tensor_tensor(out=h_parts[k, g][:, u, :].rearrange("p (c i e) -> p c e i", i=2, e=len(row_tiles)),
                                     in0=h_ps[k, g, u][:].rearrange("p e (c i) -> p c e i", i=2),
@@ -269,7 +281,7 @@ def tile_two_sided_preconditioned_step_d4_kernel(
                                     op=MULT)
 
         def join_h(k, g):
-            x = rot.tile([P, 4 * PAIR], BF16, name="h_joined", align_bytes=64)
+            x = rot.tile([P, 4 * PAIR], BF16, name="h_joined", align_bytes=ALIGN)
             nc.scalar.copy(out=x[:].bitcast(F32).rearrange("p (n u) -> p n u", u=2),
                            in_=h_parts[k, g][:].bitcast(F32).rearrange("p u n -> p n u"))
             h_joined[k, g] = x
@@ -287,17 +299,19 @@ def tile_two_sided_preconditioned_step_d4_kernel(
             if g == 1:
                 for j, b0 in enumerate(starts):
                     if B * (b0 + SECOND[j]) == n.stop:
-                        ready.extend((b0, SECOND[j], r0) for r0 in range(0, ROW_TILES, 4 // SECOND[j]))
+                        rows = 4 // SECOND[j]
+                        whole = ROW_TILES - (SPLIT_LAST * rows if n.stop == N else 0)
+                        ready.extend((b0, SECOND[j], r0, rows) for r0 in range(0, whole, rows))
+                        ready.extend((b0, SECOND[j], r0, rows // 2) for r0 in range(whole, ROW_TILES, rows // 2 or 1))
 
         ready = []
         waiting = []
         late = []
         done = []
 
-        def second_product(b0, nb, r0):
+        def second_product(b0, nb, r0, rows):
             if len(waiting) == BANKS:
                 finish_tile()
-            rows = 4 // nb
             ps = ps_o.tile([P, rows, B * nb], F32, name="bank_o")
             wide = PASS if nb == 4 else B
             for x in range(rows):
@@ -310,14 +324,13 @@ def tile_two_sided_preconditioned_step_d4_kernel(
                                             lhsT_scale=lt_s[:, g, P * r : P * r + P],
                                             rhs=h_codes[g][:, n].bitcast(E4M3X4), rhs_scale=h_bytes[g][:, n],
                                             start=(g == 0), stop=(g == GROUPS - 1))
-            waiting.append((ps, b0, nb, r0))
+            waiting.append((ps, b0, nb, r0, rows))
 
-        def store(result, b0, nb, r0):
-            nc.sync.dma_start(out=out_v[:, r0 : r0 + 4 // nb, B * b0 : B * (b0 + nb)], in_=result[:])
+        def store(result, b0, nb, r0, rows):
+            nc.sync.dma_start(out=out_v[:, r0 : r0 + rows, B * b0 : B * (b0 + nb)], in_=result[:])
 
         def finish_tile():
-            ps, b0, nb, r0 = waiting.pop(0)
-            rows = 4 // nb
+            ps, b0, nb, r0, rows = waiting.pop(0)
             j = max(x for x in range(4) if w_from[x] <= B * b0)
             w_part = w_sb[j][:, r0 : r0 + rows, B * b0 - w_from[j] : B * (b0 + nb) - w_from[j]]
             result = rot.tile([P, rows, B * nb], F32, name="result", bufs=8)
@@ -326,78 +339,71 @@ def tile_two_sided_preconditioned_step_d4_kernel(
             if POOL_FROM <= x < POOL_TO and (x - POOL_FROM) % POOL_EVERY == 0:
                 nc.scalar.copy(out=result[:], in_=ps[:])
                 nc.gpsimd.tensor_tensor(out=result[:], in0=w_part, in1=result[:], op=SUB)
-                late.append((x, result, b0, nb, r0))
+                late.append((x, result, b0, nb, r0, rows))
             else:
                 nc.vector.tensor_tensor(out=result[:], in0=w_part, in1=ps[:], op=SUB)
-                store(result, b0, nb, r0)
+                store(result, b0, nb, r0, rows)
             if late and late[0][0] + 2 <= x:
                 store(*late.pop(0)[1:])
 
-        def jobs_at(y, ahead):
-            k, q = divmod(y + ahead, SLOTS)
-            return [(k, q)] if 1 <= k < PAIRS and q < PASSES else []
+        def jobs_at(s, ahead, early):
+            jobs = [(k, s - early[k]) for k in range(2) if 0 <= s - early[k] < PASSES]
+            k, q = divmod(s - FIRST_SLOT + ahead, SLOTS)
+            return jobs + ([(k, q)] if 2 <= k < PAIRS and q < PASSES else [])
 
-        def widen_right(y):
-            for k, q in jobs_at(y, SCALE_AHEAD):
-                scale_right(k, q)
-            for k, q in jobs_at(y, CAST_AHEAD):
-                cast_right(k, q)
-
-        def quant_jobs(y):
-            for k, q in jobs_at(y, QUANT_AHEAD):
-                quant_right(k, q)
-
-        head = len(units) + 1
+        nu = len(units)
         last = len(slots) - 1
-        for s in range(head + last + 5):
-            y = s - head
-            if s < len(units):
+        joins = {}
+        quants = {}
+        for s in range(FIRST_SLOT + last + STEP_LAG + 3):
+            y = s - FIRST_SLOT
+            z = y - STEP_LAG
+            if s < nu:
                 widen_grad(s)
-            if 1 <= s <= len(units):
+            if 1 <= s <= nu:
                 turn_grad(s - 1)
             if s in WARM_UPS:
                 warm_up(WARM_UPS[s])
-            if s == EARLY:
-                first_product(*slots[0])
-                first_product(*slots[1])
-            if 2 <= y - 0 and y <= last:
+            if 0 <= y <= last:
                 first_product(*slots[y])
-            if 0 <= s - FIRST_CAST < PASSES:
-                cast_right(0, s - FIRST_CAST)
-            if s == FIRST_SCALE - 3:
+            if s == SPREAD:
                 repeat_scales()
-            if s == FIRST_SCALE - 2:
+            if s == SPREAD + 1:
                 turn_scales()
-            if s == FIRST_SCALE - 1:
+            if s == SPREAD + 2:
                 leave_scales()
-            if 0 <= s - FIRST_SCALE < PASSES:
-                scale_right(0, s - FIRST_SCALE)
-            z = y - 2
-            if z < 0:
-                widen_right(z)
-            if 1 <= s <= len(units):
+            if s in joins:
+                join_h(*joins[s])
+            if s > nu // 2 and s <= nu:
                 leave_grad(s - 1)
-            if 3 <= s < len(units) + 3:
-                quant_grad(s - 3)
-            if 0 <= s - FIRST_SCALE - 2 < PASSES:
-                quant_right(0, s - FIRST_SCALE - 2)
-            if z < 0:
-                quant_jobs(z)
-                continue
-            if 1 <= z <= last + 1 and slots[z - 1][2] == 1 and FORMS[slots[z - 1][0]] == "J":
-                join_h(*slots[z - 1][:2])
-            if z <= last:
+            if 0 <= z <= last:
                 step_h(*slots[z])
-            for back in (1, 2):
-                if 0 <= z - back <= last and (FORMS[slots[z - back][0]] == "J") == (back == 2):
-                    quant_h(*slots[z - back])
-            if len(waiting) > HELD:
+                k, g, u = slots[z]
+                if FORMS[k] == "J":
+                    if u == 1:
+                        joins[s + 1] = (k, g)
+                        quants[s + 2] = slots[z]
+                else:
+                    quants[s + 1] = slots[z]
+            if ORDER == 1 and len(waiting) > HELD:
                 finish_tile()
-            widen_right(z)
-            quant_jobs(z)
+            if s in quants:
+                quant_h(*quants[s])
+            if ORDER == 0 and len(waiting) > HELD:
+                finish_tile()
+            for k, q in jobs_at(s, SCALE_AHEAD, SCALES):
+                scale_right(k, q)
+            for k, q in jobs_at(s, CAST_AHEAD, CASTS):
+                cast_right(k, q)
+            if 1 <= s <= nu // 2:
+                leave_grad(s - 1)
+            if GQ_LAG <= s < nu + GQ_LAG:
+                quant_grad(s - GQ_LAG)
+            for k, q in jobs_at(s, QUANT_AHEAD, QUANTS):
+                quant_right(k, q)
             if ready:
                 second_product(*ready.pop(0))
-            if len(ready) > BACKLOG and z % TWO_EVERY == 0:
+            if len(ready) > BACKLOG and s % TWO_EVERY == 0:
                 if len(waiting) > HELD + 1:
                     finish_tile()
                 second_product(*ready.pop(0))

@@ -32,21 +32,21 @@ SLOTS = 4
 CAST_AHEAD = 8
 SCALE_AHEAD = 5
 QUANT_AHEAD = 3
-CASTS = [1, 6]
-SCALES = [5, 9]
-QUANTS = [7, 10]
+CASTS = [1,8]
+SCALES = [5,11]
+QUANTS = [7,13]
 SPREAD = 2
-VEC = [1] * 11
+VEC = [0, 1, 1, 1, 1, 1, 1, 1]
 WARM_UPS = {}
-BACKLOG = 1
+BACKLOG = 0
 TWO_EVERY = 2
 LOADS = 1
-FORMS = "JJJJJJ"
-SECOND = [2, 2, 2, 4, 2]
-FIRST_SLOT = 10
+FORMS = "DDJJJJ"
+SECOND = [2]*6
+FIRST_SLOT = 13
 STEP_LAG = 2
 GQ_LAG = 3
-CROSS = 2
+CROSS = 0
 POOL_FROM = 24
 POOL_TO = 24
 POOL_EVERY = 2
@@ -54,6 +54,22 @@ HELD = 1
 ORDER = 1
 SPLIT_LAST = 0
 ALIGN = 64
+HEAD_LOADS = "0x1y2z34567"
+EARLY = 12
+HALVES = 0
+COLS_LATE = 0
+R_LOADS = [1,1,1,1,2]
+CAST_GAP = 2
+SPREAD_STEP = {}
+STEP_ROW = 1
+W_LAST = 0
+SWITCH = 99
+SWITCH2 = 16
+RES_BUFS = 10
+TWO_FROM = 16
+STEP_SPLIT = 1
+W_LATE = {}
+W_TILES = [4,8]
 
 
 def tile_two_sided_preconditioned_step_d4_kernel(
@@ -74,8 +90,9 @@ def tile_two_sided_preconditioned_step_d4_kernel(
         g_scale = keep.tile([P, GROUPS, 4 * BLOCKS], F32, name="g_scale")
         nc.scalar.dma_start(out=g_scale[:], in_=grad_scale.rearrange("(g p t) c -> p g (t c)", p=P, t=4))
         r_cols = keep.tile([BLOCKS, BLOCKS], F32, name="r_cols")
-        with nc.allow_non_contiguous_dma(reason="144 scales, turned while they load"):
-            nc.scalar.dma_start(out=r_cols[:], in_=right_scale.rearrange("a c -> c a"))
+        if "c" not in HEAD_LOADS:
+            with nc.allow_non_contiguous_dma(reason="144 scales, turned while they load"):
+                nc.scalar.dma_start(out=r_cols[:], in_=right_scale.rearrange("a c -> c a"))
 
         ident = keep.tile([P, P], F32, name="ident")
         make_identity(nc, ident[:])
@@ -84,67 +101,87 @@ def tile_two_sided_preconditioned_step_d4_kernel(
         lt_s = keep.tile([P, GROUPS, M], U8, name="lt_s", align_bytes=ALIGN)
         nc.vector.memset(lt_s[:].rearrange("p g n -> p (g n)").bitcast(I32), 0)
 
-        g_raw = [[keep.tile([P, 2, N], U8, name="g_raw%d%d" % (g, u)) for u in range(2)] for g in range(GROUPS)]
-        r_raw = [[keep.tile([P, 4, PAIR], U8, name="r_raw%d%d" % (k, q)) for q in range(PASSES)] for k in range(PAIRS)]
-        w_sb = [keep.tile([P, ROW_TILES, PAIR], BF16, name="w_sb0"), keep.tile([P, ROW_TILES, PASS], BF16, name="w_sb1"),
-                keep.tile([P, ROW_TILES, PASS], BF16, name="w_sb2"), keep.tile([P, ROW_TILES, PAIR], BF16, name="w_sb3")]
-        w_from = [0, PAIR, PAIR + PASS, N - PAIR, N]
+        if SPREAD_STEP:
+            step_row = keep.tile([P, N], BF16, name="step_row")
+            ones = keep.tile([P, P], BF16, name="ones")
+            nc.vector.memset(step_row[:].bitcast(I32), 0)
+            nc.vector.memset(ones[:], 1.0)
+
+        def spread_step(j):
+            ps = ps_h.tile([P, PASS], BF16, name="bank_h")
+            nc.tensor.matmul(out=ps[:], lhsT=ones[:], rhs=step_row[:, PASS * j : PASS * j + PASS], start=True, stop=True)
+            nc.scalar.copy(out=step_all[:, PASS * j : PASS * j + PASS], in_=ps[:])
+
+        g_raw = [[keep.tile([P, N], U8, name="g_raw%d%d" % (g, t)) for t in range(4)] for g in range(GROUPS)]
+        r_first = [sum(R_LOADS[:j]) for j in range(len(R_LOADS))]
+        r_raw = {k: [keep.tile([P, 4, PAIR * x], U8, name="r_raw%d%d" % (k, q)) for q in range(PASSES)]
+                 for k, x in zip(r_first, R_LOADS)}
+        r_width = dict(zip(r_first, R_LOADS))
+        w_from = [B * sum(W_TILES[:j]) for j in range(len(W_TILES) + 1)]
+        w_sb = [keep.tile([P, ROW_TILES, B * x], BF16, name="w_sb%d" % j) for j, x in enumerate(W_TILES)]
         lt_w = keep.tile([P, GROUPS, 2 * M], U8, name="lt_w", align_bytes=ALIGN)
         step_all = keep.tile([P, N], BF16, name="step_all")
 
-        def load_grad(g, u, lo, hi):
-            nc.sync.dma_start(out=g_raw[g][u][:, :, lo:hi], in_=grad_v[g][:, 2 * u : 2 * u + 2, lo:hi])
+        def load_grad(g, t, lo=0, hi=N):
+            nc.sync.dma_start(out=g_raw[g][t][:, lo:hi], in_=grad_v[g][:, t, lo:hi])
 
         def load_right(k, q):
-            nc.sync.dma_start(out=r_raw[k][q][:], in_=right_v[q][:, :, PAIR * k : PAIR * k + PAIR])
+            nc.sync.dma_start(out=r_raw[k][q][:], in_=right_v[q][:, :, PAIR * k : PAIR * (k + r_width[k])])
 
         def load_pair(k):
-            for q in range(PASSES):
-                load_right(k, q)
+            if k in r_first:
+                for q in range(PASSES):
+                    load_right(k, q)
 
         def load_w(j):
-            for r in range(0, ROW_TILES, 4):
-                nc.sync.dma_start(out=w_sb[j][:, r : r + 4, :], in_=w_v[:, r : r + 4, w_from[j] : w_from[j + 1]])
+            rows = 16 // W_TILES[j] if W_TILES[j] <= 4 else 2
+            for r in range(0, ROW_TILES, rows):
+                nc.sync.dma_start(out=w_sb[j][:, r : r + rows, :], in_=w_v[:, r : r + rows, w_from[j] : w_from[j + 1]])
 
-        if LOADS == 0:
-            load_grad(0, 0, 0, PASS)
-            load_right(0, 0)
-            load_grad(0, 0, PASS, N)
-            load_right(0, 1)
-            load_grad(0, 1, 0, N)
-            load_right(0, 2)
-        if LOADS == 1:
-            load_grad(0, 0, 0, PASS)
-            load_grad(0, 0, PASS, 2 * PASS)
-            load_right(0, 0)
-            load_grad(0, 0, 2 * PASS, N)
-            load_grad(0, 1, 0, PASS)
-            load_right(0, 1)
-            load_grad(0, 1, PASS, N)
-            load_right(0, 2)
-        if LOADS == 2:
-            load_grad(0, 0, 0, PASS)
-            load_grad(0, 0, PASS, N)
-            load_right(0, 0)
-            load_grad(0, 1, 0, N)
-            load_right(0, 1)
-            load_right(0, 2)
-        load_grad(1, 0, 0, N)
-        load_grad(1, 1, 0, N)
+        def load_cols():
+            with nc.allow_non_contiguous_dma(reason="144 scales, turned while they load"):
+                nc.sync.dma_start(out=r_cols[:], in_=right_scale.rearrange("a c -> c a"))
+
+        for x in HEAD_LOADS:
+            if x == "a":
+                load_grad(0, 0, 0, 2 * PASS)
+            elif x == "b":
+                load_grad(0, 0, 2 * PASS, N)
+            elif x == "c":
+                load_cols()
+            elif x in "01234567":
+                load_grad(*divmod(int(x), 4))
+            else:
+                load_right(0, "xyz".index(x))
+        def load_step(j):
+            nc.sync.dma_start(out=step_all[:, PASS * j : PASS * j + PASS], in_=step[PASS * j : PASS * j + PASS].partition_broadcast(P))
+
         load_pair(1)
+        if STEP_SPLIT and not SPREAD_STEP:
+            load_step(0)
         load_pair(2)
-        nc.sync.dma_start(out=step_all[:], in_=step.partition_broadcast(P))
+        if SPREAD_STEP and STEP_ROW == 1:
+            nc.sync.dma_start(out=step_row[0:1, :], in_=step.unsqueeze(0))
+        if not STEP_SPLIT and not SPREAD_STEP:
+            nc.sync.dma_start(out=step_all[:], in_=step.partition_broadcast(P))
         for s in range(4):
             nc.sync.dma_start(out=lt_s[32 * s : 32 * s + 4, :, :].bitcast(I32),
                               in_=lt_scales.rearrange("g (s r) n -> s r g n", s=4)[s].bitcast(I32))
         nc.sync.dma_start(out=lt_w[:], in_=lt_words.rearrange("g p n -> p g n"))
-        load_w(0)
         load_pair(3)
-        load_w(1)
+        if not W_LAST:
+            load_w(0)
+        if STEP_SPLIT and not SPREAD_STEP:
+            load_step(1)
         load_pair(4)
+        if 1 not in W_LATE.values() and len(W_TILES) > 1 and not W_LAST:
+            load_w(1)
         load_pair(5)
-        load_w(2)
-        load_w(3)
+        if STEP_SPLIT and not SPREAD_STEP:
+            load_step(2)
+        for j in range(0 if W_LAST else 2, len(W_TILES)):
+            if j not in W_LATE.values():
+                load_w(j)
 
         r_scale = keep.tile([P, PASSES, BLOCKS], F32, name="r_scale")
         r_scale_ps = []
@@ -161,24 +198,22 @@ def tile_two_sided_preconditioned_step_d4_kernel(
         def leave_scales():
             nc.scalar.copy(out=r_scale[:], in_=r_scale_ps[0][:, :, 0:BLOCKS])
 
-        units = [(g, u, q) for g in range(GROUPS) for u in range(2) for q in range(PASSES)]
-        g_codes = [[keep.tile([P, PASS], U32, name="g_codes%d%d" % (g, q), align_bytes=ALIGN) for q in range(PASSES)]
-                   for g in range(GROUPS)]
-        g_bytes = [[keep.tile([P, PASS], U8, name="g_bytes%d%d" % (g, q), align_bytes=ALIGN) for q in range(PASSES)]
-                   for g in range(GROUPS)]
+        items = [(g, t, q) for g in range(GROUPS) for t in range(4) for q in range(PASSES)]
+        units = [items[x : x + 2] for x in range(0, len(items), 2)]
+        g_codes = [keep.tile([P, 4 * PASSES * P], U32, name="g_codes%d" % g, align_bytes=ALIGN) for g in range(GROUPS)]
+        g_bytes = [keep.tile([P, 4 * PASSES * P], U8, name="g_bytes%d" % g, align_bytes=ALIGN) for g in range(GROUPS)]
         g_wide = {}
         g_ps = {}
         g_turned = {}
 
         def widen_grad(s):
-            g, u, q = units[s]
-            for e in range(2):
+            for e, (g, t, q) in enumerate(units[s]):
                 wide = rot.tile([P, PASS], BF16, name="g_wide", bufs=6)
                 dst = wide[:].rearrange("p (h a f) -> p a h f", h=2, f=2)
                 for c in range(4):
                     k0 = PASS * q + B * c
-                    src = g_raw[g][u][:, e, k0 : k0 + B].bitcast(E4M3).rearrange("p (a h f) -> p a h f", h=2, f=2)
-                    col = (2 * u + e) * BLOCKS + 4 * q + c
+                    src = g_raw[g][t][:, k0 : k0 + B].bitcast(E4M3).rearrange("p (a h f) -> p a h f", h=2, f=2)
+                    col = t * BLOCKS + 4 * q + c
                     nc.vector.tensor_scalar(out=dst[:, 32 * c : 32 * c + 32, :, :], in0=src,
                                             scalar1=g_scale[:, g, col : col + 1], scalar2=None, op0=MULT)
                 g_wide[s, e] = wide
@@ -204,9 +239,9 @@ def tile_two_sided_preconditioned_step_d4_kernel(
             g_turned[s] = x
 
         def quant_grad(s):
-            g, u, q = units[s]
-            m = slice(2 * P * u, 2 * P * u + 2 * P)
-            nc.vector.quantize_mx(out=g_codes[g][q][:, m].bitcast(E4M3X4), scales=g_bytes[g][q][:, m], in_=g_turned[s][:])
+            g, t, q = units[s][0]
+            m = slice(P * (PASSES * t + q), P * (PASSES * t + q + 2))
+            nc.vector.quantize_mx(out=g_codes[g][:, m].bitcast(E4M3X4), scales=g_bytes[g][:, m], in_=g_turned[s][:])
 
         r_planes = {}
         r_wide = {}
@@ -214,8 +249,10 @@ def tile_two_sided_preconditioned_step_d4_kernel(
         r_bytes = {}
 
         def cast_right(k, q):
-            r_planes[k, q] = rot.tile([P, 4, PAIR], BF16, name="r_planes", bufs=6)
-            nc.scalar.copy(out=r_planes[k, q][:].rearrange("p t n -> p (t n)"),
+            planes = rot.tile([P, 4, PAIR * r_width[k]], BF16, name="r_planes", bufs=6)
+            for x in range(r_width[k]):
+                r_planes[k + x, q] = planes[:, :, PAIR * x : PAIR * x + PAIR]
+            nc.scalar.copy(out=planes[:].rearrange("p t n -> p (t n)"),
                            in_=r_raw[k][q][:].rearrange("p t n -> p (t n)").bitcast(E4M3))
 
         def vector_blocks(k, q):
@@ -245,6 +282,8 @@ def tile_two_sided_preconditioned_step_d4_kernel(
             slots = [(k, g, u) for g in range(GROUPS) for k in range(2) for u in range(2)] + slots[8:]
         if CROSS == 2:
             slots = slots[0:3] + slots[4:6] + [slots[3]] + slots[6:]
+        if SECOND[-1] == 1:
+            slots = slots[:-4] + [(PAIRS - 1, g, u) for u in range(2) for g in range(GROUPS)]
         h_codes = [keep.tile([P, N], U32, name="h_codes%d" % g, align_bytes=ALIGN) for g in range(GROUPS)]
         h_bytes = [keep.tile([P, N], U8, name="h_bytes%d" % g, align_bytes=ALIGN) for g in range(GROUPS)]
         h_ps = {}
@@ -253,22 +292,27 @@ def tile_two_sided_preconditioned_step_d4_kernel(
         starts = [sum(SECOND[:j]) for j in range(len(SECOND))]
         fine = [k for k in range(PAIRS) if 2 * k + 1 in starts]
 
+        assert all(FORMS[k] == "D" for k in fine)
+
         def slot_shape(k, u):
             if FORMS[k] == "D":
                 return range(4), slice(B * u, B * u + B)
             return range(2 * u, 2 * u + 2), slice(0, PAIR)
 
-        def first_product(k, g, u):
+        def first_product(k, g, u, part=None):
             row_tiles, n = slot_shape(k, u)
-            ps = ps_h.tile([P, len(row_tiles), PASS // len(row_tiles)], F32, name="bank_h")
+            if part != 1:
+                h_ps[k, g, u] = ps_h.tile([P, len(row_tiles), PASS // len(row_tiles)], F32, name="bank_h")
+            ps = h_ps[k, g, u]
             for e, t in enumerate(row_tiles):
-                m = slice(P * t, P * t + P)
+                if part is not None and t // 2 != part:
+                    continue
                 for q in range(PASSES):
+                    m = slice(P * (PASSES * t + q), P * (PASSES * t + q + 1))
                     nc.tensor.matmul_mx(out=ps[:, e, :],
-                                        lhsT=g_codes[g][q][:, m].bitcast(E4M3X4), lhsT_scale=g_bytes[g][q][:, m],
+                                        lhsT=g_codes[g][:, m].bitcast(E4M3X4), lhsT_scale=g_bytes[g][:, m],
                                         rhs=r_codes[k][:, q, n].bitcast(E4M3X4), rhs_scale=r_bytes[k][:, q, n],
                                         start=(q == 0), stop=(q == PASSES - 1))
-            h_ps[k, g, u] = ps
 
         def step_h(k, g, u):
             row_tiles, n = slot_shape(k, u)
@@ -331,9 +375,9 @@ def tile_two_sided_preconditioned_step_d4_kernel(
 
         def finish_tile():
             ps, b0, nb, r0, rows = waiting.pop(0)
-            j = max(x for x in range(4) if w_from[x] <= B * b0)
+            j = max(x for x in range(len(W_TILES)) if w_from[x] <= B * b0)
             w_part = w_sb[j][:, r0 : r0 + rows, B * b0 - w_from[j] : B * (b0 + nb) - w_from[j]]
-            result = rot.tile([P, rows, B * nb], F32, name="result", bufs=8)
+            result = rot.tile([P, rows, B * nb], F32, name="result", bufs=RES_BUFS)
             x = len(done)
             done.append(x)
             if POOL_FROM <= x < POOL_TO and (x - POOL_FROM) % POOL_EVERY == 0:
@@ -343,6 +387,8 @@ def tile_two_sided_preconditioned_step_d4_kernel(
             else:
                 nc.vector.tensor_tensor(out=result[:], in0=w_part, in1=ps[:], op=SUB)
                 store(result, b0, nb, r0, rows)
+            if x in W_LATE and W_LATE[x] < len(W_TILES):
+                load_w(W_LATE[x])
             if late and late[0][0] + 2 <= x:
                 store(*late.pop(0)[1:])
 
@@ -364,8 +410,13 @@ def tile_two_sided_preconditioned_step_d4_kernel(
                 turn_grad(s - 1)
             if s in WARM_UPS:
                 warm_up(WARM_UPS[s])
-            if 0 <= y <= last:
-                first_product(*slots[y])
+            if 0 <= s - EARLY < 2:
+                first_product(*slots[s - EARLY])
+            if HALVES and s == nu:
+                first_product(*slots[2], 0)
+                first_product(*slots[3], 0)
+            if 2 <= y <= last:
+                first_product(*slots[y], 1 if HALVES and y < 4 else None)
             if s == SPREAD:
                 repeat_scales()
             if s == SPREAD + 1:
@@ -376,25 +427,36 @@ def tile_two_sided_preconditioned_step_d4_kernel(
                 join_h(*joins[s])
             if s > nu // 2 and s <= nu:
                 leave_grad(s - 1)
-            if 0 <= z <= last:
+            for z in range(last + 1):
+                if y != z + (STEP_LAG if z < SWITCH else 1):
+                    continue
                 step_h(*slots[z])
                 k, g, u = slots[z]
                 if FORMS[k] == "J":
                     if u == 1:
-                        joins[s + 1] = (k, g)
-                        quants[s + 2] = slots[z]
+                        if z < SWITCH2:
+                            joins[s + 1] = (k, g)
+                            quants.setdefault(s + 2, []).append(slots[z])
+                        else:
+                            join_h(k, g)
+                            quants.setdefault(s + 1, []).append(slots[z])
                 else:
-                    quants[s + 1] = slots[z]
+                    quants.setdefault(s + 1, []).append(slots[z])
             if ORDER == 1 and len(waiting) > HELD:
                 finish_tile()
-            if s in quants:
-                quant_h(*quants[s])
+            for slot in quants.get(s, []):
+                quant_h(*slot)
             if ORDER == 0 and len(waiting) > HELD:
                 finish_tile()
             for k, q in jobs_at(s, SCALE_AHEAD, SCALES):
                 scale_right(k, q)
-            for k, q in jobs_at(s, CAST_AHEAD, CASTS):
-                cast_right(k, q)
+            for k in r_first:
+                gap = CAST_GAP if r_width[k] > 1 and k > 0 else 1
+                base = CASTS[k] if k < 2 else FIRST_SLOT + SLOTS * k - CAST_AHEAD - 2 * (gap - 1)
+                if s >= base and (s - base) % gap == 0 and (s - base) // gap < PASSES:
+                    cast_right(k, (s - base) // gap)
+            if s in SPREAD_STEP:
+                spread_step(SPREAD_STEP[s])
             if 1 <= s <= nu // 2:
                 leave_grad(s - 1)
             if GQ_LAG <= s < nu + GQ_LAG:
@@ -403,7 +465,7 @@ def tile_two_sided_preconditioned_step_d4_kernel(
                 quant_right(k, q)
             if ready:
                 second_product(*ready.pop(0))
-            if len(ready) > BACKLOG and s % TWO_EVERY == 0:
+            if len(ready) > BACKLOG and s % TWO_EVERY == 0 and y >= TWO_FROM:
                 if len(waiting) > HELD + 1:
                     finish_tile()
                 second_product(*ready.pop(0))

@@ -28,48 +28,19 @@ PAIRS = N // PAIR
 ROW_TILES = M // P
 BANKS = 4
 SLOTS = 4
+UNITS = GROUPS * 4 * PASSES // 2
 
-CAST_AHEAD = 8
-SCALE_AHEAD = 5
-QUANT_AHEAD = 3
-CASTS = [1,8]
-SCALES = [5,11]
-QUANTS = [7,13]
-SPREAD = 2
-VEC = [0, 1, 1, 1, 1, 1, 1, 1]
-WARM_UPS = {}
-BACKLOG = 0
-TWO_EVERY = 2
-LOADS = 1
-FORMS = "DDJJJJ"
-SECOND = [2]*6
-FIRST_SLOT = 13
-STEP_LAG = 2
-GQ_LAG = 3
-CROSS = 0
-POOL_FROM = 24
-POOL_TO = 24
-POOL_EVERY = 2
-HELD = 1
-ORDER = 1
-SPLIT_LAST = 0
-ALIGN = 64
-HEAD_LOADS = "0x1y2z34567"
-EARLY = 12
-HALVES = 0
-COLS_LATE = 0
-R_LOADS = [1,1,1,1,2]
-CAST_GAP = 2
-SPREAD_STEP = {}
-STEP_ROW = 1
-W_LAST = 0
-SWITCH = 99
-SWITCH2 = 16
-RES_BUFS = 10
-TWO_FROM = 16
-STEP_SPLIT = 1
-W_LATE = {}
-W_TILES = [4,8]
+FIRST_SLOT = UNITS + 1
+QUANT_AHEAD = PASSES
+SCALE_AHEAD = QUANT_AHEAD + 1
+CAST_AHEAD = SCALE_AHEAD + 4
+HEAD_CASTS = (1, 8)
+HEAD_SCALES = (5, 11)
+VECTOR_JOBS = range(2, 8)
+DIRECT_PAIRS = 2
+LATE_SLOT = (PAIRS - 2) * SLOTS
+WIDE_PAIR = PAIRS - 2
+W_FIRST = PASS
 
 
 def tile_two_sided_preconditioned_step_d4_kernel(
@@ -89,125 +60,77 @@ def tile_two_sided_preconditioned_step_d4_kernel(
 
         g_scale = keep.tile([P, GROUPS, 4 * BLOCKS], F32, name="g_scale")
         nc.scalar.dma_start(out=g_scale[:], in_=grad_scale.rearrange("(g p t) c -> p g (t c)", p=P, t=4))
-        r_cols = keep.tile([BLOCKS, BLOCKS], F32, name="r_cols")
-        if "c" not in HEAD_LOADS:
-            with nc.allow_non_contiguous_dma(reason="144 scales, turned while they load"):
-                nc.scalar.dma_start(out=r_cols[:], in_=right_scale.rearrange("a c -> c a"))
 
         ident = keep.tile([P, P], F32, name="ident")
         make_identity(nc, ident[:])
-        r_rep = keep.tile([P, BLOCKS, 32], F32, name="r_rep")
-        nc.vector.memset(r_rep[:], 0.0)
-        lt_s = keep.tile([P, GROUPS, M], U8, name="lt_s", align_bytes=ALIGN)
+        lt_s = keep.tile([P, GROUPS, M], U8, name="lt_s", align_bytes=64)
         nc.vector.memset(lt_s[:].rearrange("p g n -> p (g n)").bitcast(I32), 0)
 
-        if SPREAD_STEP:
-            step_row = keep.tile([P, N], BF16, name="step_row")
-            ones = keep.tile([P, P], BF16, name="ones")
-            nc.vector.memset(step_row[:].bitcast(I32), 0)
-            nc.vector.memset(ones[:], 1.0)
-
-        def spread_step(j):
-            ps = ps_h.tile([P, PASS], BF16, name="bank_h")
-            nc.tensor.matmul(out=ps[:], lhsT=ones[:], rhs=step_row[:, PASS * j : PASS * j + PASS], start=True, stop=True)
-            nc.scalar.copy(out=step_all[:, PASS * j : PASS * j + PASS], in_=ps[:])
-
         g_raw = [[keep.tile([P, N], U8, name="g_raw%d%d" % (g, t)) for t in range(4)] for g in range(GROUPS)]
-        r_first = [sum(R_LOADS[:j]) for j in range(len(R_LOADS))]
-        r_raw = {k: [keep.tile([P, 4, PAIR * x], U8, name="r_raw%d%d" % (k, q)) for q in range(PASSES)]
-                 for k, x in zip(r_first, R_LOADS)}
-        r_width = dict(zip(r_first, R_LOADS))
-        w_from = [B * sum(W_TILES[:j]) for j in range(len(W_TILES) + 1)]
-        w_sb = [keep.tile([P, ROW_TILES, B * x], BF16, name="w_sb%d" % j) for j, x in enumerate(W_TILES)]
-        lt_w = keep.tile([P, GROUPS, 2 * M], U8, name="lt_w", align_bytes=ALIGN)
+        r_width = [PAIR] * WIDE_PAIR + [N - PAIR * WIDE_PAIR]
+        r_raw = [[keep.tile([P, 4, width], U8, name="r_raw%d%d" % (k, q)) for q in range(PASSES)]
+                 for k, width in enumerate(r_width)]
+        w_first = keep.tile([P, ROW_TILES, W_FIRST], BF16, name="w_first")
+        w_rest = keep.tile([P, ROW_TILES, N - W_FIRST], BF16, name="w_rest")
+        lt_w = keep.tile([P, GROUPS, 2 * M], U8, name="lt_w", align_bytes=64)
         step_all = keep.tile([P, N], BF16, name="step_all")
+        r_scale = keep.tile([P, PASSES, BLOCKS], F32, name="r_scale")
 
-        def load_grad(g, t, lo=0, hi=N):
+        def load_grad(g, t, lo, hi):
             nc.sync.dma_start(out=g_raw[g][t][:, lo:hi], in_=grad_v[g][:, t, lo:hi])
 
         def load_right(k, q):
-            nc.sync.dma_start(out=r_raw[k][q][:], in_=right_v[q][:, :, PAIR * k : PAIR * (k + r_width[k])])
+            nc.sync.dma_start(out=r_raw[k][q][:], in_=right_v[q][:, :, PAIR * k : PAIR * k + r_width[k]])
 
-        def load_pair(k):
-            if k in r_first:
-                for q in range(PASSES):
-                    load_right(k, q)
+        def load_passes(k):
+            for q in range(PASSES):
+                load_right(k, q)
 
-        def load_w(j):
-            rows = 16 // W_TILES[j] if W_TILES[j] <= 4 else 2
-            for r in range(0, ROW_TILES, rows):
-                nc.sync.dma_start(out=w_sb[j][:, r : r + rows, :], in_=w_v[:, r : r + rows, w_from[j] : w_from[j + 1]])
-
-        def load_cols():
-            with nc.allow_non_contiguous_dma(reason="144 scales, turned while they load"):
-                nc.sync.dma_start(out=r_cols[:], in_=right_scale.rearrange("a c -> c a"))
-
-        for x in HEAD_LOADS:
-            if x == "a":
-                load_grad(0, 0, 0, 2 * PASS)
-            elif x == "b":
-                load_grad(0, 0, 2 * PASS, N)
-            elif x == "c":
-                load_cols()
-            elif x in "01234567":
-                load_grad(*divmod(int(x), 4))
-            else:
-                load_right(0, "xyz".index(x))
         def load_step(j):
-            nc.sync.dma_start(out=step_all[:, PASS * j : PASS * j + PASS], in_=step[PASS * j : PASS * j + PASS].partition_broadcast(P))
+            nc.sync.dma_start(out=step_all[:, PASS * j : PASS * j + PASS],
+                              in_=step[PASS * j : PASS * j + PASS].partition_broadcast(P))
 
-        load_pair(1)
-        if STEP_SPLIT and not SPREAD_STEP:
-            load_step(0)
-        load_pair(2)
-        if SPREAD_STEP and STEP_ROW == 1:
-            nc.sync.dma_start(out=step_row[0:1, :], in_=step.unsqueeze(0))
-        if not STEP_SPLIT and not SPREAD_STEP:
-            nc.sync.dma_start(out=step_all[:], in_=step.partition_broadcast(P))
+        def load_w(tile, lo, hi):
+            rows = 4 * PASS // (hi - lo)
+            for r in range(0, ROW_TILES, rows):
+                nc.sync.dma_start(out=tile[:, r : r + rows, :], in_=w_v[:, r : r + rows, lo:hi])
+
+        load_grad(0, 0, 0, 2 * PASS)
+        load_right(0, 0)
+        load_grad(0, 0, 2 * PASS, N)
+        load_grad(0, 1, 0, N)
+        load_right(0, 1)
+        load_grad(0, 2, 0, N)
+        for s in range(4):
+            nc.sync.dma_start(out=r_scale[32 * s : 32 * s + 32, :, :],
+                              in_=right_scale.rearrange("(q s) c -> s q c", s=4)[s].partition_broadcast(32))
+        load_right(0, 2)
+        load_grad(0, 3, 0, N)
+        for t in range(4):
+            load_grad(1, t, 0, N)
+        load_passes(1)
+        load_step(0)
+        load_passes(2)
         for s in range(4):
             nc.sync.dma_start(out=lt_s[32 * s : 32 * s + 4, :, :].bitcast(I32),
                               in_=lt_scales.rearrange("g (s r) n -> s r g n", s=4)[s].bitcast(I32))
         nc.sync.dma_start(out=lt_w[:], in_=lt_words.rearrange("g p n -> p g n"))
-        load_pair(3)
-        if not W_LAST:
-            load_w(0)
-        if STEP_SPLIT and not SPREAD_STEP:
-            load_step(1)
-        load_pair(4)
-        if 1 not in W_LATE.values() and len(W_TILES) > 1 and not W_LAST:
-            load_w(1)
-        load_pair(5)
-        if STEP_SPLIT and not SPREAD_STEP:
-            load_step(2)
-        for j in range(0 if W_LAST else 2, len(W_TILES)):
-            if j not in W_LATE.values():
-                load_w(j)
+        load_passes(3)
+        load_w(w_first, 0, W_FIRST)
+        load_step(1)
+        load_passes(WIDE_PAIR)
+        load_w(w_rest, W_FIRST, N)
+        load_step(2)
 
-        r_scale = keep.tile([P, PASSES, BLOCKS], F32, name="r_scale")
-        r_scale_ps = []
-
-        def repeat_scales():
-            nc.scalar.copy(out=r_rep[0:BLOCKS, :, :], in_=r_cols[:].unsqueeze(2).to_broadcast([BLOCKS, BLOCKS, 32]))
-
-        def turn_scales():
-            ps = ps_h.tile([P, PASSES, P], F32, name="bank_h")
-            for q in range(PASSES):
-                nc.tensor.transpose(ps[:, q, :], r_rep[:, 4 * q : 4 * q + 4, :].rearrange("p s r -> p (s r)"), ident[:])
-            r_scale_ps.append(ps)
-
-        def leave_scales():
-            nc.scalar.copy(out=r_scale[:], in_=r_scale_ps[0][:, :, 0:BLOCKS])
-
-        items = [(g, t, q) for g in range(GROUPS) for t in range(4) for q in range(PASSES)]
-        units = [items[x : x + 2] for x in range(0, len(items), 2)]
-        g_codes = [keep.tile([P, 4 * PASSES * P], U32, name="g_codes%d" % g, align_bytes=ALIGN) for g in range(GROUPS)]
-        g_bytes = [keep.tile([P, 4 * PASSES * P], U8, name="g_bytes%d" % g, align_bytes=ALIGN) for g in range(GROUPS)]
+        pieces = [(g, t, q) for g in range(GROUPS) for t in range(4) for q in range(PASSES)]
+        g_codes = [keep.tile([P, 4 * PASSES * P], U32, name="g_codes%d" % g, align_bytes=64) for g in range(GROUPS)]
+        g_bytes = [keep.tile([P, 4 * PASSES * P], U8, name="g_bytes%d" % g, align_bytes=64) for g in range(GROUPS)]
         g_wide = {}
         g_ps = {}
         g_turned = {}
 
         def widen_grad(s):
-            for e, (g, t, q) in enumerate(units[s]):
+            for e, (g, t, q) in enumerate(pieces[2 * s : 2 * s + 2]):
                 wide = rot.tile([P, PASS], BF16, name="g_wide", bufs=6)
                 dst = wide[:].rearrange("p (h a f) -> p a h f", h=2, f=2)
                 for c in range(4):
@@ -226,20 +149,14 @@ def tile_two_sided_preconditioned_step_d4_kernel(
                     nc.tensor.transpose(ps[:, e, h, :], words[:, P * h : P * h + P], ident[:])
             g_ps[s] = ps
 
-        def warm_up(count):
-            ps = ps_h.tile([P, PASS], F32, name="bank_h")
-            planes = r_planes[0, 2][:].rearrange("p t n -> p (t n)")
-            for x in range(count):
-                nc.tensor.matmul(out=ps[:], lhsT=planes[:, 0:P], rhs=planes[:, 0:PASS], start=True, stop=True)
-
         def leave_grad(s):
-            x = rot.tile([P, 2 * PASS], BF16, name="g_turned", align_bytes=ALIGN, bufs=4)
+            x = rot.tile([P, 2 * PASS], BF16, name="g_turned", align_bytes=64, bufs=4)
             nc.scalar.copy(out=x[:].bitcast(F32).rearrange("p (e m h) -> p e m h", e=2, h=2),
                            in_=g_ps[s][:].rearrange("p e h m -> p e m h"))
             g_turned[s] = x
 
         def quant_grad(s):
-            g, t, q = units[s][0]
+            g, t, q = pieces[2 * s]
             m = slice(P * (PASSES * t + q), P * (PASSES * t + q + 2))
             nc.vector.quantize_mx(out=g_codes[g][:, m].bitcast(E4M3X4), scales=g_bytes[g][:, m], in_=g_turned[s][:])
 
@@ -249,229 +166,179 @@ def tile_two_sided_preconditioned_step_d4_kernel(
         r_bytes = {}
 
         def cast_right(k, q):
-            planes = rot.tile([P, 4, PAIR * r_width[k]], BF16, name="r_planes", bufs=6)
-            for x in range(r_width[k]):
+            planes = rot.tile([P, 4, r_width[k]], BF16, name="r_planes", bufs=6)
+            for x in range(r_width[k] // PAIR):
                 r_planes[k + x, q] = planes[:, :, PAIR * x : PAIR * x + PAIR]
             nc.scalar.copy(out=planes[:].rearrange("p t n -> p (t n)"),
                            in_=r_raw[k][q][:].rearrange("p t n -> p (t n)").bitcast(E4M3))
 
-        def vector_blocks(k, q):
-            j = PASSES * k + q
-            return VEC[j] if j < len(VEC) else 0
-
         def scale_right(k, q):
-            on_vector = vector_blocks(k, q)
-            r_wide[k, q] = rot.tile([P, 4 * PAIR], BF16, name="r_wide", align_bytes=ALIGN, bufs=6)
+            r_wide[k, q] = rot.tile([P, 4 * PAIR], BF16, name="r_wide", align_bytes=64, bufs=6)
             for b in range(2):
                 dst = r_wide[k, q][:, 4 * B * b : 4 * B * b + 4 * B].rearrange("p (c i t) -> p c t i", t=4, i=4)
                 src = r_planes[k, q][:, :, B * b : B * b + B].rearrange("p t (c i) -> p c t i", i=4)
                 scale = r_scale[:, q, 2 * k + b : 2 * k + b + 1]
-                if b < on_vector:
+                if b == 0 and PASSES * k + q in VECTOR_JOBS:
                     nc.vector.tensor_scalar(out=dst, in0=src, scalar1=scale, scalar2=None, op0=MULT)
                 else:
                     nc.scalar.activation(out=dst, in_=src, func=COPY, scale=scale)
 
         def quant_right(k, q):
             if q == 0:
-                r_codes[k] = keep.tile([P, PASSES, PAIR], U32, name="r_codes%d" % k, align_bytes=ALIGN)
-                r_bytes[k] = keep.tile([P, PASSES, PAIR], U8, name="r_bytes%d" % k, align_bytes=ALIGN)
+                r_codes[k] = keep.tile([P, PASSES, PAIR], U32, name="r_codes%d" % k, align_bytes=64)
+                r_bytes[k] = keep.tile([P, PASSES, PAIR], U8, name="r_bytes%d" % k, align_bytes=64)
             nc.vector.quantize_mx(out=r_codes[k][:, q, :].bitcast(E4M3X4), scales=r_bytes[k][:, q, :], in_=r_wide[k, q][:])
 
+        def warm_up(count):
+            ps = ps_h.tile([P, PASS], F32, name="bank_h")
+            planes = r_planes[0, PASSES - 1][:].rearrange("p t n -> p (t n)")
+            for x in range(count):
+                nc.tensor.matmul(out=ps[:], lhsT=planes[:, 0:P], rhs=planes[:, 0:PASS], start=True, stop=True)
+
         slots = [(k, g, u) for k in range(PAIRS) for g in range(GROUPS) for u in range(2)]
-        if CROSS == 1:
-            slots = [(k, g, u) for g in range(GROUPS) for k in range(2) for u in range(2)] + slots[8:]
-        if CROSS == 2:
-            slots = slots[0:3] + slots[4:6] + [slots[3]] + slots[6:]
-        if SECOND[-1] == 1:
-            slots = slots[:-4] + [(PAIRS - 1, g, u) for u in range(2) for g in range(GROUPS)]
-        h_codes = [keep.tile([P, N], U32, name="h_codes%d" % g, align_bytes=ALIGN) for g in range(GROUPS)]
-        h_bytes = [keep.tile([P, N], U8, name="h_bytes%d" % g, align_bytes=ALIGN) for g in range(GROUPS)]
+        h_codes = [keep.tile([P, N], U32, name="h_codes%d" % g, align_bytes=64) for g in range(GROUPS)]
+        h_bytes = [keep.tile([P, N], U8, name="h_bytes%d" % g, align_bytes=64) for g in range(GROUPS)]
         h_ps = {}
         h_parts = {}
         h_joined = {}
-        starts = [sum(SECOND[:j]) for j in range(len(SECOND))]
-        fine = [k for k in range(PAIRS) if 2 * k + 1 in starts]
-
-        assert all(FORMS[k] == "D" for k in fine)
 
         def slot_shape(k, u):
-            if FORMS[k] == "D":
+            if k < DIRECT_PAIRS:
                 return range(4), slice(B * u, B * u + B)
             return range(2 * u, 2 * u + 2), slice(0, PAIR)
 
-        def first_product(k, g, u, part=None):
+        def first_product(y, lo, hi):
+            k, g, u = slots[y]
             row_tiles, n = slot_shape(k, u)
-            if part != 1:
-                h_ps[k, g, u] = ps_h.tile([P, len(row_tiles), PASS // len(row_tiles)], F32, name="bank_h")
-            ps = h_ps[k, g, u]
-            for e, t in enumerate(row_tiles):
-                if part is not None and t // 2 != part:
-                    continue
+            if lo == 0:
+                h_ps[y] = ps_h.tile([P, len(row_tiles), PASS // len(row_tiles)], F32, name="bank_h")
+            for e in range(lo, hi):
                 for q in range(PASSES):
-                    m = slice(P * (PASSES * t + q), P * (PASSES * t + q + 1))
-                    nc.tensor.matmul_mx(out=ps[:, e, :],
+                    m = slice(P * (PASSES * row_tiles[e] + q), P * (PASSES * row_tiles[e] + q + 1))
+                    nc.tensor.matmul_mx(out=h_ps[y][:, e, :],
                                         lhsT=g_codes[g][:, m].bitcast(E4M3X4), lhsT_scale=g_bytes[g][:, m],
                                         rhs=r_codes[k][:, q, n].bitcast(E4M3X4), rhs_scale=r_bytes[k][:, q, n],
                                         start=(q == 0), stop=(q == PASSES - 1))
 
-        def step_h(k, g, u):
+        def step_h(y):
+            k, g, u = slots[y]
             row_tiles, n = slot_shape(k, u)
             if u == 0:
-                h_parts[k, g] = rot.tile([P, 2, PASS], BF16, name="h_parts", align_bytes=ALIGN, bufs=4)
+                h_parts[k, g] = rot.tile([P, 2, PASS], BF16, name="h_parts", align_bytes=64, bufs=4)
             steps = step_all[:, PAIR * k + n.start : PAIR * k + n.stop].rearrange("p (c i) -> p c i", i=2)
             nc.vector.tensor_tensor(out=h_parts[k, g][:, u, :].rearrange("p (c i e) -> p c e i", i=2, e=len(row_tiles)),
-                                    in0=h_ps[k, g, u][:].rearrange("p e (c i) -> p c e i", i=2),
+                                    in0=h_ps[y][:].rearrange("p e (c i) -> p c e i", i=2),
                                     in1=steps.unsqueeze(2).to_broadcast([P, (n.stop - n.start) // 2, len(row_tiles), 2]),
                                     op=MULT)
 
         def join_h(k, g):
-            x = rot.tile([P, 4 * PAIR], BF16, name="h_joined", align_bytes=ALIGN)
+            x = rot.tile([P, 4 * PAIR], BF16, name="h_joined", align_bytes=64)
             nc.scalar.copy(out=x[:].bitcast(F32).rearrange("p (n u) -> p n u", u=2),
                            in_=h_parts[k, g][:].bitcast(F32).rearrange("p u n -> p n u"))
             h_joined[k, g] = x
 
-        def quant_h(k, g, u):
-            if k in fine and g == 1:
-                n = slice(PAIR * k + B * u, PAIR * k + B * u + B)
-                src = h_parts[k, g][:, u, :]
-            elif u == 1:
-                n = slice(PAIR * k, PAIR * k + PAIR)
-                src = h_parts[k, g][:].rearrange("p u n -> p (u n)") if FORMS[k] == "D" else h_joined[k, g][:]
-            else:
-                return
+        def quant_h(k, g):
+            n = slice(PAIR * k, PAIR * k + PAIR)
+            src = h_parts[k, g][:].rearrange("p u n -> p (u n)") if k < DIRECT_PAIRS else h_joined[k, g][:]
             nc.vector.quantize_mx(out=h_codes[g][:, n].bitcast(E4M3X4), scales=h_bytes[g][:, n], in_=src)
-            if g == 1:
-                for j, b0 in enumerate(starts):
-                    if B * (b0 + SECOND[j]) == n.stop:
-                        rows = 4 // SECOND[j]
-                        whole = ROW_TILES - (SPLIT_LAST * rows if n.stop == N else 0)
-                        ready.extend((b0, SECOND[j], r0, rows) for r0 in range(0, whole, rows))
-                        ready.extend((b0, SECOND[j], r0, rows // 2) for r0 in range(whole, ROW_TILES, rows // 2 or 1))
+            if g == GROUPS - 1:
+                ready.extend((k, r0) for r0 in range(0, ROW_TILES, 2))
 
         ready = []
         waiting = []
-        late = []
-        done = []
 
-        def second_product(b0, nb, r0, rows):
+        def second_product(k, r0):
             if len(waiting) == BANKS:
                 finish_tile()
-            ps = ps_o.tile([P, rows, B * nb], F32, name="bank_o")
-            wide = PASS if nb == 4 else B
-            for x in range(rows):
+            ps = ps_o.tile([P, 2, PAIR], F32, name="bank_o")
+            passes = [(x, g, b) for x in range(2) for g in range(GROUPS) for b in range(2)]
+            for j, (x, g, b) in enumerate(passes):
                 r = r0 + x
-                for c in range(0, B * nb, wide):
-                    n = slice(B * b0 + c, B * b0 + c + wide)
-                    for g in range(GROUPS):
-                        nc.tensor.matmul_mx(out=ps[:, x, c : c + wide],
-                                            lhsT=lt_w[:, g, 2 * P * r : 2 * P * r + 2 * P].bitcast(E2M1X4),
-                                            lhsT_scale=lt_s[:, g, P * r : P * r + P],
-                                            rhs=h_codes[g][:, n].bitcast(E4M3X4), rhs_scale=h_bytes[g][:, n],
-                                            start=(g == 0), stop=(g == GROUPS - 1))
-            waiting.append((ps, b0, nb, r0, rows))
-
-        def store(result, b0, nb, r0, rows):
-            nc.sync.dma_start(out=out_v[:, r0 : r0 + rows, B * b0 : B * (b0 + nb)], in_=result[:])
+                n = slice(PAIR * k + B * b, PAIR * k + B * b + B)
+                nc.tensor.matmul_mx(out=ps[:, x, B * b : B * b + B],
+                                    lhsT=lt_w[:, g, 2 * P * r : 2 * P * r + 2 * P].bitcast(E2M1X4),
+                                    lhsT_scale=lt_s[:, g, P * r : P * r + P],
+                                    rhs=h_codes[g][:, n].bitcast(E4M3X4), rhs_scale=h_bytes[g][:, n],
+                                    start=(j == 0), stop=(j == len(passes) - 1))
+            waiting.append((ps, k, r0))
 
         def finish_tile():
-            ps, b0, nb, r0, rows = waiting.pop(0)
-            j = max(x for x in range(len(W_TILES)) if w_from[x] <= B * b0)
-            w_part = w_sb[j][:, r0 : r0 + rows, B * b0 - w_from[j] : B * (b0 + nb) - w_from[j]]
-            result = rot.tile([P, rows, B * nb], F32, name="result", bufs=RES_BUFS)
-            x = len(done)
-            done.append(x)
-            if POOL_FROM <= x < POOL_TO and (x - POOL_FROM) % POOL_EVERY == 0:
-                nc.scalar.copy(out=result[:], in_=ps[:])
-                nc.gpsimd.tensor_tensor(out=result[:], in0=w_part, in1=result[:], op=SUB)
-                late.append((x, result, b0, nb, r0, rows))
-            else:
-                nc.vector.tensor_tensor(out=result[:], in0=w_part, in1=ps[:], op=SUB)
-                store(result, b0, nb, r0, rows)
-            if x in W_LATE and W_LATE[x] < len(W_TILES):
-                load_w(W_LATE[x])
-            if late and late[0][0] + 2 <= x:
-                store(*late.pop(0)[1:])
+            ps, k, r0 = waiting.pop(0)
+            tile, n0 = (w_first, PAIR * k) if PAIR * k < W_FIRST else (w_rest, PAIR * k - W_FIRST)
+            result = rot.tile([P, 2, PAIR], F32, name="result", bufs=10)
+            nc.vector.tensor_tensor(out=result[:], in0=tile[:, r0 : r0 + 2, n0 : n0 + PAIR], in1=ps[:], op=SUB)
+            nc.sync.dma_start(out=out_v[:, r0 : r0 + 2, PAIR * k : PAIR * k + PAIR], in_=result[:])
 
-        def jobs_at(s, ahead, early):
-            jobs = [(k, s - early[k]) for k in range(2) if 0 <= s - early[k] < PASSES]
+        def jobs_at(s, head_steps, ahead):
+            jobs = [(k, s - first) for k, first in enumerate(head_steps) if 0 <= s - first < PASSES]
             k, q = divmod(s - FIRST_SLOT + ahead, SLOTS)
-            return jobs + ([(k, q)] if 2 <= k < PAIRS and q < PASSES else [])
+            return jobs + ([(k, q)] if len(head_steps) <= k < PAIRS and q < PASSES else [])
 
-        nu = len(units)
+        def casts_at(s):
+            jobs = [(k, q) for k, q in jobs_at(s, HEAD_CASTS, CAST_AHEAD) if k < WIDE_PAIR]
+            q, odd = divmod(s - (FIRST_SLOT + SLOTS * WIDE_PAIR - CAST_AHEAD - 2), 2)
+            return jobs + ([(WIDE_PAIR, q)] if 0 <= q < PASSES and not odd else [])
+
+        halves = [(0, 0), (0, 2), (1, 0), (1, 2), (2, 0), (3, 0)]
         last = len(slots) - 1
         joins = {}
         quants = {}
-        for s in range(FIRST_SLOT + last + STEP_LAG + 3):
+        for s in range(FIRST_SLOT + last + 5):
             y = s - FIRST_SLOT
-            z = y - STEP_LAG
-            if s < nu:
+            if s < UNITS:
                 widen_grad(s)
-            if 1 <= s <= nu:
+            if 1 <= s <= UNITS:
                 turn_grad(s - 1)
-            if s in WARM_UPS:
-                warm_up(WARM_UPS[s])
-            if 0 <= s - EARLY < 2:
-                first_product(*slots[s - EARLY])
-            if HALVES and s == nu:
-                first_product(*slots[2], 0)
-                first_product(*slots[3], 0)
-            if 2 <= y <= last:
-                first_product(*slots[y], 1 if HALVES and y < 4 else None)
-            if s == SPREAD:
-                repeat_scales()
-            if s == SPREAD + 1:
-                turn_scales()
-            if s == SPREAD + 2:
-                leave_scales()
+            if s == UNITS - 3:
+                warm_up(2)
+            if s == UNITS - 2:
+                warm_up(1)
+            if s >= UNITS - 1:
+                for z, lo in halves[: 1 if s < UNITS else 2]:
+                    first_product(z, lo, lo + 2)
+                halves = halves[1 if s < UNITS else 2 :]
+            if y == 2:
+                first_product(2, 2, 4)
+                first_product(3, 2, 4)
+            if SLOTS <= y <= last:
+                first_product(y, 0, 4 if slots[y][0] < DIRECT_PAIRS else 2)
             if s in joins:
                 join_h(*joins[s])
-            if s > nu // 2 and s <= nu:
+            if UNITS // 2 < s <= UNITS:
                 leave_grad(s - 1)
-            for z in range(last + 1):
-                if y != z + (STEP_LAG if z < SWITCH else 1):
-                    continue
-                step_h(*slots[z])
+            z = y - 1 if y <= SLOTS else y - 2
+            if 0 <= z <= last and y != SLOTS + 1:
+                step_h(z)
                 k, g, u = slots[z]
-                if FORMS[k] == "J":
-                    if u == 1:
-                        if z < SWITCH2:
-                            joins[s + 1] = (k, g)
-                            quants.setdefault(s + 2, []).append(slots[z])
-                        else:
-                            join_h(k, g)
-                            quants.setdefault(s + 1, []).append(slots[z])
-                else:
-                    quants.setdefault(s + 1, []).append(slots[z])
-            if ORDER == 1 and len(waiting) > HELD:
+                if u == 1 and k < DIRECT_PAIRS:
+                    quants[s + 1] = (k, g)
+                elif u == 1 and z < LATE_SLOT:
+                    joins[s + 1] = (k, g)
+                    quants[s + 2] = (k, g)
+                elif u == 1:
+                    join_h(k, g)
+                    quants[s + 1] = (k, g)
+            if len(waiting) > 1:
                 finish_tile()
-            for slot in quants.get(s, []):
-                quant_h(*slot)
-            if ORDER == 0 and len(waiting) > HELD:
-                finish_tile()
-            for k, q in jobs_at(s, SCALE_AHEAD, SCALES):
+            if s in quants:
+                quant_h(*quants[s])
+            for k, q in jobs_at(s, HEAD_SCALES, SCALE_AHEAD):
                 scale_right(k, q)
-            for k in r_first:
-                gap = CAST_GAP if r_width[k] > 1 and k > 0 else 1
-                base = CASTS[k] if k < 2 else FIRST_SLOT + SLOTS * k - CAST_AHEAD - 2 * (gap - 1)
-                if s >= base and (s - base) % gap == 0 and (s - base) // gap < PASSES:
-                    cast_right(k, (s - base) // gap)
-            if s in SPREAD_STEP:
-                spread_step(SPREAD_STEP[s])
-            if 1 <= s <= nu // 2:
+            for k, q in casts_at(s):
+                cast_right(k, q)
+            if 1 <= s <= UNITS // 2:
                 leave_grad(s - 1)
-            if GQ_LAG <= s < nu + GQ_LAG:
-                quant_grad(s - GQ_LAG)
-            for k, q in jobs_at(s, QUANT_AHEAD, QUANTS):
+            if 3 <= s < UNITS + 3:
+                quant_grad(s - 3)
+            for k, q in jobs_at(s, [first + 2 for first in HEAD_SCALES], QUANT_AHEAD):
                 quant_right(k, q)
             if ready:
                 second_product(*ready.pop(0))
-            if len(ready) > BACKLOG and s % TWO_EVERY == 0 and y >= TWO_FROM:
-                if len(waiting) > HELD + 1:
+            if ready and y >= LATE_SLOT and y % 2 == 1:
+                if len(waiting) > 2:
                     finish_tile()
                 second_product(*ready.pop(0))
-        for tile in list(ready):
-            second_product(*tile)
+        for k, r0 in ready:
+            second_product(k, r0)
         for x in range(len(waiting)):
             finish_tile()
-        for x in late:
-            store(*x[1:])

@@ -15,6 +15,7 @@ E4M3 = mybir.dt.float8_e4m3fn
 E4M3X4 = mybir.dt.float8_e4m3fn_x4
 E2M1X4 = mybir.dt.float4_e2m1fn_x4
 MULT = mybir.AluOpType.mult
+ADD = mybir.AluOpType.add
 SUB = mybir.AluOpType.subtract
 COPY = mybir.ActivationFunctionType.Copy
 
@@ -33,13 +34,14 @@ UNITS = GROUPS * 4 * PASSES // 2
 FIRST_SLOT = UNITS + 1
 QUANT_AHEAD = PASSES
 SCALE_AHEAD = QUANT_AHEAD + 1
-CAST_AHEAD = SCALE_AHEAD + 4
+CAST_AHEAD = SCALE_AHEAD + 3
 HEAD_CASTS = (1, 8)
 HEAD_SCALES = (5, 11)
-VECTOR_JOBS = range(2, 8)
-DIRECT_PAIRS = 2
-LATE_SLOT = (PAIRS - 2) * SLOTS
-WIDE_PAIR = PAIRS - 2
+VECTOR_JOBS = range(2, 7)
+POOL_JOBS = range(10, 15)
+DIRECT_PAIRS = 1
+QUICK_JOIN = 3 * SLOTS
+TWO_TILES = 4 * SLOTS
 W_FIRST = PASS
 
 
@@ -67,9 +69,7 @@ def tile_two_sided_preconditioned_step_d4_kernel(
         nc.vector.memset(lt_s[:].rearrange("p g n -> p (g n)").bitcast(I32), 0)
 
         g_raw = [[keep.tile([P, N], U8, name="g_raw%d%d" % (g, t)) for t in range(4)] for g in range(GROUPS)]
-        r_width = [PAIR] * WIDE_PAIR + [N - PAIR * WIDE_PAIR]
-        r_raw = [[keep.tile([P, 4, width], U8, name="r_raw%d%d" % (k, q)) for q in range(PASSES)]
-                 for k, width in enumerate(r_width)]
+        r_raw = [[keep.tile([P, 4, PAIR], U8, name="r_raw%d%d" % (k, q)) for q in range(PASSES)] for k in range(PAIRS)]
         w_first = keep.tile([P, ROW_TILES, W_FIRST], BF16, name="w_first")
         w_rest = keep.tile([P, ROW_TILES, N - W_FIRST], BF16, name="w_rest")
         lt_w = keep.tile([P, GROUPS, 2 * M], U8, name="lt_w", align_bytes=64)
@@ -80,7 +80,7 @@ def tile_two_sided_preconditioned_step_d4_kernel(
             nc.sync.dma_start(out=g_raw[g][t][:, lo:hi], in_=grad_v[g][:, t, lo:hi])
 
         def load_right(k, q):
-            nc.sync.dma_start(out=r_raw[k][q][:], in_=right_v[q][:, :, PAIR * k : PAIR * k + r_width[k]])
+            nc.sync.dma_start(out=r_raw[k][q][:], in_=right_v[q][:, :, PAIR * k : PAIR * k + PAIR])
 
         def load_passes(k):
             for q in range(PASSES):
@@ -118,13 +118,15 @@ def tile_two_sided_preconditioned_step_d4_kernel(
         load_passes(3)
         load_w(w_first, 0, W_FIRST)
         load_step(1)
-        load_passes(WIDE_PAIR)
+        load_passes(4)
         load_w(w_rest, W_FIRST, N)
+        load_passes(5)
         load_step(2)
 
         pieces = [(g, t, q) for g in range(GROUPS) for t in range(4) for q in range(PASSES)]
         g_codes = [keep.tile([P, 4 * PASSES * P], U32, name="g_codes%d" % g, align_bytes=64) for g in range(GROUPS)]
-        g_bytes = [keep.tile([P, 4 * PASSES * P], U8, name="g_bytes%d" % g, align_bytes=64) for g in range(GROUPS)]
+        g_bytes = [keep.tile([P, 4 * PASSES * P + 256], U8, name="g_bytes%d" % g, align_bytes=64)[:, 64 : 64 + 4 * PASSES * P]
+                   for g in range(GROUPS)]
         g_wide = {}
         g_ps = {}
         g_turned = {}
@@ -162,19 +164,18 @@ def tile_two_sided_preconditioned_step_d4_kernel(
 
         r_planes = {}
         r_wide = {}
+        r_pool = {}
         r_codes = {}
         r_bytes = {}
 
         def cast_right(k, q):
-            planes = rot.tile([P, 4, r_width[k]], BF16, name="r_planes", bufs=6)
-            for x in range(r_width[k] // PAIR):
-                r_planes[k + x, q] = planes[:, :, PAIR * x : PAIR * x + PAIR]
-            nc.scalar.copy(out=planes[:].rearrange("p t n -> p (t n)"),
+            r_planes[k, q] = rot.tile([P, 4, PAIR], BF16, name="r_planes", bufs=6)
+            nc.scalar.copy(out=r_planes[k, q][:].rearrange("p t n -> p (t n)"),
                            in_=r_raw[k][q][:].rearrange("p t n -> p (t n)").bitcast(E4M3))
 
         def scale_right(k, q):
             r_wide[k, q] = rot.tile([P, 4 * PAIR], BF16, name="r_wide", align_bytes=64, bufs=6)
-            for b in range(2):
+            for b in range(1 if PASSES * k + q in POOL_JOBS else 2):
                 dst = r_wide[k, q][:, 4 * B * b : 4 * B * b + 4 * B].rearrange("p (c i t) -> p c t i", t=4, i=4)
                 src = r_planes[k, q][:, :, B * b : B * b + B].rearrange("p t (c i) -> p c t i", i=4)
                 scale = r_scale[:, q, 2 * k + b : 2 * k + b + 1]
@@ -183,11 +184,24 @@ def tile_two_sided_preconditioned_step_d4_kernel(
                 else:
                     nc.scalar.activation(out=dst, in_=src, func=COPY, scale=scale)
 
+        def scale_on_pool(k, q):
+            r_pool[k, q] = rot.tile([P, 4 * B], BF16, name="r_pool", align_bytes=64, bufs=1)
+            nc.gpsimd.tensor_scalar(out=r_pool[k, q][:].rearrange("p (n t) -> p n t", t=4),
+                                    in0=r_planes[k, q][:, :, B:PAIR].rearrange("p t n -> p n t"),
+                                    scalar1=r_scale[:, q, 2 * k + 1 : 2 * k + 2], scalar2=0.0, op0=MULT, op1=ADD)
+
         def quant_right(k, q):
             if q == 0:
                 r_codes[k] = keep.tile([P, PASSES, PAIR], U32, name="r_codes%d" % k, align_bytes=64)
                 r_bytes[k] = keep.tile([P, PASSES, PAIR], U8, name="r_bytes%d" % k, align_bytes=64)
-            nc.vector.quantize_mx(out=r_codes[k][:, q, :].bitcast(E4M3X4), scales=r_bytes[k][:, q, :], in_=r_wide[k, q][:])
+            job = PASSES * k + q
+            parts = [(0, PAIR, r_wide[k, q][:])]
+            if job in POOL_JOBS:
+                parts = [(0, B, r_wide[k, q][:, 0 : 4 * B]), (B, PAIR, r_pool[k, q][:])]
+            for lo, hi, src in parts:
+                nc.vector.quantize_mx(out=r_codes[k][:, q, lo:hi].bitcast(E4M3X4), scales=r_bytes[k][:, q, lo:hi], in_=src)
+            if job + 1 in POOL_JOBS:
+                scale_on_pool(*divmod(job + 1, PASSES))
 
         def warm_up(count):
             ps = ps_h.tile([P, PASS], F32, name="bank_h")
@@ -274,11 +288,6 @@ def tile_two_sided_preconditioned_step_d4_kernel(
             k, q = divmod(s - FIRST_SLOT + ahead, SLOTS)
             return jobs + ([(k, q)] if len(head_steps) <= k < PAIRS and q < PASSES else [])
 
-        def casts_at(s):
-            jobs = [(k, q) for k, q in jobs_at(s, HEAD_CASTS, CAST_AHEAD) if k < WIDE_PAIR]
-            q, odd = divmod(s - (FIRST_SLOT + SLOTS * WIDE_PAIR - CAST_AHEAD - 2), 2)
-            return jobs + ([(WIDE_PAIR, q)] if 0 <= q < PASSES and not odd else [])
-
         halves = [(0, 0), (0, 2), (1, 0), (1, 2), (2, 0), (3, 0)]
         last = len(slots) - 1
         joins = {}
@@ -312,7 +321,7 @@ def tile_two_sided_preconditioned_step_d4_kernel(
                 k, g, u = slots[z]
                 if u == 1 and k < DIRECT_PAIRS:
                     quants[s + 1] = (k, g)
-                elif u == 1 and z < LATE_SLOT:
+                elif u == 1 and z < QUICK_JOIN:
                     joins[s + 1] = (k, g)
                     quants[s + 2] = (k, g)
                 elif u == 1:
@@ -324,7 +333,7 @@ def tile_two_sided_preconditioned_step_d4_kernel(
                 quant_h(*quants[s])
             for k, q in jobs_at(s, HEAD_SCALES, SCALE_AHEAD):
                 scale_right(k, q)
-            for k, q in casts_at(s):
+            for k, q in jobs_at(s, HEAD_CASTS, CAST_AHEAD):
                 cast_right(k, q)
             if 1 <= s <= UNITS // 2:
                 leave_grad(s - 1)
@@ -334,7 +343,7 @@ def tile_two_sided_preconditioned_step_d4_kernel(
                 quant_right(k, q)
             if ready:
                 second_product(*ready.pop(0))
-            if ready and y >= LATE_SLOT and y % 2 == 1:
+            if ready and y >= TWO_TILES and y % 2 == 1:
                 if len(waiting) > 2:
                     finish_tile()
                 second_product(*ready.pop(0))

@@ -27,21 +27,24 @@ BLOCKS = N // B
 PAIR = 2 * B
 PAIRS = N // PAIR
 ROW_TILES = M // P
-BANKS = 4
+BANKS = 8
 SLOTS = 4
 UNITS = GROUPS * 4 * PASSES // 2
+JOBS = PAIRS * PASSES
 
-FIRST_SLOT = UNITS + 1
-QUANT_AHEAD = PASSES
-SCALE_AHEAD = QUANT_AHEAD + 1
-CAST_AHEAD = SCALE_AHEAD + 3
-HEAD_CASTS = (1, 8)
-HEAD_SCALES = (5, 11)
-VECTOR_JOBS = range(2, 7)
-POOL_JOBS = range(10, 15)
-DIRECT_PAIRS = 1
-QUICK_JOIN = 3 * SLOTS
-TWO_TILES = 4 * SLOTS
+SCALAR, VECTOR, POOL = range(3)
+CAST_STEPS = (3, 4, 5, 8, 9, 10)
+S_SCALES = (6, 8)
+V_SCALES = (5, 7, 9, 10)
+S_PIECES = (1, 3, 5)
+LEAVE_LAG = 2
+Q_FROM = 9
+V1_FROM = 5
+V_EXTRA = 0
+LOADS = 0
+TB = 12
+DIRECT = (0,)
+POOL_SUBS = (3, 7, 11, 14, 15)
 W_FIRST = PASS
 
 
@@ -51,8 +54,7 @@ def tile_two_sided_preconditioned_step_d4_kernel(
     with ExitStack() as ctx:
         keep = ctx.enter_context(tc.tile_pool(name="keep", bufs=1))
         rot = ctx.enter_context(tc.tile_pool(name="rot", bufs=3))
-        ps_h = ctx.enter_context(tc.psum_pool(name="ps_h", bufs=BANKS))
-        ps_o = ctx.enter_context(tc.psum_pool(name="ps_o", bufs=BANKS))
+        psum = ctx.enter_context(tc.psum_pool(name="psum", bufs=BANKS))
         ctx.enter_context(tc.manual_schedule())
 
         grad_v = grad_bytes.rearrange("(g p t) k -> g p t k", p=P, t=4)
@@ -95,19 +97,21 @@ def tile_two_sided_preconditioned_step_d4_kernel(
             for r in range(0, ROW_TILES, rows):
                 nc.sync.dma_start(out=tile[:, r : r + rows, :], in_=w_v[:, r : r + rows, lo:hi])
 
+        def load_scales():
+            for s in range(4):
+                nc.sync.dma_start(out=r_scale[32 * s : 32 * s + 32, :, :],
+                                  in_=right_scale.rearrange("(q s) c -> s q c", s=4)[s].partition_broadcast(32))
+
         load_grad(0, 0, 0, 2 * PASS)
-        load_right(0, 0)
         load_grad(0, 0, 2 * PASS, N)
-        load_grad(0, 1, 0, N)
-        load_right(0, 1)
-        load_grad(0, 2, 0, N)
-        for s in range(4):
-            nc.sync.dma_start(out=r_scale[32 * s : 32 * s + 32, :, :],
-                              in_=right_scale.rearrange("(q s) c -> s q c", s=4)[s].partition_broadcast(32))
-        load_right(0, 2)
-        load_grad(0, 3, 0, N)
-        for t in range(4):
-            load_grad(1, t, 0, N)
+        seq = ("g1 g2 r0 g3 r1 s g4 r2 g5 g6 g7", "g1 r0 g2 r1 g3 s r2 g4 g5 g6 g7", "g1 g2 g3 r0 r1 g4 s r2 g5 g6 g7", "g1 g2 r0 g3 r1 g4 r2 s g5 g6 g7")[LOADS]
+        for x in seq.split():
+            if x == "s":
+                load_scales()
+            elif x[0] == "g":
+                load_grad(int(x[1]) // 4, int(x[1]) % 4, 0, N)
+            else:
+                load_right(0, int(x[1]))
         load_passes(1)
         load_step(0)
         load_passes(2)
@@ -115,8 +119,8 @@ def tile_two_sided_preconditioned_step_d4_kernel(
             nc.sync.dma_start(out=lt_s[32 * s : 32 * s + 4, :, :].bitcast(I32),
                               in_=lt_scales.rearrange("g (s r) n -> s r g n", s=4)[s].bitcast(I32))
         nc.sync.dma_start(out=lt_w[:], in_=lt_words.rearrange("g p n -> p g n"))
-        load_passes(3)
         load_w(w_first, 0, W_FIRST)
+        load_passes(3)
         load_step(1)
         load_passes(4)
         load_w(w_rest, W_FIRST, N)
@@ -125,18 +129,21 @@ def tile_two_sided_preconditioned_step_d4_kernel(
 
         pieces = [(g, t, q) for g in range(GROUPS) for t in range(4) for q in range(PASSES)]
         g_codes = [keep.tile([P, 4 * PASSES * P], U32, name="g_codes%d" % g, align_bytes=64) for g in range(GROUPS)]
-        g_bytes = [keep.tile([P, 4 * PASSES * P + 256], U8, name="g_bytes%d" % g, align_bytes=64)[:, 64 : 64 + 4 * PASSES * P]
-                   for g in range(GROUPS)]
+        g_bytes = [keep.tile([P, 4 * PASSES * P], U8, name="g_bytes%d" % g, align_bytes=64) for g in range(GROUPS)]
         g_wide = {}
         g_ps = {}
         g_turned = {}
 
         def widen_grad(s):
             for e, (g, t, q) in enumerate(pieces[2 * s : 2 * s + 2]):
-                wide = rot.tile([P, PASS], BF16, name="g_wide", bufs=6)
+                wide = rot.tile([P, PASS], BF16, name="g_wide", bufs=10)
                 dst = wide[:].rearrange("p (h a f) -> p a h f", h=2, f=2)
                 for c in range(4):
                     k0 = PASS * q + B * c
+                    if 2 * s + e in S_PIECES:
+                        nc.scalar.activation(out=wide[:, B * c : B * c + B], in_=g_raw[g][t][:, k0 : k0 + B].bitcast(E4M3), func=COPY,
+                                             scale=g_scale[:, g, t * BLOCKS + 4 * q + c : t * BLOCKS + 4 * q + c + 1])
+                        continue
                     src = g_raw[g][t][:, k0 : k0 + B].bitcast(E4M3).rearrange("p (a h f) -> p a h f", h=2, f=2)
                     col = t * BLOCKS + 4 * q + c
                     nc.vector.tensor_scalar(out=dst[:, 32 * c : 32 * c + 32, :, :], in0=src,
@@ -144,15 +151,16 @@ def tile_two_sided_preconditioned_step_d4_kernel(
                 g_wide[s, e] = wide
 
         def turn_grad(s):
-            ps = ps_o.tile([P, 2, 2, P], F32, name="bank_o")
+            ps = psum.tile([P, 2, 2, P], F32, name="bank")
             for e in range(2):
                 words = g_wide[s, e][:].bitcast(F32)
                 for h in range(2):
-                    nc.tensor.transpose(ps[:, e, h, :], words[:, P * h : P * h + P], ident[:])
+                    src = words[:, h : 2 * P : 2] if 2 * s + e in S_PIECES else words[:, P * h : P * h + P]
+                    nc.tensor.transpose(ps[:, e, h, :], src, ident[:])
             g_ps[s] = ps
 
         def leave_grad(s):
-            x = rot.tile([P, 2 * PASS], BF16, name="g_turned", align_bytes=64, bufs=4)
+            x = rot.tile([P, 2 * PASS], BF16, name="g_turned", align_bytes=64, bufs=TB)
             nc.scalar.copy(out=x[:].bitcast(F32).rearrange("p (e m h) -> p e m h", e=2, h=2),
                            in_=g_ps[s][:].rearrange("p e h m -> p e m h"))
             g_turned[s] = x
@@ -164,7 +172,6 @@ def tile_two_sided_preconditioned_step_d4_kernel(
 
         r_planes = {}
         r_wide = {}
-        r_pool = {}
         r_codes = {}
         r_bytes = {}
 
@@ -173,41 +180,35 @@ def tile_two_sided_preconditioned_step_d4_kernel(
             nc.scalar.copy(out=r_planes[k, q][:].rearrange("p t n -> p (t n)"),
                            in_=r_raw[k][q][:].rearrange("p t n -> p (t n)").bitcast(E4M3))
 
-        def scale_right(k, q):
-            r_wide[k, q] = rot.tile([P, 4 * PAIR], BF16, name="r_wide", align_bytes=64, bufs=6)
-            for b in range(1 if PASSES * k + q in POOL_JOBS else 2):
-                dst = r_wide[k, q][:, 4 * B * b : 4 * B * b + 4 * B].rearrange("p (c i t) -> p c t i", t=4, i=4)
-                src = r_planes[k, q][:, :, B * b : B * b + B].rearrange("p t (c i) -> p c t i", i=4)
-                scale = r_scale[:, q, 2 * k + b : 2 * k + b + 1]
-                if b == 0 and PASSES * k + q in VECTOR_JOBS:
-                    nc.vector.tensor_scalar(out=dst, in0=src, scalar1=scale, scalar2=None, op0=MULT)
-                else:
-                    nc.scalar.activation(out=dst, in_=src, func=COPY, scale=scale)
+        def scale_right(k, q, b, engine):
+            if engine == POOL or (k, b) == (1, 1):
+                r_wide[k, q, b] = rot.tile([P, 4 * B], BF16, name="r_pool", align_bytes=64, bufs=PASSES)
+            else:
+                r_wide[k, q, b] = rot.tile([P, 4 * B], BF16, name="r_wide", align_bytes=64, bufs=8)
+            dst = r_wide[k, q, b][:]
+            src = r_planes[k, q][:, :, B * b : B * b + B]
+            scale = r_scale[:, q, 2 * k + b : 2 * k + b + 1]
+            if engine == POOL:
+                nc.gpsimd.tensor_scalar(out=dst.rearrange("p (n t) -> p n t", t=4), in0=src.rearrange("p t n -> p n t"),
+                                        scalar1=scale, scalar2=0.0, op0=MULT, op1=ADD)
+                return
+            dst = dst.rearrange("p (c i t) -> p c t i", t=4, i=4)
+            src = src.rearrange("p t (c i) -> p c t i", i=4)
+            if engine == VECTOR:
+                nc.vector.tensor_scalar(out=dst, in0=src, scalar1=scale, scalar2=None, op0=MULT)
+            else:
+                nc.scalar.activation(out=dst, in_=src, func=COPY, scale=scale)
 
-        def scale_on_pool(k, q):
-            r_pool[k, q] = rot.tile([P, 4 * B], BF16, name="r_pool", align_bytes=64, bufs=1)
-            nc.gpsimd.tensor_scalar(out=r_pool[k, q][:].rearrange("p (n t) -> p n t", t=4),
-                                    in0=r_planes[k, q][:, :, B:PAIR].rearrange("p t n -> p n t"),
-                                    scalar1=r_scale[:, q, 2 * k + 1 : 2 * k + 2], scalar2=0.0, op0=MULT, op1=ADD)
-
-        def quant_right(k, q):
-            if q == 0:
+        def quant_block(k, q, b):
+            if k not in r_codes:
                 r_codes[k] = keep.tile([P, PASSES, PAIR], U32, name="r_codes%d" % k, align_bytes=64)
                 r_bytes[k] = keep.tile([P, PASSES, PAIR], U8, name="r_bytes%d" % k, align_bytes=64)
-            job = PASSES * k + q
-            parts = [(0, PAIR, r_wide[k, q][:])]
-            if job in POOL_JOBS:
-                parts = [(0, B, r_wide[k, q][:, 0 : 4 * B]), (B, PAIR, r_pool[k, q][:])]
-            for lo, hi, src in parts:
-                nc.vector.quantize_mx(out=r_codes[k][:, q, lo:hi].bitcast(E4M3X4), scales=r_bytes[k][:, q, lo:hi], in_=src)
-            if job + 1 in POOL_JOBS:
-                scale_on_pool(*divmod(job + 1, PASSES))
+            n = slice(B * b, B * b + B)
+            nc.vector.quantize_mx(out=r_codes[k][:, q, n].bitcast(E4M3X4), scales=r_bytes[k][:, q, n], in_=r_wide[k, q, b][:])
 
-        def warm_up(count):
-            ps = ps_h.tile([P, PASS], F32, name="bank_h")
-            planes = r_planes[0, PASSES - 1][:].rearrange("p t n -> p (t n)")
-            for x in range(count):
-                nc.tensor.matmul(out=ps[:], lhsT=planes[:, 0:P], rhs=planes[:, 0:PASS], start=True, stop=True)
+        def quant_right(k, q):
+            quant_block(k, q, 1)
+            quant_block(k, q, 0)
 
         slots = [(k, g, u) for k in range(PAIRS) for g in range(GROUPS) for u in range(2)]
         h_codes = [keep.tile([P, N], U32, name="h_codes%d" % g, align_bytes=64) for g in range(GROUPS)]
@@ -217,7 +218,7 @@ def tile_two_sided_preconditioned_step_d4_kernel(
         h_joined = {}
 
         def slot_shape(k, u):
-            if k < DIRECT_PAIRS:
+            if k in DIRECT:
                 return range(4), slice(B * u, B * u + B)
             return range(2 * u, 2 * u + 2), slice(0, PAIR)
 
@@ -225,7 +226,7 @@ def tile_two_sided_preconditioned_step_d4_kernel(
             k, g, u = slots[y]
             row_tiles, n = slot_shape(k, u)
             if lo == 0:
-                h_ps[y] = ps_h.tile([P, len(row_tiles), PASS // len(row_tiles)], F32, name="bank_h")
+                h_ps[y] = psum.tile([P, len(row_tiles), PASS // len(row_tiles)], F32, name="bank")
             for e in range(lo, hi):
                 for q in range(PASSES):
                     m = slice(P * (PASSES * row_tiles[e] + q), P * (PASSES * row_tiles[e] + q + 1))
@@ -253,101 +254,128 @@ def tile_two_sided_preconditioned_step_d4_kernel(
 
         def quant_h(k, g):
             n = slice(PAIR * k, PAIR * k + PAIR)
-            src = h_parts[k, g][:].rearrange("p u n -> p (u n)") if k < DIRECT_PAIRS else h_joined[k, g][:]
+            src = h_parts[k, g][:].rearrange("p u n -> p (u n)") if k in DIRECT else h_joined[k, g][:]
             nc.vector.quantize_mx(out=h_codes[g][:, n].bitcast(E4M3X4), scales=h_bytes[g][:, n], in_=src)
-            if g == GROUPS - 1:
-                ready.extend((k, r0) for r0 in range(0, ROW_TILES, 2))
 
-        ready = []
-        waiting = []
+        tiles = [(k, r0) for k in range(PAIRS) for r0 in range(0, ROW_TILES, 2)]
+        u_ps = {}
 
-        def second_product(k, r0):
-            if len(waiting) == BANKS:
-                finish_tile()
-            ps = ps_o.tile([P, 2, PAIR], F32, name="bank_o")
-            passes = [(x, g, b) for x in range(2) for g in range(GROUPS) for b in range(2)]
-            for j, (x, g, b) in enumerate(passes):
+        def second_product(j):
+            k, r0 = tiles[j]
+            u_ps[j] = psum.tile([P, 2, PAIR], F32, name="bank")
+            n = slice(PAIR * k, PAIR * k + PAIR)
+            for x in range(2):
                 r = r0 + x
-                n = slice(PAIR * k + B * b, PAIR * k + B * b + B)
-                nc.tensor.matmul_mx(out=ps[:, x, B * b : B * b + B],
-                                    lhsT=lt_w[:, g, 2 * P * r : 2 * P * r + 2 * P].bitcast(E2M1X4),
-                                    lhsT_scale=lt_s[:, g, P * r : P * r + P],
-                                    rhs=h_codes[g][:, n].bitcast(E4M3X4), rhs_scale=h_bytes[g][:, n],
-                                    start=(j == 0), stop=(j == len(passes) - 1))
-            waiting.append((ps, k, r0))
+                for g in range(GROUPS):
+                    nc.tensor.matmul_mx(out=u_ps[j][:, x, :],
+                                        lhsT=lt_w[:, g, 2 * P * r : 2 * P * r + 2 * P].bitcast(E2M1X4),
+                                        lhsT_scale=lt_s[:, g, P * r : P * r + P],
+                                        rhs=h_codes[g][:, n].bitcast(E4M3X4), rhs_scale=h_bytes[g][:, n],
+                                        start=(g == 0), stop=(g == GROUPS - 1))
 
-        def finish_tile():
-            ps, k, r0 = waiting.pop(0)
+        def finish_tile(j):
+            k, r0 = tiles[j]
             tile, n0 = (w_first, PAIR * k) if PAIR * k < W_FIRST else (w_rest, PAIR * k - W_FIRST)
             result = rot.tile([P, 2, PAIR], F32, name="result", bufs=10)
-            nc.vector.tensor_tensor(out=result[:], in0=tile[:, r0 : r0 + 2, n0 : n0 + PAIR], in1=ps[:], op=SUB)
+            if j in POOL_SUBS:
+                u = rot.tile([P, 2, PAIR], F32, name="u", bufs=2)
+                nc.scalar.copy(out=u[:], in_=u_ps[j][:])
+                nc.gpsimd.tensor_tensor(out=result[:], in0=tile[:, r0 : r0 + 2, n0 : n0 + PAIR], in1=u[:], op=SUB)
+            else:
+                nc.vector.tensor_tensor(out=result[:], in0=tile[:, r0 : r0 + 2, n0 : n0 + PAIR], in1=u_ps[j][:], op=SUB)
             nc.sync.dma_start(out=out_v[:, r0 : r0 + 2, PAIR * k : PAIR * k + PAIR], in_=result[:])
 
-        def jobs_at(s, head_steps, ahead):
-            jobs = [(k, s - first) for k, first in enumerate(head_steps) if 0 <= s - first < PASSES]
-            k, q = divmod(s - FIRST_SLOT + ahead, SLOTS)
-            return jobs + ([(k, q)] if len(head_steps) <= k < PAIRS and q < PASSES else [])
-
-        halves = [(0, 0), (0, 2), (1, 0), (1, 2), (2, 0), (3, 0)]
-        last = len(slots) - 1
-        joins = {}
-        quants = {}
-        for s in range(FIRST_SLOT + last + 5):
-            y = s - FIRST_SLOT
-            if s < UNITS:
-                widen_grad(s)
-            if 1 <= s <= UNITS:
+        casts = [(0, q) for q in range(PASSES)] + [(1, q) for q in range(PASSES)]
+        blocks = [(0, q, b) for q in range(PASSES) for b in range(2)]
+        for s in range(UNITS):
+            widen_grad(s)
+            if s >= 1:
                 turn_grad(s - 1)
-            if s == UNITS - 3:
-                warm_up(2)
-            if s == UNITS - 2:
-                warm_up(1)
-            if s >= UNITS - 1:
-                for z, lo in halves[: 1 if s < UNITS else 2]:
-                    first_product(z, lo, lo + 2)
-                halves = halves[1 if s < UNITS else 2 :]
-            if y == 2:
-                first_product(2, 2, 4)
-                first_product(3, 2, 4)
-            if SLOTS <= y <= last:
-                first_product(y, 0, 4 if slots[y][0] < DIRECT_PAIRS else 2)
-            if s in joins:
-                join_h(*joins[s])
-            if UNITS // 2 < s <= UNITS:
-                leave_grad(s - 1)
-            z = y - 1 if y <= SLOTS else y - 2
-            if 0 <= z <= last and y != SLOTS + 1:
-                step_h(z)
-                k, g, u = slots[z]
-                if u == 1 and k < DIRECT_PAIRS:
-                    quants[s + 1] = (k, g)
-                elif u == 1 and z < QUICK_JOIN:
-                    joins[s + 1] = (k, g)
-                    quants[s + 2] = (k, g)
-                elif u == 1:
-                    join_h(k, g)
-                    quants[s + 1] = (k, g)
-            if len(waiting) > 1:
-                finish_tile()
-            if s in quants:
-                quant_h(*quants[s])
-            for k, q in jobs_at(s, HEAD_SCALES, SCALE_AHEAD):
-                scale_right(k, q)
-            for k, q in jobs_at(s, HEAD_CASTS, CAST_AHEAD):
-                cast_right(k, q)
-            if 1 <= s <= UNITS // 2:
-                leave_grad(s - 1)
-            if 3 <= s < UNITS + 3:
-                quant_grad(s - 3)
-            for k, q in jobs_at(s, [first + 2 for first in HEAD_SCALES], QUANT_AHEAD):
-                quant_right(k, q)
-            if ready:
-                second_product(*ready.pop(0))
-            if ready and y >= TWO_TILES and y % 2 == 1:
-                if len(waiting) > 2:
-                    finish_tile()
-                second_product(*ready.pop(0))
-        for k, r0 in ready:
-            second_product(k, r0)
-        for x in range(len(waiting)):
-            finish_tile()
+            if s in CAST_STEPS:
+                cast_right(*casts.pop(0))
+            if s >= LEAVE_LAG:
+                leave_grad(s - LEAVE_LAG)
+            if s in S_SCALES:
+                scale_right(*blocks.pop(0), SCALAR)
+            if s in V_SCALES:
+                scale_right(*blocks.pop(0), VECTOR)
+            if s >= Q_FROM:
+                quant_grad(s - Q_FROM)
+        turn_grad(UNITS - 1)
+        for s in range(UNITS - LEAVE_LAG, UNITS):
+            leave_grad(s)
+        for q in range(PASSES):
+            quant_right(0, q)
+        for q in range(PASSES):
+            scale_right(1, q, 0, SCALAR if q >= V_EXTRA else VECTOR)
+        for q in range(PASSES):
+            cast_right(2, q)
+        for s in range(UNITS):
+            if s >= UNITS - Q_FROM:
+                quant_grad(s)
+            if s % PASSES == PASSES - 1:
+                g, half = divmod(s // PASSES, 2)
+                first_product(2 * g, 2 * half, 2 * half + 2)
+                first_product(2 * g + 1, 2 * half, 2 * half + 2)
+            if 0 <= s - V1_FROM < PASSES:
+                scale_right(1, s - V1_FROM, 1, VECTOR)
+        for q in range(PASSES):
+            quant_right(1, q)
+        for q in range(PASSES):
+            scale_right(2, q, 1, POOL)
+            scale_right(2, q, 0, SCALAR)
+        for y in range(SLOTS):
+            step_h(y)
+        quant_h(0, 0)
+        quant_h(0, 1)
+
+        for k in range(PAIRS - 1):
+            y = SLOTS * (k + 1)
+            j = SLOTS * k
+            now = k + 2 < PAIRS
+            nxt = k + 3 < PAIRS
+            for x in range(SLOTS):
+                first_product(y + x, 0, 2)
+            if k > 0:
+                finish_tile(j - 2)
+                finish_tile(j - 1)
+                if now:
+                    scale_right(k + 2, 2, 0, SCALAR)
+                    scale_right(k + 2, 2, 1, SCALAR)
+            if nxt:
+                cast_right(k + 3, 0)
+                cast_right(k + 3, 1)
+            if k == 0:
+                for q in range(PASSES):
+                    quant_right(k + 2, q)
+            step_h(y)
+            step_h(y + 1)
+            join_h(k + 1, 0)
+            if now and k > 0:
+                for q in range(PASSES):
+                    quant_right(k + 2, q)
+            if nxt:
+                scale_right(k + 3, 0, 1, POOL)
+                scale_right(k + 3, 1, 1, POOL)
+                cast_right(k + 3, 2)
+                scale_right(k + 3, 0, 0, SCALAR)
+            step_h(y + 2)
+            step_h(y + 3)
+            join_h(k + 1, 1)
+            if nxt:
+                scale_right(k + 3, 1, 0, SCALAR)
+            for x in range(SLOTS):
+                second_product(j + x)
+            finish_tile(j)
+            if k == PAIRS - 2:
+                quant_h(k + 1, 0)
+            finish_tile(j + 1)
+            if k < PAIRS - 2:
+                quant_h(k + 1, 0)
+            quant_h(k + 1, 1)
+        j = len(tiles) - SLOTS
+        finish_tile(j - 2)
+        finish_tile(j - 1)
+        for x in range(SLOTS):
+            second_product(j + x)
+            finish_tile(j + x)

@@ -36,7 +36,7 @@ SCALAR, VECTOR, POOL = range(3)
 CAST_STEPS = (3, 4, 5, 8, 9, 10)
 S_SCALES = (6, 8)
 V_SCALES = (5, 7, 9, 10)
-S_PIECES = (1, 3, 5)
+S_PIECES = ()
 LEAVE_LAG = 2
 Q_FROM = 9
 V1_FROM = 5

@@ -129,7 +129,8 @@ def tile_two_sided_preconditioned_step_d4_kernel(
 
         pieces = [(g, t, q) for g in range(GROUPS) for t in range(4) for q in range(PASSES)]
         g_codes = [keep.tile([P, 4 * PASSES * P], U32, name="g_codes%d" % g, align_bytes=64) for g in range(GROUPS)]
-        g_bytes = [keep.tile([P, 4 * PASSES * P], U8, name="g_bytes%d" % g, align_bytes=64) for g in range(GROUPS)]
+        g_bytes = [keep.tile([P, 4 * PASSES * P + 256], U8, name="g_bytes%d" % g, align_bytes=64)[:, 64 : 64 + 4 * PASSES * P]
+                   for g in range(GROUPS)]
         g_wide = {}
         g_ps = {}
         g_turned = {}

@@ -30,22 +30,12 @@ ROW_TILES = M // P
 BANKS = 8
 SLOTS = 4
 UNITS = GROUPS * 4 * PASSES // 2
-JOBS = PAIRS * PASSES
-
 SCALAR, VECTOR, POOL = range(3)
-CAST_STEPS = (3, 4, 5, 8, 9, 10)
-S_SCALES = (6, 8)
-V_SCALES = (5, 7, 9, 10)
-S_PIECES = ()
+
 LEAVE_LAG = 2
-Q_FROM = 9
-V1_FROM = 5
-V_EXTRA = 0
-LOADS = 0
-TB = 12
-DIRECT = (0,)
-POOL_SUBS = (3, 7, 11, 14, 15)
-W_FIRST = PASS
+CAST_FROM = (3, 8)
+SCALE_FROM = 5
+QUANT_FROM = 9
 
 
 def tile_two_sided_preconditioned_step_d4_kernel(
@@ -72,19 +62,19 @@ def tile_two_sided_preconditioned_step_d4_kernel(
 
         g_raw = [[keep.tile([P, N], U8, name="g_raw%d%d" % (g, t)) for t in range(4)] for g in range(GROUPS)]
         r_raw = [[keep.tile([P, 4, PAIR], U8, name="r_raw%d%d" % (k, q)) for q in range(PASSES)] for k in range(PAIRS)]
-        w_first = keep.tile([P, ROW_TILES, W_FIRST], BF16, name="w_first")
-        w_rest = keep.tile([P, ROW_TILES, N - W_FIRST], BF16, name="w_rest")
+        w_first = keep.tile([P, ROW_TILES, PASS], BF16, name="w_first")
+        w_rest = keep.tile([P, ROW_TILES, N - PASS], BF16, name="w_rest")
         lt_w = keep.tile([P, GROUPS, 2 * M], U8, name="lt_w", align_bytes=64)
         step_all = keep.tile([P, N], BF16, name="step_all")
         r_scale = keep.tile([P, PASSES, BLOCKS], F32, name="r_scale")
 
-        def load_grad(g, t, lo, hi):
+        def load_grad(g, t, lo=0, hi=N):
             nc.sync.dma_start(out=g_raw[g][t][:, lo:hi], in_=grad_v[g][:, t, lo:hi])
 
         def load_right(k, q):
             nc.sync.dma_start(out=r_raw[k][q][:], in_=right_v[q][:, :, PAIR * k : PAIR * k + PAIR])
 
-        def load_passes(k):
+        def load_pair(k):
             for q in range(PASSES):
                 load_right(k, q)
 
@@ -97,34 +87,33 @@ def tile_two_sided_preconditioned_step_d4_kernel(
             for r in range(0, ROW_TILES, rows):
                 nc.sync.dma_start(out=tile[:, r : r + rows, :], in_=w_v[:, r : r + rows, lo:hi])
 
-        def load_scales():
-            for s in range(4):
-                nc.sync.dma_start(out=r_scale[32 * s : 32 * s + 32, :, :],
-                                  in_=right_scale.rearrange("(q s) c -> s q c", s=4)[s].partition_broadcast(32))
-
         load_grad(0, 0, 0, 2 * PASS)
         load_grad(0, 0, 2 * PASS, N)
-        seq = ("g1 g2 r0 g3 r1 s g4 r2 g5 g6 g7", "g1 r0 g2 r1 g3 s r2 g4 g5 g6 g7", "g1 g2 g3 r0 r1 g4 s r2 g5 g6 g7", "g1 g2 r0 g3 r1 g4 r2 s g5 g6 g7")[LOADS]
-        for x in seq.split():
-            if x == "s":
-                load_scales()
-            elif x[0] == "g":
-                load_grad(int(x[1]) // 4, int(x[1]) % 4, 0, N)
-            else:
-                load_right(0, int(x[1]))
-        load_passes(1)
+        load_grad(0, 1)
+        load_grad(0, 2)
+        load_right(0, 0)
+        load_grad(0, 3)
+        load_right(0, 1)
+        for s in range(4):
+            nc.sync.dma_start(out=r_scale[32 * s : 32 * s + 32, :, :],
+                              in_=right_scale.rearrange("(q s) c -> s q c", s=4)[s].partition_broadcast(32))
+        load_grad(1, 0)
+        load_right(0, 2)
+        for t in range(1, 4):
+            load_grad(1, t)
+        load_pair(1)
         load_step(0)
-        load_passes(2)
+        load_pair(2)
         for s in range(4):
             nc.sync.dma_start(out=lt_s[32 * s : 32 * s + 4, :, :].bitcast(I32),
                               in_=lt_scales.rearrange("g (s r) n -> s r g n", s=4)[s].bitcast(I32))
         nc.sync.dma_start(out=lt_w[:], in_=lt_words.rearrange("g p n -> p g n"))
-        load_w(w_first, 0, W_FIRST)
-        load_passes(3)
+        load_w(w_first, 0, PASS)
+        load_pair(3)
         load_step(1)
-        load_passes(4)
-        load_w(w_rest, W_FIRST, N)
-        load_passes(5)
+        load_pair(4)
+        load_w(w_rest, PASS, N)
+        load_pair(5)
         load_step(2)
 
         pieces = [(g, t, q) for g in range(GROUPS) for t in range(4) for q in range(PASSES)]
@@ -141,10 +130,6 @@ def tile_two_sided_preconditioned_step_d4_kernel(
                 dst = wide[:].rearrange("p (h a f) -> p a h f", h=2, f=2)
                 for c in range(4):
                     k0 = PASS * q + B * c
-                    if 2 * s + e in S_PIECES:
-                        nc.scalar.activation(out=wide[:, B * c : B * c + B], in_=g_raw[g][t][:, k0 : k0 + B].bitcast(E4M3), func=COPY,
-                                             scale=g_scale[:, g, t * BLOCKS + 4 * q + c : t * BLOCKS + 4 * q + c + 1])
-                        continue
                     src = g_raw[g][t][:, k0 : k0 + B].bitcast(E4M3).rearrange("p (a h f) -> p a h f", h=2, f=2)
                     col = t * BLOCKS + 4 * q + c
                     nc.vector.tensor_scalar(out=dst[:, 32 * c : 32 * c + 32, :, :], in0=src,
@@ -152,19 +137,16 @@ def tile_two_sided_preconditioned_step_d4_kernel(
                 g_wide[s, e] = wide
 
         def turn_grad(s):
-            ps = psum.tile([P, 2, 2, P], F32, name="bank")
+            g_ps[s] = psum.tile([P, 2, 2, P], F32, name="bank")
             for e in range(2):
                 words = g_wide[s, e][:].bitcast(F32)
                 for h in range(2):
-                    src = words[:, h : 2 * P : 2] if 2 * s + e in S_PIECES else words[:, P * h : P * h + P]
-                    nc.tensor.transpose(ps[:, e, h, :], src, ident[:])
-            g_ps[s] = ps
+                    nc.tensor.transpose(g_ps[s][:, e, h, :], words[:, P * h : P * h + P], ident[:])
 
         def leave_grad(s):
-            x = rot.tile([P, 2 * PASS], BF16, name="g_turned", align_bytes=64, bufs=TB)
-            nc.scalar.copy(out=x[:].bitcast(F32).rearrange("p (e m h) -> p e m h", e=2, h=2),
+            g_turned[s] = rot.tile([P, 2 * PASS], BF16, name="g_turned", align_bytes=64, bufs=UNITS)
+            nc.scalar.copy(out=g_turned[s][:].bitcast(F32).rearrange("p (e m h) -> p e m h", e=2, h=2),
                            in_=g_ps[s][:].rearrange("p e h m -> p e m h"))
-            g_turned[s] = x
 
         def quant_grad(s):
             g, t, q = pieces[2 * s]
@@ -177,7 +159,7 @@ def tile_two_sided_preconditioned_step_d4_kernel(
         r_bytes = {}
 
         def cast_right(k, q):
-            r_planes[k, q] = rot.tile([P, 4, PAIR], BF16, name="r_planes", bufs=6)
+            r_planes[k, q] = rot.tile([P, 4, PAIR], BF16, name="r_planes", bufs=2 * PASSES)
             nc.scalar.copy(out=r_planes[k, q][:].rearrange("p t n -> p (t n)"),
                            in_=r_raw[k][q][:].rearrange("p t n -> p (t n)").bitcast(E4M3))
 
@@ -200,16 +182,14 @@ def tile_two_sided_preconditioned_step_d4_kernel(
             else:
                 nc.scalar.activation(out=dst, in_=src, func=COPY, scale=scale)
 
-        def quant_block(k, q, b):
-            if k not in r_codes:
-                r_codes[k] = keep.tile([P, PASSES, PAIR], U32, name="r_codes%d" % k, align_bytes=64)
-                r_bytes[k] = keep.tile([P, PASSES, PAIR], U8, name="r_bytes%d" % k, align_bytes=64)
-            n = slice(B * b, B * b + B)
-            nc.vector.quantize_mx(out=r_codes[k][:, q, n].bitcast(E4M3X4), scales=r_bytes[k][:, q, n], in_=r_wide[k, q, b][:])
-
-        def quant_right(k, q):
-            quant_block(k, q, 1)
-            quant_block(k, q, 0)
+        def quant_pair(k):
+            r_codes[k] = keep.tile([P, PASSES, PAIR], U32, name="r_codes%d" % k, align_bytes=64)
+            r_bytes[k] = keep.tile([P, PASSES, PAIR], U8, name="r_bytes%d" % k, align_bytes=64)
+            for q in range(PASSES):
+                for b in (1, 0):
+                    n = slice(B * b, B * b + B)
+                    nc.vector.quantize_mx(out=r_codes[k][:, q, n].bitcast(E4M3X4), scales=r_bytes[k][:, q, n],
+                                          in_=r_wide[k, q, b][:])
 
         slots = [(k, g, u) for k in range(PAIRS) for g in range(GROUPS) for u in range(2)]
         h_codes = [keep.tile([P, N], U32, name="h_codes%d" % g, align_bytes=64) for g in range(GROUPS)]
@@ -219,16 +199,16 @@ def tile_two_sided_preconditioned_step_d4_kernel(
         h_joined = {}
 
         def slot_shape(k, u):
-            if k in DIRECT:
+            if k == 0:
                 return range(4), slice(B * u, B * u + B)
             return range(2 * u, 2 * u + 2), slice(0, PAIR)
 
-        def first_product(y, lo, hi):
+        def first_product(y, lo=0):
             k, g, u = slots[y]
             row_tiles, n = slot_shape(k, u)
             if lo == 0:
                 h_ps[y] = psum.tile([P, len(row_tiles), PASS // len(row_tiles)], F32, name="bank")
-            for e in range(lo, hi):
+            for e in range(lo, lo + 2):
                 for q in range(PASSES):
                     m = slice(P * (PASSES * row_tiles[e] + q), P * (PASSES * row_tiles[e] + q + 1))
                     nc.tensor.matmul_mx(out=h_ps[y][:, e, :],
@@ -243,19 +223,18 @@ def tile_two_sided_preconditioned_step_d4_kernel(
                 h_parts[k, g] = rot.tile([P, 2, PASS], BF16, name="h_parts", align_bytes=64, bufs=4)
             steps = step_all[:, PAIR * k + n.start : PAIR * k + n.stop].rearrange("p (c i) -> p c i", i=2)
             nc.vector.tensor_tensor(out=h_parts[k, g][:, u, :].rearrange("p (c i e) -> p c e i", i=2, e=len(row_tiles)),
-                                    in0=h_ps[y][:].rearrange("p e (c i) -> p c e i", i=2),
-                                    in1=steps.unsqueeze(2).to_broadcast([P, (n.stop - n.start) // 2, len(row_tiles), 2]),
+                                    in0=steps.unsqueeze(2).to_broadcast([P, (n.stop - n.start) // 2, len(row_tiles), 2]),
+                                    in1=h_ps[y][:].rearrange("p e (c i) -> p c e i", i=2),
                                     op=MULT)
 
         def join_h(k, g):
-            x = rot.tile([P, 4 * PAIR], BF16, name="h_joined", align_bytes=64)
-            nc.scalar.copy(out=x[:].bitcast(F32).rearrange("p (n u) -> p n u", u=2),
+            h_joined[k, g] = rot.tile([P, 4 * PAIR], BF16, name="h_joined", align_bytes=64)
+            nc.scalar.copy(out=h_joined[k, g][:].bitcast(F32).rearrange("p (n u) -> p n u", u=2),
                            in_=h_parts[k, g][:].bitcast(F32).rearrange("p u n -> p n u"))
-            h_joined[k, g] = x
 
         def quant_h(k, g):
             n = slice(PAIR * k, PAIR * k + PAIR)
-            src = h_parts[k, g][:].rearrange("p u n -> p (u n)") if k in DIRECT else h_joined[k, g][:]
+            src = h_parts[k, g][:].rearrange("p u n -> p (u n)") if k == 0 else h_joined[k, g][:]
             nc.vector.quantize_mx(out=h_codes[g][:, n].bitcast(E4M3X4), scales=h_bytes[g][:, n], in_=src)
 
         tiles = [(k, r0) for k in range(PAIRS) for r0 in range(0, ROW_TILES, 2)]
@@ -274,54 +253,53 @@ def tile_two_sided_preconditioned_step_d4_kernel(
                                         rhs=h_codes[g][:, n].bitcast(E4M3X4), rhs_scale=h_bytes[g][:, n],
                                         start=(g == 0), stop=(g == GROUPS - 1))
 
-        def finish_tile(j):
+        def finish_tile(j, engine=VECTOR):
             k, r0 = tiles[j]
-            tile, n0 = (w_first, PAIR * k) if PAIR * k < W_FIRST else (w_rest, PAIR * k - W_FIRST)
+            tile, n0 = (w_first, PAIR * k) if PAIR * k < PASS else (w_rest, PAIR * k - PASS)
+            old = tile[:, r0 : r0 + 2, n0 : n0 + PAIR]
             result = rot.tile([P, 2, PAIR], F32, name="result", bufs=10)
-            if j in POOL_SUBS:
+            if engine == POOL:
                 u = rot.tile([P, 2, PAIR], F32, name="u", bufs=2)
                 nc.scalar.copy(out=u[:], in_=u_ps[j][:])
-                nc.gpsimd.tensor_tensor(out=result[:], in0=tile[:, r0 : r0 + 2, n0 : n0 + PAIR], in1=u[:], op=SUB)
+                nc.gpsimd.tensor_tensor(out=result[:], in0=old, in1=u[:], op=SUB)
             else:
-                nc.vector.tensor_tensor(out=result[:], in0=tile[:, r0 : r0 + 2, n0 : n0 + PAIR], in1=u_ps[j][:], op=SUB)
+                nc.vector.tensor_tensor(out=result[:], in0=old, in1=u_ps[j][:], op=SUB)
             nc.sync.dma_start(out=out_v[:, r0 : r0 + 2, PAIR * k : PAIR * k + PAIR], in_=result[:])
 
-        casts = [(0, q) for q in range(PASSES)] + [(1, q) for q in range(PASSES)]
-        blocks = [(0, q, b) for q in range(PASSES) for b in range(2)]
+        blocks = [(q, b) for q in range(PASSES) for b in range(2)]
         for s in range(UNITS):
             widen_grad(s)
             if s >= 1:
                 turn_grad(s - 1)
-            if s in CAST_STEPS:
-                cast_right(*casts.pop(0))
+            for k, first in enumerate(CAST_FROM):
+                if 0 <= s - first < PASSES:
+                    cast_right(k, s - first)
             if s >= LEAVE_LAG:
                 leave_grad(s - LEAVE_LAG)
-            if s in S_SCALES:
-                scale_right(*blocks.pop(0), SCALAR)
-            if s in V_SCALES:
-                scale_right(*blocks.pop(0), VECTOR)
-            if s >= Q_FROM:
-                quant_grad(s - Q_FROM)
+            x = s - SCALE_FROM
+            if 0 <= x < len(blocks):
+                scale_right(0, *blocks[x], SCALAR if x % 2 and x < len(blocks) - 1 else VECTOR)
+            if s >= QUANT_FROM:
+                quant_grad(s - QUANT_FROM)
         turn_grad(UNITS - 1)
         for s in range(UNITS - LEAVE_LAG, UNITS):
             leave_grad(s)
+        quant_pair(0)
         for q in range(PASSES):
-            quant_right(0, q)
-        for q in range(PASSES):
-            scale_right(1, q, 0, SCALAR if q >= V_EXTRA else VECTOR)
+            scale_right(1, q, 0, SCALAR)
         for q in range(PASSES):
             cast_right(2, q)
         for s in range(UNITS):
-            if s >= UNITS - Q_FROM:
+            if s >= UNITS - QUANT_FROM:
                 quant_grad(s)
             if s % PASSES == PASSES - 1:
                 g, half = divmod(s // PASSES, 2)
-                first_product(2 * g, 2 * half, 2 * half + 2)
-                first_product(2 * g + 1, 2 * half, 2 * half + 2)
-            if 0 <= s - V1_FROM < PASSES:
-                scale_right(1, s - V1_FROM, 1, VECTOR)
-        for q in range(PASSES):
-            quant_right(1, q)
+                first_product(2 * g, 2 * half)
+                first_product(2 * g + 1, 2 * half)
+            q = s - (UNITS // GROUPS - 1)
+            if 0 <= q < PASSES:
+                scale_right(1, q, 1, VECTOR)
+        quant_pair(1)
         for q in range(PASSES):
             scale_right(2, q, 1, POOL)
             scale_right(2, q, 0, SCALAR)
@@ -330,32 +308,30 @@ def tile_two_sided_preconditioned_step_d4_kernel(
         quant_h(0, 0)
         quant_h(0, 1)
 
-        for k in range(PAIRS - 1):
+        last = PAIRS - 2
+        for k in range(last + 1):
             y = SLOTS * (k + 1)
             j = SLOTS * k
-            now = k + 2 < PAIRS
-            nxt = k + 3 < PAIRS
             for x in range(SLOTS):
-                first_product(y + x, 0, 2)
+                first_product(y + x)
             if k > 0:
-                finish_tile(j - 2)
-                finish_tile(j - 1)
-                if now:
-                    scale_right(k + 2, 2, 0, SCALAR)
-                    scale_right(k + 2, 2, 1, SCALAR)
-            if nxt:
+                finish_tile(j - 2, POOL if k == last else VECTOR)
+                finish_tile(j - 1, POOL)
+            if 0 < k < last:
+                scale_right(k + 2, 2, 0, SCALAR)
+                scale_right(k + 2, 2, 1, SCALAR)
+            ahead = k + 3 < PAIRS
+            if ahead:
                 cast_right(k + 3, 0)
                 cast_right(k + 3, 1)
             if k == 0:
-                for q in range(PASSES):
-                    quant_right(k + 2, q)
+                quant_pair(k + 2)
             step_h(y)
             step_h(y + 1)
             join_h(k + 1, 0)
-            if now and k > 0:
-                for q in range(PASSES):
-                    quant_right(k + 2, q)
-            if nxt:
+            if 0 < k < last:
+                quant_pair(k + 2)
+            if ahead:
                 scale_right(k + 3, 0, 1, POOL)
                 scale_right(k + 3, 1, 1, POOL)
                 cast_right(k + 3, 2)
@@ -363,15 +339,15 @@ def tile_two_sided_preconditioned_step_d4_kernel(
             step_h(y + 2)
             step_h(y + 3)
             join_h(k + 1, 1)
-            if nxt:
+            if ahead:
                 scale_right(k + 3, 1, 0, SCALAR)
             for x in range(SLOTS):
                 second_product(j + x)
             finish_tile(j)
-            if k == PAIRS - 2:
+            if k == last:
                 quant_h(k + 1, 0)
             finish_tile(j + 1)
-            if k < PAIRS - 2:
+            if k < last:
                 quant_h(k + 1, 0)
             quant_h(k + 1, 1)
         j = len(tiles) - SLOTS

from contextlib import ExitStack

import concourse.mybir as mybir
from concourse.masks import make_identity

M, N, B = 1024, 1536, 128
FLOPS = 2 * M * N * N + 2 * M * M * N

F32 = mybir.dt.float32
BF16 = mybir.dt.bfloat16
U32 = mybir.dt.uint32
I32 = mybir.dt.int32
U8 = mybir.dt.uint8
E4M3 = mybir.dt.float8_e4m3fn
E4M3X4 = mybir.dt.float8_e4m3fn_x4
E2M1X4 = mybir.dt.float4_e2m1fn_x4
MULT = mybir.AluOpType.mult
ADD = mybir.AluOpType.add
SUB = mybir.AluOpType.subtract
COPY = mybir.ActivationFunctionType.Copy

P = 128
PASS = 4 * P
GROUPS = M // PASS
PASSES = N // PASS
BLOCKS = N // B
PAIR = 2 * B
PAIRS = N // PAIR
ROW_TILES = M // P
BANKS = 8
SLOTS = 4
UNITS = GROUPS * 4 * PASSES // 2
SCALAR, VECTOR, POOL = range(3)

LEAVE_LAG = 2
CAST_FROM = (3, 8)
SCALE_FROM = 5
QUANT_FROM = 9


def tile_two_sided_preconditioned_step_d4_kernel(
        tc, grad_bytes, grad_scale, right_bytes, right_scale, step, lt_words, lt_scales, w, out):
    nc = tc.nc
    with ExitStack() as ctx:
        keep = ctx.enter_context(tc.tile_pool(name="keep", bufs=1))
        rot = ctx.enter_context(tc.tile_pool(name="rot", bufs=3))
        psum = ctx.enter_context(tc.psum_pool(name="psum", bufs=BANKS))
        ctx.enter_context(tc.manual_schedule())

        grad_v = grad_bytes.rearrange("(g p t) k -> g p t k", p=P, t=4)
        right_v = right_bytes.rearrange("(q p t) n -> q p t n", p=P, t=4)
        out_v = out.rearrange("(r p) n -> p r n", p=P)
        w_v = w.rearrange("(r p) n -> p r n", p=P)

        g_scale = keep.tile([P, GROUPS, 4 * BLOCKS], F32, name="g_scale")
        nc.scalar.dma_start(out=g_scale[:], in_=grad_scale.rearrange("(g p t) c -> p g (t c)", p=P, t=4))

        ident = keep.tile([P, P], F32, name="ident")
        make_identity(nc, ident[:])
        lt_s = keep.tile([P, GROUPS, M], U8, name="lt_s", align_bytes=64)
        nc.vector.memset(lt_s[:].rearrange("p g n -> p (g n)").bitcast(I32), 0)

        g_raw = [[keep.tile([P, N], U8, name="g_raw%d%d" % (g, t)) for t in range(4)] for g in range(GROUPS)]
        r_raw = [[keep.tile([P, 4, PAIR], U8, name="r_raw%d%d" % (k, q)) for q in range(PASSES)] for k in range(PAIRS)]
        w_first = keep.tile([P, ROW_TILES, PASS], BF16, name="w_first")
        w_rest = keep.tile([P, ROW_TILES, N - PASS], BF16, name="w_rest")
        lt_w = keep.tile([P, GROUPS, 2 * M], U8, name="lt_w", align_bytes=64)
        step_all = keep.tile([P, N], BF16, name="step_all")
        r_scale = keep.tile([P, PASSES, BLOCKS], F32, name="r_scale")

        def load_grad(g, t, lo=0, hi=N):
            nc.sync.dma_start(out=g_raw[g][t][:, lo:hi], in_=grad_v[g][:, t, lo:hi])

        def load_right(k, q):
            nc.sync.dma_start(out=r_raw[k][q][:], in_=right_v[q][:, :, PAIR * k : PAIR * k + PAIR])

        def load_pair(k):
            for q in range(PASSES):
                load_right(k, q)

        def load_step(j):
            nc.sync.dma_start(out=step_all[:, PASS * j : PASS * j + PASS],
                              in_=step[PASS * j : PASS * j + PASS].partition_broadcast(P))

        def load_w(tile, lo, hi):
            rows = 4 * PASS // (hi - lo)
            for r in range(0, ROW_TILES, rows):
                nc.sync.dma_start(out=tile[:, r : r + rows, :], in_=w_v[:, r : r + rows, lo:hi])

        load_grad(0, 0, 0, 2 * PASS)
        load_grad(0, 0, 2 * PASS, N)
        load_grad(0, 1)
        load_grad(0, 2)
        load_right(0, 0)
        load_grad(0, 3)
        load_right(0, 1)
        for s in range(4):
            nc.sync.dma_start(out=r_scale[32 * s : 32 * s + 32, :, :],
                              in_=right_scale.rearrange("(q s) c -> s q c", s=4)[s].partition_broadcast(32))
        load_grad(1, 0)
        load_right(0, 2)
        for t in range(1, 4):
            load_grad(1, t)
        load_pair(1)
        load_step(0)
        load_pair(2)
        for s in range(4):
            nc.sync.dma_start(out=lt_s[32 * s : 32 * s + 4, :, :].bitcast(I32),
                              in_=lt_scales.rearrange("g (s r) n -> s r g n", s=4)[s].bitcast(I32))
        nc.sync.dma_start(out=lt_w[:], in_=lt_words.rearrange("g p n -> p g n"))
        load_w(w_first, 0, PASS)
        load_pair(3)
        load_step(1)
        load_pair(4)
        load_w(w_rest, PASS, N)
        load_pair(5)
        load_step(2)

        pieces = [(g, t, q) for g in range(GROUPS) for t in range(4) for q in range(PASSES)]
        g_codes = [keep.tile([P, 4 * PASSES * P], U32, name="g_codes%d" % g, align_bytes=64) for g in range(GROUPS)]
        g_bytes = [keep.tile([P, 4 * PASSES * P + 256], U8, name="g_bytes%d" % g, align_bytes=64)[:, 64 : 64 + 4 * PASSES * P]
                   for g in range(GROUPS)]
        g_wide = {}
        g_ps = {}
        g_turned = {}

        def widen_grad(s):
            for e, (g, t, q) in enumerate(pieces[2 * s : 2 * s + 2]):
                wide = rot.tile([P, PASS], BF16, name="g_wide", bufs=10)
                dst = wide[:].rearrange("p (h a f) -> p a h f", h=2, f=2)
                for c in range(4):
                    k0 = PASS * q + B * c
                    src = g_raw[g][t][:, k0 : k0 + B].bitcast(E4M3).rearrange("p (a h f) -> p a h f", h=2, f=2)
                    col = t * BLOCKS + 4 * q + c
                    nc.vector.tensor_scalar(out=dst[:, 32 * c : 32 * c + 32, :, :], in0=src,
                                            scalar1=g_scale[:, g, col : col + 1], scalar2=None, op0=MULT)
                g_wide[s, e] = wide

        def turn_grad(s):
            g_ps[s] = psum.tile([P, 2, 2, P], F32, name="bank")
            for e in range(2):
                words = g_wide[s, e][:].bitcast(F32)
                for h in range(2):
                    nc.tensor.transpose(g_ps[s][:, e, h, :], words[:, P * h : P * h + P], ident[:])

        def leave_grad(s):
            g_turned[s] = rot.tile([P, 2 * PASS], BF16, name="g_turned", align_bytes=64, bufs=UNITS)
            nc.scalar.copy(out=g_turned[s][:].bitcast(F32).rearrange("p (e m h) -> p e m h", e=2, h=2),
                           in_=g_ps[s][:].rearrange("p e h m -> p e m h"))

        def quant_grad(s):
            g, t, q = pieces[2 * s]
            m = slice(P * (PASSES * t + q), P * (PASSES * t + q + 2))
            nc.vector.quantize_mx(out=g_codes[g][:, m].bitcast(E4M3X4), scales=g_bytes[g][:, m], in_=g_turned[s][:])

        r_planes = {}
        r_wide = {}
        r_codes = {}
        r_bytes = {}

        def cast_right(k, q):
            r_planes[k, q] = rot.tile([P, 4, PAIR], BF16, name="r_planes", bufs=2 * PASSES)
            nc.scalar.copy(out=r_planes[k, q][:].rearrange("p t n -> p (t n)"),
                           in_=r_raw[k][q][:].rearrange("p t n -> p (t n)").bitcast(E4M3))

        def scale_right(k, q, b, engine):
            if engine == POOL or (k, b) == (1, 1):
                r_wide[k, q, b] = rot.tile([P, 4 * B], BF16, name="r_pool", align_bytes=64, bufs=PASSES)
            else:
                r_wide[k, q, b] = rot.tile([P, 4 * B], BF16, name="r_wide", align_bytes=64, bufs=8)
            dst = r_wide[k, q, b][:]
            src = r_planes[k, q][:, :, B * b : B * b + B]
            scale = r_scale[:, q, 2 * k + b : 2 * k + b + 1]
            if engine == POOL:
                nc.gpsimd.tensor_scalar(out=dst.rearrange("p (n t) -> p n t", t=4), in0=src.rearrange("p t n -> p n t"),
                                        scalar1=scale, scalar2=0.0, op0=MULT, op1=ADD)
                return
            dst = dst.rearrange("p (c i t) -> p c t i", t=4, i=4)
            src = src.rearrange("p t (c i) -> p c t i", i=4)
            if engine == VECTOR:
                nc.vector.tensor_scalar(out=dst, in0=src, scalar1=scale, scalar2=None, op0=MULT)
            else:
                nc.scalar.activation(out=dst, in_=src, func=COPY, scale=scale)

        def quant_pair(k):
            r_codes[k] = keep.tile([P, PASSES, PAIR], U32, name="r_codes%d" % k, align_bytes=64)
            r_bytes[k] = keep.tile([P, PASSES, PAIR], U8, name="r_bytes%d" % k, align_bytes=64)
            for q in range(PASSES):
                for b in (1, 0):
                    n = slice(B * b, B * b + B)
                    nc.vector.quantize_mx(out=r_codes[k][:, q, n].bitcast(E4M3X4), scales=r_bytes[k][:, q, n],
                                          in_=r_wide[k, q, b][:])

        slots = [(k, g, u) for k in range(PAIRS) for g in range(GROUPS) for u in range(2)]
        h_codes = [keep.tile([P, N], U32, name="h_codes%d" % g, align_bytes=64) for g in range(GROUPS)]
        h_bytes = [keep.tile([P, N], U8, name="h_bytes%d" % g, align_bytes=64) for g in range(GROUPS)]
        h_ps = {}
        h_parts = {}
        h_joined = {}

        def slot_shape(k, u):
            if k == 0:
                return range(4), slice(B * u, B * u + B)
            return range(2 * u, 2 * u + 2), slice(0, PAIR)

        def first_product(y, lo=0):
            k, g, u = slots[y]
            row_tiles, n = slot_shape(k, u)
            if lo == 0:
                h_ps[y] = psum.tile([P, len(row_tiles), PASS // len(row_tiles)], F32, name="bank")
            for e in range(lo, lo + 2):
                for q in range(PASSES):
                    m = slice(P * (PASSES * row_tiles[e] + q), P * (PASSES * row_tiles[e] + q + 1))
                    nc.tensor.matmul_mx(out=h_ps[y][:, e, :],
                                        lhsT=g_codes[g][:, m].bitcast(E4M3X4), lhsT_scale=g_bytes[g][:, m],
                                        rhs=r_codes[k][:, q, n].bitcast(E4M3X4), rhs_scale=r_bytes[k][:, q, n],
                                        start=(q == 0), stop=(q == PASSES - 1))

        def step_h(y):
            k, g, u = slots[y]
            row_tiles, n = slot_shape(k, u)
            if u == 0:
                h_parts[k, g] = rot.tile([P, 2, PASS], BF16, name="h_parts", align_bytes=64, bufs=4)
            steps = step_all[:, PAIR * k + n.start : PAIR * k + n.stop].rearrange("p (c i) -> p c i", i=2)
            nc.vector.tensor_tensor(out=h_parts[k, g][:, u, :].rearrange("p (c i e) -> p c e i", i=2, e=len(row_tiles)),
                                    in0=steps.unsqueeze(2).to_broadcast([P, (n.stop - n.start) // 2, len(row_tiles), 2]),
                                    in1=h_ps[y][:].rearrange("p e (c i) -> p c e i", i=2),
                                    op=MULT)

        def join_h(k, g):
            h_joined[k, g] = rot.tile([P, 4 * PAIR], BF16, name="h_joined", align_bytes=64)
            nc.scalar.copy(out=h_joined[k, g][:].bitcast(F32).rearrange("p (n u) -> p n u", u=2),
                           in_=h_parts[k, g][:].bitcast(F32).rearrange("p u n -> p n u"))

        def quant_h(k, g):
            n = slice(PAIR * k, PAIR * k + PAIR)
            src = h_parts[k, g][:].rearrange("p u n -> p (u n)") if k == 0 else h_joined[k, g][:]
            nc.vector.quantize_mx(out=h_codes[g][:, n].bitcast(E4M3X4), scales=h_bytes[g][:, n], in_=src)

        tiles = [(k, r0) for k in range(PAIRS) for r0 in range(0, ROW_TILES, 2)]
        u_ps = {}

        def second_product(j):
            k, r0 = tiles[j]
            u_ps[j] = psum.tile([P, 2, PAIR], F32, name="bank")
            n = slice(PAIR * k, PAIR * k + PAIR)
            for x in range(2):
                r = r0 + x
                for g in range(GROUPS):
                    nc.tensor.matmul_mx(out=u_ps[j][:, x, :],
                                        lhsT=lt_w[:, g, 2 * P * r : 2 * P * r + 2 * P].bitcast(E2M1X4),
                                        lhsT_scale=lt_s[:, g, P * r : P * r + P],
                                        rhs=h_codes[g][:, n].bitcast(E4M3X4), rhs_scale=h_bytes[g][:, n],
                                        start=(g == 0), stop=(g == GROUPS - 1))

        def finish_tile(j, engine=VECTOR):
            k, r0 = tiles[j]
            tile, n0 = (w_first, PAIR * k) if PAIR * k < PASS else (w_rest, PAIR * k - PASS)
            old = tile[:, r0 : r0 + 2, n0 : n0 + PAIR]
            result = rot.tile([P, 2, PAIR], F32, name="result", bufs=10)
            if engine == POOL:
                u = rot.tile([P, 2, PAIR], F32, name="u", bufs=2)
                nc.scalar.copy(out=u[:], in_=u_ps[j][:])
                nc.gpsimd.tensor_tensor(out=result[:], in0=old, in1=u[:], op=SUB)
            else:
                nc.vector.tensor_tensor(out=result[:], in0=old, in1=u_ps[j][:], op=SUB)
            nc.sync.dma_start(out=out_v[:, r0 : r0 + 2, PAIR * k : PAIR * k + PAIR], in_=result[:])

        blocks = [(q, b) for q in range(PASSES) for b in range(2)]
        for s in range(UNITS):
            widen_grad(s)
            if s >= 1:
                turn_grad(s - 1)
            for k, first in enumerate(CAST_FROM):
                if 0 <= s - first < PASSES:
                    cast_right(k, s - first)
            if s >= LEAVE_LAG:
                leave_grad(s - LEAVE_LAG)
            x = s - SCALE_FROM
            if 0 <= x < len(blocks):
                scale_right(0, *blocks[x], SCALAR if x % 2 and x < len(blocks) - 1 else VECTOR)
            if s >= QUANT_FROM:
                quant_grad(s - QUANT_FROM)
        turn_grad(UNITS - 1)
        for s in range(UNITS - LEAVE_LAG, UNITS):
            leave_grad(s)
        quant_pair(0)
        for q in range(PASSES):
            scale_right(1, q, 0, SCALAR)
        for q in range(PASSES):
            cast_right(2, q)
        for s in range(UNITS):
            if s >= UNITS - QUANT_FROM:
                quant_grad(s)
            if s % PASSES == PASSES - 1:
                g, half = divmod(s // PASSES, 2)
                first_product(2 * g, 2 * half)
                first_product(2 * g + 1, 2 * half)
            q = s - (UNITS // GROUPS - 1)
            if 0 <= q < PASSES:
                scale_right(1, q, 1, VECTOR)
        quant_pair(1)
        for q in range(PASSES):
            scale_right(2, q, 1, POOL)
            scale_right(2, q, 0, SCALAR)
        for y in range(SLOTS):
            step_h(y)
        quant_h(0, 0)
        quant_h(0, 1)

        last = PAIRS - 2
        for k in range(last + 1):
            y = SLOTS * (k + 1)
            j = SLOTS * k
            for x in range(SLOTS):
                first_product(y + x)
            if k > 0:
                finish_tile(j - 2, POOL if k == last else VECTOR)
                finish_tile(j - 1, POOL)
            if 0 < k < last:
                scale_right(k + 2, 2, 0, SCALAR)
                scale_right(k + 2, 2, 1, SCALAR)
            ahead = k + 3 < PAIRS
            if ahead:
                cast_right(k + 3, 0)
                cast_right(k + 3, 1)
            if k == 0:
                quant_pair(k + 2)
            step_h(y)
            step_h(y + 1)
            join_h(k + 1, 0)
            if 0 < k < last:
                quant_pair(k + 2)
            if ahead:
                scale_right(k + 3, 0, 1, POOL)
                scale_right(k + 3, 1, 1, POOL)
                cast_right(k + 3, 2)
                scale_right(k + 3, 0, 0, SCALAR)
            step_h(y + 2)
            step_h(y + 3)
            join_h(k + 1, 1)
            if ahead:
                scale_right(k + 3, 1, 0, SCALAR)
            for x in range(SLOTS):
                second_product(j + x)
            finish_tile(j)
            if k == last:
                quant_h(k + 1, 0)
            finish_tile(j + 1)
            if k < last:
                quant_h(k + 1, 0)
            quant_h(k + 1, 1)
        j = len(tiles) - SLOTS
        finish_tile(j - 2)
        finish_tile(j - 1)
        for x in range(SLOTS):
            second_product(j + x)
            finish_tile(j + x)
